import numpy as np
import ml_dtypes


def mxq(x, axis, fmt="e4m3"):
    dtype, down = {"e4m3": (ml_dtypes.float8_e4m3fn, 7), "e5m2": (ml_dtypes.float8_e5m2, 14)}[fmt]
    v = np.moveaxis(np.asarray(x, np.float32).astype(ml_dtypes.bfloat16).astype(np.float64), axis, -1)
    blocks = v.reshape(v.shape[:-1] + (-1, 32))
    amax = np.abs(blocks).max(-1, keepdims=True)
    byte = np.maximum(np.where(amax > 0, np.frexp(amax)[1] - 1 + 127, 0) - down, 1)
    scale = np.exp2(byte - 127.0)
    codes = (blocks / scale).astype(np.float32).astype(dtype).astype(np.float64)
    return np.moveaxis((codes * scale).reshape(v.shape), -1, axis)


WIDE = False


def mx_kscale(k):
    if not WIDE:
        return np.ones(k)
    levels = np.array([10, -10, 5, -5, 0])
    if k % 512:
        return np.exp2(np.random.permutation(np.resize(levels, k // 32))).repeat(32)
    a = np.empty((k // 512, 16))
    for p in range(k // 512):
        a[p, :8] = np.random.permutation(np.resize(levels, 8))
        for g in range(8):
            far = levels[np.abs(levels - a[p, g]) >= 10]
            a[p, g + 8] = far[np.random.randint(len(far))]
    return np.exp2(a.ravel()).repeat(32)


def f64(x):
    return np.asarray(x).astype(np.float64)


def striped(idx):
    return np.tile(idx.reshape(-1, 16).T, (8, 1)).astype(np.uint16)


def unstriped(offs):
    return offs[:16].T.reshape(-1).astype(np.int64)


E2M1 = np.array([0.0, 0.5, 1.0, 1.5, 2.0, 3.0, 4.0, 6.0, -0.0, -0.5, -1.0, -1.5, -2.0, -3.0, -4.0, -6.0])


def pack_weight(w, fmt):
    k, n = w.shape
    w = f64(np.asarray(w, np.float32).astype(ml_dtypes.bfloat16)).reshape(k // 32, 32, n)
    amax = np.abs(w).max(1)
    if fmt == "e4m3":
        byte = np.frexp(amax)[1] - 1 + 127 - 7
    else:
        mant, ex = np.frexp(amax / 6.0)
        byte = np.where(mant > 0.5, ex, ex - 1) + 127
    byte = np.clip(np.where(amax > 0, byte, 1), 1, 254)
    scaled = (w * np.exp2(127.0 - byte)[:, None, :]).reshape(k, n).astype(np.float32)
    by_word = np.ascontiguousarray(scaled.reshape(k // 512, 128, 4, n).transpose(0, 1, 3, 2))
    if fmt == "e4m3":
        words = by_word.astype(ml_dtypes.float8_e4m3fn).view(np.uint8)
    else:
        c = by_word.astype(ml_dtypes.float4_e2m1fn).view(np.uint8) & 0xF
        words = (c[..., 0::2] | (c[..., 1::2] << 4)).reshape(k // 512, 128, 2 * n)
    return np.ascontiguousarray(words), np.ascontiguousarray(byte.astype(np.uint8).reshape(k // 512, 16, n))


def unpack_weight(words, scales, fmt):
    g, _, n = scales.shape
    words = np.ascontiguousarray(words).reshape(g, 128, n, -1)
    if fmt == "e4m3":
        vals = words.view(ml_dtypes.float8_e4m3fn).astype(np.float64)
    else:
        nib = np.empty((g, 128, n, 4), np.uint8)
        nib[..., 0::2] = words & 0xF
        nib[..., 1::2] = words >> 4
        vals = E2M1[nib]
    vals = vals * np.repeat(np.exp2(scales.astype(np.float64) - 127.0), 8, axis=1)[..., None]
    return vals.transpose(0, 1, 3, 2).reshape(g * 512, n)


def planes(y):
    n, m = y.shape
    v = y.astype(np.float32).astype(ml_dtypes.bfloat16).astype(np.float64).reshape(n // 32, 32, m)
    top = np.abs(v).max(1)
    byte = np.clip(np.where(top > 0, np.frexp(top)[1] - 1 + 127 - 7, 1), 1, 254)
    codes = (v * np.exp2(127.0 - byte)[:, None, :]).reshape(n, m).astype(np.float32).astype(ml_dtypes.float8_e4m3fn).view(np.uint8)
    words = codes.reshape(n // 512, 128, 4, m).transpose(0, 1, 3, 2)
    return np.ascontiguousarray(words), np.ascontiguousarray(byte.astype(np.uint8).reshape(n // 512, 16, m))


def d_relu(v):
    return (v > 0).astype(np.float64)


K, T, E, C, H, N = 1024, 1024, 4, 256, 512, 512


def by_expert(wq, xq):
    return np.concatenate([wq[e].T @ xq[:, e * C:(e + 1) * C] for e in range(E)], axis=1)


def setup_inputs():
    n = np.random.standard_normal
    v = mx_kscale(N)
    u = mx_kscale(H)
    slot_token = np.random.permutation(T)[:E * C]
    w_slot = np.random.uniform(0.2, 1.0, E * C)
    dy = pack_weight(n((N, T)) * v[:, None], "e4m3")
    w2t = pack_weight(n((N, H)) / np.sqrt(N) / v[:, None] * u, "e4m3")
    w1t = [pack_weight(m, "e2m1") for m in n((E, H, K)) / np.sqrt(H) / u[None, :, None]]
    return {
        "dy_words": dy[0],
        "dy_scales": dy[1],
        "w2t_words": w2t[0],
        "w2t_scales": w2t[1],
        "w1t_words": np.stack([m[0] for m in w1t]),
        "w1t_scales": np.stack([m[1] for m in w1t]),
        "a": (n((H, E * C))).astype(np.float32),
        "gate": (np.tile(w_slot, (128, 1))).astype(np.float32),
        "offs": striped(slot_token),
    }


def reference(dy_words, dy_scales, w2t_words, w2t_scales, w1t_words, w1t_scales, a, gate, offs):
    w2t = unpack_weight(w2t_words, w2t_scales, "e4m3")
    w1t = np.stack([unpack_weight(w1t_words[e], w1t_scales[e], "e2m1") for e in range(E)])
    idx = unstriped(offs)
    dc = w2t.T @ unpack_weight(dy_words, dy_scales, "e4m3")
    da = f64(gate[:1]) * dc[:, idx] * d_relu(f64(a))
    dx = by_expert(w1t, mxq(da, 0, "e4m3"))
    out = np.zeros((K, T))
    out[:, idx] = dx
    out_0 = out
    return (out_0,) + planes(out_0)

@@ -1,0 +1,226 @@
+from contextlib import ExitStack
+
+import concourse.mybir as mybir
+from concourse.masks import make_identity
+
+K, T, E, C, H, N = 1024, 1024, 4, 256, 512, 512
+FLOPS = 2 * N * H * T + 2 * H * K * E * C
+
+F32 = mybir.dt.float32
+BF16 = mybir.dt.bfloat16
+I32 = mybir.dt.int32
+U16 = mybir.dt.uint16
+U8 = mybir.dt.uint8
+FP8X4 = mybir.dt.float8_e4m3fn_x4
+FP4X4 = mybir.dt.float4_e2m1fn_x4
+ALU = mybir.AluOpType
+
+P = 128
+PACK = 4
+BANK = 512
+LANES = 16
+S = E * C
+HALF = S // 2
+WINDOW = 1376
+
+
+def scale_rows(queues, plane, rows):
+    for q, queue in enumerate(queues):
+        queue.dma_start(out=plane[32 * q : 32 * q + 4].bitcast(I32), in_=rows[4 * q : 4 * q + 4].bitcast(I32))
+
+
+def tile_moe_sdb_relu_kernel(
+    tc, dy_words, dy_scales, w2t_words, w2t_scales, w1t_words, w1t_scales, a, gate, offs, out_0, out_1, out_2
+):
+    nc = tc.nc
+    with ExitStack() as ctx:
+        keep = ctx.enter_context(tc.tile_pool(name="keep", bufs=1))
+        ring = ctx.enter_context(tc.tile_pool(name="ring", bufs=4))
+        psum = ctx.enter_context(tc.psum_pool(name="psum", bufs=4))
+
+        offsets = keep.tile([P, S // LANES], U16, name="offsets")
+        w2_raw = keep.tile([P, H], I32, name="w2_raw", align_bytes=64)
+        w2_raw_s = keep.tile([P, H], U8, name="w2_raw_s", align_bytes=64)
+        w2_codes = keep.tile([P, H], I32, name="w2_codes", align_bytes=64)
+        w2_s = keep.tile([P, H], U8, name="w2_s", align_bytes=64)
+        dy_codes = keep.tile([P, T], I32, name="dy_codes", align_bytes=64)
+        dy_s = keep.tile([P, T], U8, name="dy_s", align_bytes=64)
+        w1_s = keep.tile([P, E, K], U8, name="w1_s", align_bytes=64)
+        w1_codes = [keep.tile([P, 2, 2 * K], U8, name=f"w1_codes{i}", align_bytes=64) for i in range(2)]
+        a_first = [keep.tile([P, HALF], F32, name=f"a_first{t}") for t in range(PACK)]
+        a_second = keep.tile([P, PACK, HALF], F32, name="a_second")
+        gate_sb = [keep.tile([P, HALF], F32, name=f"gate{i}") for i in range(2)]
+        ident = keep.tile([P, P], F32, name="ident")
+
+        nc.gpsimd.memset(w2_raw_s[:].bitcast(I32), 0)
+
+        a_rows = a.rearrange("(p t) j -> p t j", t=PACK)
+        scale_rows([nc.sync] * 4, dy_s, dy_scales[0])
+        nc.sync.dma_start(out=w2_raw[:], in_=w2t_words[0].rearrange("p i d -> p (i d)").bitcast(I32))
+        nc.sync.dma_start(out=dy_codes[:], in_=dy_words[0].rearrange("p t d -> p (t d)").bitcast(I32))
+        scale_rows([nc.sync] * 4, w2_raw_s, w2t_scales[0])
+        make_identity(nc, ident[:])
+        nc.sync.dma_start(offsets[:], offs)
+        nc.sync.dma_start(out=gate_sb[0][:], in_=gate[:, 0:HALF])
+        nc.sync.dma_start(out=a_first[0][:], in_=a_rows[:, 0, 0:HALF])
+        for t in range(1, PACK):
+            nc.sync.dma_start(out=a_first[t][:], in_=a_rows[:, t, 0:HALF])
+        nc.sync.dma_start(out=gate_sb[1][:], in_=gate[:, HALF:S])
+        nc.sync.dma_start(out=a_second[:], in_=a_rows[:, :, HALF:S])
+        scale_rows([nc.sync] * 4, w1_s, w1t_scales.rearrange("e s b k -> (s b) e k"))
+        w1_rows = w1t_words.rearrange("e s p c -> (s p) e c")
+        for i in range(2):
+            nc.sync.dma_start(out=w1_codes[i][:].bitcast(I32), in_=w1_rows[:, 2 * i : 2 * i + 2, :].bitcast(I32))
+
+        nc.vector.tensor_copy(
+            out=w2_codes[:].rearrange("p (t m) -> p m t", t=PACK), in_=w2_raw[:].rearrange("p (m t) -> p m t", t=PACK)
+        )
+        nc.vector.tensor_copy(
+            out=w2_s[:].rearrange("p (t m) -> p m t", t=PACK), in_=w2_raw_s[:].rearrange("p (m t) -> p m t", t=PACK)
+        )
+
+        dc = [keep.tile([P, T], F32, name=f"dc{t}") for t in range(PACK)]
+        for t in range(PACK):
+            for h in range(T // BANK):
+                cols = slice(h * BANK, (h + 1) * BANK)
+                acc = psum.tile([P, BANK], F32, name="acc")
+                nc.tensor.matmul_mx(
+                    out=acc[:],
+                    lhsT=w2_codes[:, t * P : (t + 1) * P].bitcast(FP8X4),
+                    lhsT_scale=w2_s[:, t * P : (t + 1) * P],
+                    rhs=dy_codes[:, cols].bitcast(FP8X4),
+                    rhs_scale=dy_s[:, cols],
+                    start=True,
+                    stop=True,
+                )
+                nc.scalar.copy(out=dc[t][:, cols], in_=acc[:])
+
+        da, da_bf, da_codes, da_s = {}, {}, {}, {}
+
+        def gather(i, t, factor):
+            slots = offsets[:, i * HALF // LANES : (i + 1) * HALF // LANES]
+            nc.vector.tensor_tensor(da[i][:, t, :], dc[t][:].indirect(slots), factor, ALU.mult)
+
+        def round_da(first, width, tag):
+            da_bf[first] = keep.tile([P, width, PACK], BF16, name=f"da_bf{first}", tag=tag, align_bytes=64)
+            cols = slice(first % HALF, first % HALF + width)
+            nc.scalar.copy(out=da_bf[first][:], in_=da[first // HALF][:, :, cols].rearrange("p t j -> p j t"))
+
+        def quantize_da(first, width):
+            codes = keep.tile([P, width], I32, name=f"da_codes{first}", align_bytes=64)
+            scales = keep.tile([P, width], U8, name=f"da_s{first}", align_bytes=64)
+            nc.vector.quantize_mx(out=codes[:].bitcast(FP8X4), scales=scales[:], in_=da_bf[first][:].rearrange("p j t -> p (j t)"))
+            for u in range(width // P):
+                da_codes[first // P + u] = codes[:, u * P : (u + 1) * P]
+                da_s[first // P + u] = scales[:, u * P : (u + 1) * P]
+
+        dx = [
+            [keep.tile([P, PACK, S // 2], F32, name="dx00"), keep.tile([P, PACK, S // 2], F32, name="dx01")],
+            [keep.tile([P, PACK, S], F32, name="dx1")],
+        ]
+
+        def expert_block(s, b, tag=None):
+            e = b * P // C
+            acc = psum.tile([P, BANK], F32, name="acc")
+            nc.tensor.matmul_mx(
+                out=acc[:],
+                lhsT=da_codes[b].bitcast(FP8X4),
+                lhsT_scale=da_s[b],
+                rhs=w1_codes[e // 2][:, e % 2, 2 * s * BANK : 2 * (s + 1) * BANK].bitcast(FP4X4),
+                rhs_scale=w1_s[:, e, s * BANK : (s + 1) * BANK],
+                start=True,
+                stop=True,
+            )
+            if tag is None:
+                by_slot = ring.tile([P, PACK, P], F32, name="by_slot")
+            else:
+                by_slot = keep.tile([P, PACK, P], F32, name="by_slot_held", tag=tag, align_bytes=64)
+            nc.scalar.copy(out=by_slot[:], in_=acc[:].rearrange("p (m d) -> p d m", d=PACK))
+            turned = psum.tile([P, PACK, P], F32, name="turned")
+            for d in range(PACK):
+                nc.tensor.transpose(turned[:, d, :], by_slot[:, d, :], ident[:])
+            width = S // len(dx[s])
+            part, first = divmod(b * P, width)
+            nc.scalar.copy(out=dx[s][part][:, :, first : first + P], in_=turned[:])
+
+        windows = {}
+
+        def scatter(s, d, part):
+            if part == 0:
+                windows[s, d] = keep.tile([P, WINDOW], F32, name=f"window{s}{d}", tag=f"window{d}", align_bytes=64)
+            width = S // len(dx[s])
+            slots = offsets[:, part * width // LANES : (part + 1) * width // LANES]
+            nc.vector.tensor_copy(windows[s, d][:].indirect(slots), dx[s][part][:, d, :])
+
+        out_rows = out_0.rearrange("(s p d) t -> s d p t", p=P, d=PACK)
+
+        def hand_out(s, pieces):
+            step = T // pieces
+            y_bf = keep.tile([P, T, PACK], BF16, name=f"y_bf{s}", tag=f"y_bf{s}", align_bytes=64)
+            shared = T - step if pieces > 1 else T
+            for d in range(PACK):
+                nc.sync.dma_start(out=out_rows[s, d], in_=windows[s, d][:, 0:T])
+                if d < 2 or pieces == 1:
+                    nc.scalar.copy(out=y_bf[:, :, d], in_=windows[s, d][:, 0:T])
+                elif d == 2:
+                    nc.scalar.copy(out=y_bf[:, 0:shared, d], in_=windows[s, d][:, 0:shared])
+                else:
+                    for c in range(pieces - 1):
+                        nc.scalar.copy(out=y_bf[:, c * step : (c + 1) * step, d], in_=windows[s, d][:, c * step : (c + 1) * step])
+            if pieces > 1:
+                for d in (2, 3):
+                    nc.vector.tensor_copy(out=y_bf[:, shared:T, d], in_=windows[s, d][:, shared:T])
+            y_codes = keep.tile([P, T], I32, name=f"y_codes{s}", align_bytes=64)
+            y_s = keep.tile([P, T], U8, name=f"y_s{s}", align_bytes=64)
+            words = out_1[s].rearrange("p t d -> p (t d)").bitcast(I32)
+            for c in [pieces - 1] + list(range(pieces - 1)):
+                cols = slice(c * step, (c + 1) * step)
+                nc.vector.quantize_mx(
+                    out=y_codes[:, cols].bitcast(FP8X4), scales=y_s[:, cols], in_=y_bf[:, cols, :].rearrange("p t d -> p (t d)")
+                )
+                if pieces == 1:
+                    nc.sync.dma_start(out=words[:], in_=y_codes[:])
+                elif c == 1:
+                    nc.sync.dma_start(out=words[:, 0 : 2 * step], in_=y_codes[:, 0 : 2 * step])
+                elif c == 2:
+                    nc.sync.dma_start(out=words[:, 2 * step : T], in_=y_codes[:, 2 * step : T])
+            for q in range(4):
+                queue = nc.scalar if pieces > 1 and q % 2 else nc.sync
+                queue.dma_start(out=out_2[s, 4 * q : 4 * q + 4, :].bitcast(I32), in_=y_s[32 * q : 32 * q + 4, :].bitcast(I32))
+
+        da[0] = keep.tile([P, PACK, HALF], F32, name="da_first")
+        factor = keep.tile([P, PACK, HALF], F32, name="factor_first", tag="factor")
+        for t in range(PACK):
+            nc.vector.scalar_tensor_tensor(
+                out=factor[:, t, :], in0=a_first[t][:], scalar=0.0, in1=gate_sb[0][:], op0=ALU.is_gt, op1=ALU.mult
+            )
+            gather(0, t, factor[:, t, :])
+        round_da(0, C, "window3")
+        round_da(C, C, "da_bf1")
+        factor = keep.tile([P, PACK, HALF], F32, name="factor_second", tag="factor")
+        nc.vector.scalar_tensor_tensor(
+            out=factor[:], in0=a_second[:], scalar=0.0, in1=gate_sb[1][:].unsqueeze(1).to_broadcast([P, PACK, HALF]),
+            op0=ALU.is_gt, op1=ALU.mult,
+        )
+        quantize_da(0, C)
+        quantize_da(C, C)
+        da[1] = keep.tile([P, PACK, HALF], F32, name="da_second", tag="window3", align_bytes=64)
+        for t in range(PACK):
+            gather(1, t, factor[:, t, :])
+        for b in range(4):
+            expert_block(0, b, "window1" if b == 3 else None)
+        round_da(HALF, HALF, "window1")
+        scatter(0, 0, 0)
+        quantize_da(HALF, HALF)
+        for b in range(4, 8):
+            expert_block(0, b)
+        for d in range(1, PACK):
+            scatter(0, d, 0)
+        for b in range(8):
+            expert_block(1, b, "y_bf0" if b == 7 else None)
+        for d in range(PACK):
+            scatter(0, d, 1)
+        hand_out(0, 1)
+        for d in range(PACK):
+            scatter(1, d, 0)
+        hand_out(1, 4)

@@ -35,7 +35,6 @@ def tile_moe_sdb_relu_kernel(
     nc = tc.nc
     with ExitStack() as ctx:
         keep = ctx.enter_context(tc.tile_pool(name="keep", bufs=1))
-        ring = ctx.enter_context(tc.tile_pool(name="ring", bufs=4))
         psum = ctx.enter_context(tc.psum_pool(name="psum", bufs=4))
 
         offsets = keep.tile([P, S // LANES], U16, name="offsets")
@@ -47,7 +46,7 @@ def tile_moe_sdb_relu_kernel(
         dy_s = keep.tile([P, T], U8, name="dy_s", align_bytes=64)
         w1_s = keep.tile([P, E, K], U8, name="w1_s", align_bytes=64)
         w1_codes = [keep.tile([P, 2, 2 * K], U8, name=f"w1_codes{i}", align_bytes=64) for i in range(2)]
-        a_first = [keep.tile([P, HALF], F32, name=f"a_first{t}") for t in range(PACK)]
+        a_first = [keep.tile([P, 2, HALF], F32, name=f"a_first{i}") for i in range(2)]
         a_second = keep.tile([P, PACK, HALF], F32, name="a_second")
         gate_sb = [keep.tile([P, HALF], F32, name=f"gate{i}") for i in range(2)]
         ident = keep.tile([P, P], F32, name="ident")
@@ -59,12 +58,11 @@ def tile_moe_sdb_relu_kernel(
         nc.sync.dma_start(out=w2_raw[:], in_=w2t_words[0].rearrange("p i d -> p (i d)").bitcast(I32))
         nc.sync.dma_start(out=dy_codes[:], in_=dy_words[0].rearrange("p t d -> p (t d)").bitcast(I32))
         scale_rows([nc.sync] * 4, w2_raw_s, w2t_scales[0])
+        nc.sync.dma_start(out=gate_sb[0][:], in_=gate[:, 0:HALF])
+        nc.sync.dma_start(out=a_first[0][:], in_=a_rows[:, 0:2, 0:HALF])
         make_identity(nc, ident[:])
         nc.sync.dma_start(offsets[:], offs)
-        nc.sync.dma_start(out=gate_sb[0][:], in_=gate[:, 0:HALF])
-        nc.sync.dma_start(out=a_first[0][:], in_=a_rows[:, 0, 0:HALF])
-        for t in range(1, PACK):
-            nc.sync.dma_start(out=a_first[t][:], in_=a_rows[:, t, 0:HALF])
+        nc.sync.dma_start(out=a_first[1][:], in_=a_rows[:, 2:4, 0:HALF])
         nc.sync.dma_start(out=gate_sb[1][:], in_=gate[:, HALF:S])
         nc.sync.dma_start(out=a_second[:], in_=a_rows[:, :, HALF:S])
         scale_rows([nc.sync] * 4, w1_s, w1t_scales.rearrange("e s b k -> (s b) e k"))
@@ -115,85 +113,88 @@ def tile_moe_sdb_relu_kernel(
                 da_s[first // P + u] = scales[:, u * P : (u + 1) * P]
 
         dx = [
-            [keep.tile([P, PACK, S // 2], F32, name="dx00"), keep.tile([P, PACK, S // 2], F32, name="dx01")],
+            [keep.tile([P, PACK, HALF], F32, name="dx00"), keep.tile([P, PACK, HALF], F32, name="dx01")],
             [keep.tile([P, PACK, S], F32, name="dx1")],
         ]
 
-        def expert_block(s, b, tag=None):
-            e = b * P // C
-            acc = psum.tile([P, BANK], F32, name="acc")
-            nc.tensor.matmul_mx(
-                out=acc[:],
-                lhsT=da_codes[b].bitcast(FP8X4),
-                lhsT_scale=da_s[b],
-                rhs=w1_codes[e // 2][:, e % 2, 2 * s * BANK : 2 * (s + 1) * BANK].bitcast(FP4X4),
-                rhs_scale=w1_s[:, e, s * BANK : (s + 1) * BANK],
-                start=True,
-                stop=True,
-            )
-            if tag is None:
-                by_slot = ring.tile([P, PACK, P], F32, name="by_slot")
-            else:
-                by_slot = keep.tile([P, PACK, P], F32, name="by_slot_held", tag=tag, align_bytes=64)
-            nc.scalar.copy(out=by_slot[:], in_=acc[:].rearrange("p (m d) -> p d m", d=PACK))
-            turned = psum.tile([P, PACK, P], F32, name="turned")
+        def expert_products(s, i, tag):
+            by_slot = []
+            for u in range(HALF // P):
+                b = i * HALF // P + u
+                e = b * P // C
+                acc = psum.tile([P, BANK], F32, name="acc")
+                nc.tensor.matmul_mx(
+                    out=acc[:],
+                    lhsT=da_codes[b].bitcast(FP8X4),
+                    lhsT_scale=da_s[b],
+                    rhs=w1_codes[e // 2][:, e % 2, 2 * s * BANK : 2 * (s + 1) * BANK].bitcast(FP4X4),
+                    rhs_scale=w1_s[:, e, s * BANK : (s + 1) * BANK],
+                    start=True,
+                    stop=True,
+                )
+                tile = keep.tile([P, PACK, P], F32, name="by_slot", tag=tag if u == 3 else f"by_slot{u}", align_bytes=64)
+                nc.scalar.copy(out=tile[:], in_=acc[:].rearrange("p (m d) -> p d m", d=PACK))
+                by_slot.append(tile)
             for d in range(PACK):
-                nc.tensor.transpose(turned[:, d, :], by_slot[:, d, :], ident[:])
-            width = S // len(dx[s])
-            part, first = divmod(b * P, width)
-            nc.scalar.copy(out=dx[s][part][:, :, first : first + P], in_=turned[:])
+                turned = psum.tile([P, HALF], F32, name="turned")
+                for u, tile in enumerate(by_slot):
+                    nc.tensor.transpose(turned[:, u * P : (u + 1) * P], tile[:, d, :], ident[:])
+                if s == 0:
+                    nc.scalar.copy(out=dx[s][i][:, d, :], in_=turned[:])
+                else:
+                    nc.scalar.copy(out=dx[s][0][:, d, i * HALF : (i + 1) * HALF], in_=turned[:])
 
         windows = {}
 
-        def scatter(s, d, part):
+        def scatter(s, d, part, tag=None):
             if part == 0:
-                windows[s, d] = keep.tile([P, WINDOW], F32, name=f"window{s}{d}", tag=f"window{d}", align_bytes=64)
+                windows[s, d] = keep.tile([P, WINDOW], F32, name=f"window{s}{d}", tag=tag or f"window{d}", align_bytes=64)
             width = S // len(dx[s])
             slots = offsets[:, part * width // LANES : (part + 1) * width // LANES]
             nc.vector.tensor_copy(windows[s, d][:].indirect(slots), dx[s][part][:, d, :])
 
         out_rows = out_0.rearrange("(s p d) t -> s d p t", p=P, d=PACK)
 
-        def hand_out(s, pieces):
-            step = T // pieces
-            y_bf = keep.tile([P, T, PACK], BF16, name=f"y_bf{s}", tag=f"y_bf{s}", align_bytes=64)
-            shared = T - step if pieces > 1 else T
-            for d in range(PACK):
-                nc.sync.dma_start(out=out_rows[s, d], in_=windows[s, d][:, 0:T])
-                if d < 2 or pieces == 1:
-                    nc.scalar.copy(out=y_bf[:, :, d], in_=windows[s, d][:, 0:T])
-                elif d == 2:
-                    nc.scalar.copy(out=y_bf[:, 0:shared, d], in_=windows[s, d][:, 0:shared])
+        y_bf = {}
+        cuts = [[0, T], [0, T // 2, 3 * T // 4, T]]
+
+        def store_plane(s, d):
+            spans = [slice(lo, hi) for lo, hi in zip(cuts[s], cuts[s][1:])]
+            if s not in y_bf:
+                y_bf[s] = [
+                    keep.tile([P, cols.stop - cols.start, PACK], BF16, name=f"y_bf{s}{c}", tag=f"y_bf{s + c}", align_bytes=64)
+                    for c, cols in enumerate(spans)
+                ]
+            window = windows[s, d]
+            nc.sync.dma_start(out=out_rows[s, d], in_=window[:, 0:T])
+            for c, cols in enumerate(spans):
+                if (s, d, c) == (1, 1, 0):
+                    nc.vector.tensor_copy(out=y_bf[s][c][:, :, d], in_=window[:, cols])
                 else:
-                    for c in range(pieces - 1):
-                        nc.scalar.copy(out=y_bf[:, c * step : (c + 1) * step, d], in_=windows[s, d][:, c * step : (c + 1) * step])
-            if pieces > 1:
-                for d in (2, 3):
-                    nc.vector.tensor_copy(out=y_bf[:, shared:T, d], in_=windows[s, d][:, shared:T])
+                    nc.scalar.copy(out=y_bf[s][c][:, :, d], in_=window[:, cols])
+
+        def quantize_out(s):
             y_codes = keep.tile([P, T], I32, name=f"y_codes{s}", align_bytes=64)
             y_s = keep.tile([P, T], U8, name=f"y_s{s}", align_bytes=64)
             words = out_1[s].rearrange("p t d -> p (t d)").bitcast(I32)
-            for c in [pieces - 1] + list(range(pieces - 1)):
-                cols = slice(c * step, (c + 1) * step)
-                nc.vector.quantize_mx(
-                    out=y_codes[:, cols].bitcast(FP8X4), scales=y_s[:, cols], in_=y_bf[:, cols, :].rearrange("p t d -> p (t d)")
-                )
-                if pieces == 1:
-                    nc.sync.dma_start(out=words[:], in_=y_codes[:])
-                elif c == 1:
-                    nc.sync.dma_start(out=words[:, 0 : 2 * step], in_=y_codes[:, 0 : 2 * step])
-                elif c == 2:
-                    nc.sync.dma_start(out=words[:, 2 * step : T], in_=y_codes[:, 2 * step : T])
+            stored = 0
+            for tile, lo, hi in zip(y_bf[s], cuts[s], cuts[s][1:]):
+                nc.vector.quantize_mx(out=y_codes[:, lo:hi].bitcast(FP8X4), scales=y_s[:, lo:hi], in_=tile[:].rearrange("p t d -> p (t d)"))
+                if hi - stored >= T // 2:
+                    nc.sync.dma_start(out=words[:, stored:hi], in_=y_codes[:, stored:hi])
+                    stored = hi
             for q in range(4):
-                queue = nc.scalar if pieces > 1 and q % 2 else nc.sync
+                queue = nc.scalar if s == 1 and q % 2 else nc.sync
                 queue.dma_start(out=out_2[s, 4 * q : 4 * q + 4, :].bitcast(I32), in_=y_s[32 * q : 32 * q + 4, :].bitcast(I32))
 
         da[0] = keep.tile([P, PACK, HALF], F32, name="da_first")
         factor = keep.tile([P, PACK, HALF], F32, name="factor_first", tag="factor")
-        for t in range(PACK):
+        for i in range(2):
             nc.vector.scalar_tensor_tensor(
-                out=factor[:, t, :], in0=a_first[t][:], scalar=0.0, in1=gate_sb[0][:], op0=ALU.is_gt, op1=ALU.mult
+                out=factor[:, 2 * i : 2 * i + 2, :], in0=a_first[i][:], scalar=0.0,
+                in1=gate_sb[0][:].unsqueeze(1).to_broadcast([P, 2, HALF]), op0=ALU.is_gt, op1=ALU.mult,
             )
+        for t in range(PACK):
             gather(0, t, factor[:, t, :])
         round_da(0, C, "window3")
         round_da(C, C, "da_bf1")
@@ -207,20 +208,20 @@ def tile_moe_sdb_relu_kernel(
         da[1] = keep.tile([P, PACK, HALF], F32, name="da_second", tag="window3", align_bytes=64)
         for t in range(PACK):
             gather(1, t, factor[:, t, :])
-        for b in range(4):
-            expert_block(0, b, "window1" if b == 3 else None)
+        expert_products(0, 0, "window1")
         round_da(HALF, HALF, "window1")
         scatter(0, 0, 0)
         quantize_da(HALF, HALF)
-        for b in range(4, 8):
-            expert_block(0, b)
-        for d in range(1, PACK):
+        expert_products(0, 1, "window2")
+        for d in (1, 3, 2):
             scatter(0, d, 0)
-        for b in range(8):
-            expert_block(1, b, "y_bf0" if b == 7 else None)
+        expert_products(1, 0, "by_slot3")
+        expert_products(1, 1, "y_bf0")
         for d in range(PACK):
             scatter(0, d, 1)
-        hand_out(0, 1)
-        for d in range(PACK):
-            scatter(1, d, 0)
-        hand_out(1, 4)
+            store_plane(0, d)
+        quantize_out(0)
+        for d, tag in ((0, "window4"), (2, "window5"), (3, "window4"), (1, "y_bf0")):
+            scatter(1, d, 0, tag)
+            store_plane(1, d)
+        quantize_out(1)

@@ -46,7 +46,7 @@ def tile_moe_sdb_relu_kernel(
         dy_s = keep.tile([P, T], U8, name="dy_s", align_bytes=64)
         w1_s = keep.tile([P, E, K], U8, name="w1_s", align_bytes=64)
         w1_codes = [keep.tile([P, 2, 2 * K], U8, name=f"w1_codes{i}", align_bytes=64) for i in range(2)]
-        a_first = [keep.tile([P, 2, HALF], F32, name=f"a_first{i}") for i in range(2)]
+        a_first = [keep.tile([P, HALF], F32, name=f"a_first{t}") for t in range(PACK)]
         a_second = keep.tile([P, PACK, HALF], F32, name="a_second")
         gate_sb = [keep.tile([P, HALF], F32, name=f"gate{i}") for i in range(2)]
         ident = keep.tile([P, P], F32, name="ident")
@@ -59,10 +59,10 @@ def tile_moe_sdb_relu_kernel(
         nc.sync.dma_start(out=dy_codes[:], in_=dy_words[0].rearrange("p t d -> p (t d)").bitcast(I32))
         scale_rows([nc.sync] * 4, w2_raw_s, w2t_scales[0])
         nc.sync.dma_start(out=gate_sb[0][:], in_=gate[:, 0:HALF])
-        nc.sync.dma_start(out=a_first[0][:], in_=a_rows[:, 0:2, 0:HALF])
-        make_identity(nc, ident[:])
+        for t in range(PACK):
+            nc.sync.dma_start(out=a_first[t][:], in_=a_rows[:, t, 0:HALF])
         nc.sync.dma_start(offsets[:], offs)
-        nc.sync.dma_start(out=a_first[1][:], in_=a_rows[:, 2:4, 0:HALF])
+        make_identity(nc, ident[:])
         nc.sync.dma_start(out=gate_sb[1][:], in_=gate[:, HALF:S])
         nc.sync.dma_start(out=a_second[:], in_=a_rows[:, :, HALF:S])
         scale_rows([nc.sync] * 4, w1_s, w1t_scales.rearrange("e s b k -> (s b) e k"))
@@ -177,22 +177,18 @@ def tile_moe_sdb_relu_kernel(
             y_codes = keep.tile([P, T], I32, name=f"y_codes{s}", align_bytes=64)
             y_s = keep.tile([P, T], U8, name=f"y_s{s}", align_bytes=64)
             words = out_1[s].rearrange("p t d -> p (t d)").bitcast(I32)
-            stored = 0
             for tile, lo, hi in zip(y_bf[s], cuts[s], cuts[s][1:]):
                 nc.vector.quantize_mx(out=y_codes[:, lo:hi].bitcast(FP8X4), scales=y_s[:, lo:hi], in_=tile[:].rearrange("p t d -> p (t d)"))
-                if hi - stored >= T // 2:
-                    nc.sync.dma_start(out=words[:, stored:hi], in_=y_codes[:, stored:hi])
-                    stored = hi
+            nc.sync.dma_start(out=words, in_=y_codes[:])
             for q in range(4):
                 queue = nc.scalar if s == 1 and q % 2 else nc.sync
                 queue.dma_start(out=out_2[s, 4 * q : 4 * q + 4, :].bitcast(I32), in_=y_s[32 * q : 32 * q + 4, :].bitcast(I32))
 
         da[0] = keep.tile([P, PACK, HALF], F32, name="da_first")
         factor = keep.tile([P, PACK, HALF], F32, name="factor_first", tag="factor")
-        for i in range(2):
+        for t in range(PACK):
             nc.vector.scalar_tensor_tensor(
-                out=factor[:, 2 * i : 2 * i + 2, :], in0=a_first[i][:], scalar=0.0,
-                in1=gate_sb[0][:].unsqueeze(1).to_broadcast([P, 2, HALF]), op0=ALU.is_gt, op1=ALU.mult,
+                out=factor[:, t, :], in0=a_first[t][:], scalar=0.0, in1=gate_sb[0][:], op0=ALU.is_gt, op1=ALU.mult
             )
         for t in range(PACK):
             gather(0, t, factor[:, t, :])

@@ -19,14 +19,16 @@ P = 128
 PACK = 4
 BANK = 512
 LANES = 16
+QUADRANTS = 4
 S = E * C
 HALF = S // 2
 WINDOW = 1376
+PSUM_BUFS = 4
 
 
-def scale_rows(queues, plane, rows):
-    for q, queue in enumerate(queues):
-        queue.dma_start(out=plane[32 * q : 32 * q + 4].bitcast(I32), in_=rows[4 * q : 4 * q + 4].bitcast(I32))
+def load_scale_rows(nc, plane, rows):
+    for q in range(QUADRANTS):
+        nc.sync.dma_start(out=plane[32 * q : 32 * q + 4].bitcast(I32), in_=rows[4 * q : 4 * q + 4].bitcast(I32))
 
 
 def tile_moe_sdb_relu_kernel(
@@ -35,7 +37,7 @@ def tile_moe_sdb_relu_kernel(
     nc = tc.nc
     with ExitStack() as ctx:
         keep = ctx.enter_context(tc.tile_pool(name="keep", bufs=1))
-        psum = ctx.enter_context(tc.psum_pool(name="psum", bufs=4))
+        psum = ctx.enter_context(tc.psum_pool(name="psum", bufs=PSUM_BUFS))
 
         offsets = keep.tile([P, S // LANES], U16, name="offsets")
         w2_raw = keep.tile([P, H], I32, name="w2_raw", align_bytes=64)
@@ -54,10 +56,10 @@ def tile_moe_sdb_relu_kernel(
         nc.gpsimd.memset(w2_raw_s[:].bitcast(I32), 0)
 
         a_rows = a.rearrange("(p t) j -> p t j", t=PACK)
-        scale_rows([nc.sync] * 4, dy_s, dy_scales[0])
+        load_scale_rows(nc, dy_s, dy_scales[0])
         nc.sync.dma_start(out=w2_raw[:], in_=w2t_words[0].rearrange("p i d -> p (i d)").bitcast(I32))
         nc.sync.dma_start(out=dy_codes[:], in_=dy_words[0].rearrange("p t d -> p (t d)").bitcast(I32))
-        scale_rows([nc.sync] * 4, w2_raw_s, w2t_scales[0])
+        load_scale_rows(nc, w2_raw_s, w2t_scales[0])
         nc.sync.dma_start(out=gate_sb[0][:], in_=gate[:, 0:HALF])
         for t in range(PACK):
             nc.sync.dma_start(out=a_first[t][:], in_=a_rows[:, t, 0:HALF])
@@ -65,7 +67,7 @@ def tile_moe_sdb_relu_kernel(
         make_identity(nc, ident[:])
         nc.sync.dma_start(out=gate_sb[1][:], in_=gate[:, HALF:S])
         nc.sync.dma_start(out=a_second[:], in_=a_rows[:, :, HALF:S])
-        scale_rows([nc.sync] * 4, w1_s, w1t_scales.rearrange("e s b k -> (s b) e k"))
+        load_scale_rows(nc, w1_s, w1t_scales.rearrange("e s b k -> (s b) e k"))
         w1_rows = w1t_words.rearrange("e s p c -> (s p) e c")
         for i in range(2):
             nc.sync.dma_start(out=w1_codes[i][:].bitcast(I32), in_=w1_rows[:, 2 * i : 2 * i + 2, :].bitcast(I32))
@@ -95,9 +97,10 @@ def tile_moe_sdb_relu_kernel(
 
         da, da_bf, da_codes, da_s = {}, {}, {}, {}
 
-        def gather(i, t, factor):
-            slots = offsets[:, i * HALF // LANES : (i + 1) * HALF // LANES]
-            nc.vector.tensor_tensor(da[i][:, t, :], dc[t][:].indirect(slots), factor, ALU.mult)
+        def gather(half, t, factor, first=0, width=HALF):
+            slots = offsets[:, (half * HALF + first) // LANES : (half * HALF + first + width) // LANES]
+            cols = slice(first, first + width)
+            nc.vector.tensor_tensor(da[half][:, t, cols], dc[t][:].indirect(slots), factor[:, cols], ALU.mult)
 
         def round_da(first, width, tag):
             da_bf[first] = keep.tile([P, width, PACK], BF16, name=f"da_bf{first}", tag=tag, align_bytes=64)
@@ -107,7 +110,9 @@ def tile_moe_sdb_relu_kernel(
         def quantize_da(first, width):
             codes = keep.tile([P, width], I32, name=f"da_codes{first}", align_bytes=64)
             scales = keep.tile([P, width], U8, name=f"da_s{first}", align_bytes=64)
-            nc.vector.quantize_mx(out=codes[:].bitcast(FP8X4), scales=scales[:], in_=da_bf[first][:].rearrange("p j t -> p (j t)"))
+            nc.vector.quantize_mx(
+                out=codes[:].bitcast(FP8X4), scales=scales[:], in_=da_bf[first][:].rearrange("p j t -> p (j t)")
+            )
             for u in range(width // P):
                 da_codes[first // P + u] = codes[:, u * P : (u + 1) * P]
                 da_s[first // P + u] = scales[:, u * P : (u + 1) * P]
@@ -117,10 +122,11 @@ def tile_moe_sdb_relu_kernel(
             [keep.tile([P, PACK, S], F32, name="dx1")],
         ]
 
-        def expert_products(s, i, tag):
+        def expert_products(s, half, last_tag):
+            blocks = HALF // P
             by_slot = []
-            for u in range(HALF // P):
-                b = i * HALF // P + u
+            for u in range(blocks):
+                b = half * blocks + u
                 e = b * P // C
                 acc = psum.tile([P, BANK], F32, name="acc")
                 nc.tensor.matmul_mx(
@@ -132,43 +138,44 @@ def tile_moe_sdb_relu_kernel(
                     start=True,
                     stop=True,
                 )
-                tile = keep.tile([P, PACK, P], F32, name="by_slot", tag=tag if u == 3 else f"by_slot{u}", align_bytes=64)
-                nc.scalar.copy(out=tile[:], in_=acc[:].rearrange("p (m d) -> p d m", d=PACK))
-                by_slot.append(tile)
+                tag = last_tag if u == blocks - 1 else f"by_slot{u}"
+                sorted_k = keep.tile([P, PACK, P], F32, name="by_slot", tag=tag, align_bytes=64)
+                nc.scalar.copy(out=sorted_k[:], in_=acc[:].rearrange("p (m d) -> p d m", d=PACK))
+                by_slot.append(sorted_k)
             for d in range(PACK):
                 turned = psum.tile([P, HALF], F32, name="turned")
-                for u, tile in enumerate(by_slot):
-                    nc.tensor.transpose(turned[:, u * P : (u + 1) * P], tile[:, d, :], ident[:])
-                if s == 0:
-                    nc.scalar.copy(out=dx[s][i][:, d, :], in_=turned[:])
-                else:
-                    nc.scalar.copy(out=dx[s][0][:, d, i * HALF : (i + 1) * HALF], in_=turned[:])
+                for u in range(blocks):
+                    nc.tensor.transpose(turned[:, u * P : (u + 1) * P], by_slot[u][:, d, :], ident[:])
+                rows = dx[0][half][:, d, :] if s == 0 else dx[1][0][:, d, half * HALF : (half + 1) * HALF]
+                nc.scalar.copy(out=rows, in_=turned[:])
 
         windows = {}
 
         def scatter(s, d, part, tag=None):
             if part == 0:
-                windows[s, d] = keep.tile([P, WINDOW], F32, name=f"window{s}{d}", tag=tag or f"window{d}", align_bytes=64)
+                windows[s, d] = keep.tile([P, WINDOW], F32, name=f"window{s}{d}", tag=tag, align_bytes=64)
             width = S // len(dx[s])
             slots = offsets[:, part * width // LANES : (part + 1) * width // LANES]
             nc.vector.tensor_copy(windows[s, d][:].indirect(slots), dx[s][part][:, d, :])
 
         out_rows = out_0.rearrange("(s p d) t -> s d p t", p=P, d=PACK)
 
-        y_bf = {}
         cuts = [[0, T], [0, T // 2, 3 * T // 4, T]]
+        last_set = (1, 1)
+        y_tags = [["hold_y"], ["y_half", "y_third_quarter", "y_last_quarter"]]
+        y_bf = {}
 
-        def store_plane(s, d):
+        def hand_out(s, d):
             spans = [slice(lo, hi) for lo, hi in zip(cuts[s], cuts[s][1:])]
             if s not in y_bf:
                 y_bf[s] = [
-                    keep.tile([P, cols.stop - cols.start, PACK], BF16, name=f"y_bf{s}{c}", tag=f"y_bf{s + c}", align_bytes=64)
+                    keep.tile([P, cols.stop - cols.start, PACK], BF16, name=f"y_bf{s}{c}", tag=y_tags[s][c], align_bytes=64)
                     for c, cols in enumerate(spans)
                 ]
             window = windows[s, d]
             nc.sync.dma_start(out=out_rows[s, d], in_=window[:, 0:T])
             for c, cols in enumerate(spans):
-                if (s, d, c) == (1, 1, 0):
+                if (s, d) == last_set and c == 0:
                     nc.vector.tensor_copy(out=y_bf[s][c][:, :, d], in_=window[:, cols])
                 else:
                     nc.scalar.copy(out=y_bf[s][c][:, :, d], in_=window[:, cols])
@@ -177,47 +184,64 @@ def tile_moe_sdb_relu_kernel(
             y_codes = keep.tile([P, T], I32, name=f"y_codes{s}", align_bytes=64)
             y_s = keep.tile([P, T], U8, name=f"y_s{s}", align_bytes=64)
             words = out_1[s].rearrange("p t d -> p (t d)").bitcast(I32)
-            for tile, lo, hi in zip(y_bf[s], cuts[s], cuts[s][1:]):
-                nc.vector.quantize_mx(out=y_codes[:, lo:hi].bitcast(FP8X4), scales=y_s[:, lo:hi], in_=tile[:].rearrange("p t d -> p (t d)"))
+            for woven, lo, hi in zip(y_bf[s], cuts[s], cuts[s][1:]):
+                nc.vector.quantize_mx(
+                    out=y_codes[:, lo:hi].bitcast(FP8X4), scales=y_s[:, lo:hi], in_=woven[:].rearrange("p t d -> p (t d)")
+                )
             nc.sync.dma_start(out=words, in_=y_codes[:])
-            for q in range(4):
+            for q in range(QUADRANTS):
                 queue = nc.scalar if s == 1 and q % 2 else nc.sync
-                queue.dma_start(out=out_2[s, 4 * q : 4 * q + 4, :].bitcast(I32), in_=y_s[32 * q : 32 * q + 4, :].bitcast(I32))
+                queue.dma_start(
+                    out=out_2[s, 4 * q : 4 * q + 4, :].bitcast(I32), in_=y_s[32 * q : 32 * q + 4, :].bitcast(I32)
+                )
 
         da[0] = keep.tile([P, PACK, HALF], F32, name="da_first")
-        factor = keep.tile([P, PACK, HALF], F32, name="factor_first", tag="factor")
+        factor_first = keep.tile([P, PACK, HALF], F32, name="factor_first", tag="hold_factor", align_bytes=64)
         for t in range(PACK):
             nc.vector.scalar_tensor_tensor(
-                out=factor[:, t, :], in0=a_first[t][:], scalar=0.0, in1=gate_sb[0][:], op0=ALU.is_gt, op1=ALU.mult
+                out=factor_first[:, t, :], in0=a_first[t][:], scalar=0.0, in1=gate_sb[0][:], op0=ALU.is_gt, op1=ALU.mult
             )
+        for t in range(PACK - 1):
+            gather(0, t, factor_first[:, t, :])
+        gather(0, PACK - 1, factor_first[:, PACK - 1, :], 0, C)
+        gather(0, PACK - 1, factor_first[:, PACK - 1, :], C, C)
+        round_da(0, C, "hold_expert0")
+        round_da(C, C, "hold_expert1")
+
+        factor_second = []
+        for i, tag in enumerate(("hold_factor", "hold_expert0")):
+            pair = keep.tile([P, 2, HALF], F32, name="factor_second", tag=tag, align_bytes=64)
+            nc.vector.scalar_tensor_tensor(
+                out=pair[:],
+                in0=a_second[:, 2 * i : 2 * i + 2, :],
+                scalar=0.0,
+                in1=gate_sb[1][:].unsqueeze(1).to_broadcast([P, 2, HALF]),
+                op0=ALU.is_gt,
+                op1=ALU.mult,
+            )
+            quantize_da(i * C, C)
+            factor_second.append(pair)
+        da[1] = keep.tile([P, PACK, HALF], F32, name="da_second", tag="hold_expert1", align_bytes=64)
         for t in range(PACK):
-            gather(0, t, factor[:, t, :])
-        round_da(0, C, "window3")
-        round_da(C, C, "da_bf1")
-        factor = keep.tile([P, PACK, HALF], F32, name="factor_second", tag="factor")
-        nc.vector.scalar_tensor_tensor(
-            out=factor[:], in0=a_second[:], scalar=0.0, in1=gate_sb[1][:].unsqueeze(1).to_broadcast([P, PACK, HALF]),
-            op0=ALU.is_gt, op1=ALU.mult,
-        )
-        quantize_da(0, C)
-        quantize_da(C, C)
-        da[1] = keep.tile([P, PACK, HALF], F32, name="da_second", tag="window3", align_bytes=64)
-        for t in range(PACK):
-            gather(1, t, factor[:, t, :])
-        expert_products(0, 0, "window1")
-        round_da(HALF, HALF, "window1")
-        scatter(0, 0, 0)
+            gather(1, t, factor_second[t // 2][:, t % 2, :])
+
+        expert_products(0, 0, "hold_second")
+        round_da(HALF, HALF, "hold_second")
+        scatter(0, 0, 0, "window00")
+        scatter(0, 2, 0, "window02")
         quantize_da(HALF, HALF)
-        expert_products(0, 1, "window2")
-        for d in (1, 3, 2):
-            scatter(0, d, 0)
+        expert_products(0, 1, "by_slot3")
+        scatter(0, 1, 0, "hold_second")
+        scatter(0, 3, 0, "hold_expert1")
+
         expert_products(1, 0, "by_slot3")
-        expert_products(1, 1, "y_bf0")
+        expert_products(1, 1, "hold_y")
         for d in range(PACK):
             scatter(0, d, 1)
-            store_plane(0, d)
+            hand_out(0, d)
         quantize_out(0)
-        for d, tag in ((0, "window4"), (2, "window5"), (3, "window4"), (1, "y_bf0")):
+
+        for d, tag in ((0, "hold_pair"), (2, "window12"), (3, "hold_pair"), (last_set[1], "hold_y")):
             scatter(1, d, 0, tag)
-            store_plane(1, d)
+            hand_out(1, d)
         quantize_out(1)

@@ -1,7 +1,6 @@
 from contextlib import ExitStack
 
 import concourse.mybir as mybir
-from concourse.masks import make_identity
 
 K, T, E, C, H, N = 1024, 1024, 4, 256, 512, 512
 FLOPS = 2 * N * H * T + 2 * H * K * E * C
@@ -14,6 +13,7 @@ U8 = mybir.dt.uint8
 FP8X4 = mybir.dt.float8_e4m3fn_x4
 FP4X4 = mybir.dt.float4_e2m1fn_x4
 ALU = mybir.AluOpType
+COPY = mybir.ActivationFunctionType.Copy
 
 P = 128
 PACK = 4
@@ -22,8 +22,9 @@ LANES = 16
 QUADRANTS = 4
 S = E * C
 HALF = S // 2
-WINDOW = 1376
-PSUM_BUFS = 4
+PASS = P * PACK
+BANKS = 4
+RUN = 4
 
 
 def load_scale_rows(nc, plane, rows):
@@ -37,7 +38,21 @@ def tile_moe_sdb_relu_kernel(
     nc = tc.nc
     with ExitStack() as ctx:
         keep = ctx.enter_context(tc.tile_pool(name="keep", bufs=1))
-        psum = ctx.enter_context(tc.psum_pool(name="psum", bufs=PSUM_BUFS))
+        turns = ctx.enter_context(tc.tile_pool(name="turns", bufs=1))
+        psum = ctx.enter_context(tc.psum_pool(name="psum", bufs=1))
+        taken = []
+
+        def next_bank():
+            taken.append(len(taken))
+            return psum.tile([P, BANK], F32, name="acc", tag=f"bank{taken[-1] % BANKS}")
+
+        def copy(engine, out, in_):
+            if engine == "vector":
+                nc.vector.tensor_copy(out=out, in_=in_)
+            else:
+                nc.scalar.copy(out=out, in_=in_)
+
+        groups = [(0, C), (C, C), (HALF, HALF)]
 
         offsets = keep.tile([P, S // LANES], U16, name="offsets")
         w2_raw = keep.tile([P, H], I32, name="w2_raw", align_bytes=64)
@@ -46,31 +61,29 @@ def tile_moe_sdb_relu_kernel(
         w2_s = keep.tile([P, H], U8, name="w2_s", align_bytes=64)
         dy_codes = keep.tile([P, T], I32, name="dy_codes", align_bytes=64)
         dy_s = keep.tile([P, T], U8, name="dy_s", align_bytes=64)
-        w1_s = keep.tile([P, E, K], U8, name="w1_s", align_bytes=64)
-        w1_codes = [keep.tile([P, 2, 2 * K], U8, name=f"w1_codes{i}", align_bytes=64) for i in range(2)]
-        a_first = [keep.tile([P, HALF], F32, name=f"a_first{t}") for t in range(PACK)]
-        a_second = keep.tile([P, PACK, HALF], F32, name="a_second")
+        w1_raw_s = keep.tile([P, E, K], U8, name="w1_raw_s", align_bytes=64)
+        w1_raw = [keep.tile([P, 2, 2 * K], U8, name=f"w1_raw{i}", align_bytes=64) for i in range(2)]
+        a_sb = [keep.tile([P, PACK, width], F32, name=f"a{g}") for g, (first, width) in enumerate(groups)]
         gate_sb = [keep.tile([P, HALF], F32, name=f"gate{i}") for i in range(2)]
-        ident = keep.tile([P, P], F32, name="ident")
 
         nc.gpsimd.memset(w2_raw_s[:].bitcast(I32), 0)
+        nc.gpsimd.memset(w1_raw_s[:].bitcast(I32), 0)
 
         a_rows = a.rearrange("(p t) j -> p t j", t=PACK)
+        w1_rows = w1t_words.rearrange("e s p c -> (s p) e c")
         load_scale_rows(nc, dy_s, dy_scales[0])
         nc.sync.dma_start(out=w2_raw[:], in_=w2t_words[0].rearrange("p i d -> p (i d)").bitcast(I32))
         nc.sync.dma_start(out=dy_codes[:], in_=dy_words[0].rearrange("p t d -> p (t d)").bitcast(I32))
         load_scale_rows(nc, w2_raw_s, w2t_scales[0])
         nc.sync.dma_start(out=gate_sb[0][:], in_=gate[:, 0:HALF])
-        for t in range(PACK):
-            nc.sync.dma_start(out=a_first[t][:], in_=a_rows[:, t, 0:HALF])
+        nc.sync.dma_start(out=a_sb[0][:], in_=a_rows[:, :, 0:C])
         nc.sync.dma_start(offsets[:], offs)
-        make_identity(nc, ident[:])
+        nc.sync.dma_start(out=a_sb[1][:], in_=a_rows[:, :, C:HALF])
+        load_scale_rows(nc, w1_raw_s, w1t_scales.rearrange("e s b k -> (s b) e k"))
+        nc.sync.dma_start(out=w1_raw[0][:].bitcast(I32), in_=w1_rows[:, 0:2, :].bitcast(I32))
         nc.sync.dma_start(out=gate_sb[1][:], in_=gate[:, HALF:S])
-        nc.sync.dma_start(out=a_second[:], in_=a_rows[:, :, HALF:S])
-        load_scale_rows(nc, w1_s, w1t_scales.rearrange("e s b k -> (s b) e k"))
-        w1_rows = w1t_words.rearrange("e s p c -> (s p) e c")
-        for i in range(2):
-            nc.sync.dma_start(out=w1_codes[i][:].bitcast(I32), in_=w1_rows[:, 2 * i : 2 * i + 2, :].bitcast(I32))
+        nc.sync.dma_start(out=a_sb[2][:], in_=a_rows[:, :, HALF:S])
+        nc.sync.dma_start(out=w1_raw[1][:].bitcast(I32), in_=w1_rows[:, 2:4, :].bitcast(I32))
 
         nc.vector.tensor_copy(
             out=w2_codes[:].rearrange("p (t m) -> p m t", t=PACK), in_=w2_raw[:].rearrange("p (m t) -> p m t", t=PACK)
@@ -79,169 +92,247 @@ def tile_moe_sdb_relu_kernel(
             out=w2_s[:].rearrange("p (t m) -> p m t", t=PACK), in_=w2_raw_s[:].rearrange("p (m t) -> p m t", t=PACK)
         )
 
-        dc = [keep.tile([P, T], F32, name=f"dc{t}") for t in range(PACK)]
-        for t in range(PACK):
-            for h in range(T // BANK):
-                cols = slice(h * BANK, (h + 1) * BANK)
-                acc = psum.tile([P, BANK], F32, name="acc")
-                nc.tensor.matmul_mx(
-                    out=acc[:],
-                    lhsT=w2_codes[:, t * P : (t + 1) * P].bitcast(FP8X4),
-                    lhsT_scale=w2_s[:, t * P : (t + 1) * P],
-                    rhs=dy_codes[:, cols].bitcast(FP8X4),
-                    rhs_scale=dy_s[:, cols],
-                    start=True,
-                    stop=True,
-                )
-                nc.scalar.copy(out=dc[t][:, cols], in_=acc[:])
+        factor, da, da_bf, da_codes, da_s = {}, {}, {}, {}, {}
 
-        da, da_bf, da_codes, da_s = {}, {}, {}, {}
-
-        def gather(half, t, factor, first=0, width=HALF):
-            slots = offsets[:, (half * HALF + first) // LANES : (half * HALF + first + width) // LANES]
-            cols = slice(first, first + width)
-            nc.vector.tensor_tensor(da[half][:, t, cols], dc[t][:].indirect(slots), factor[:, cols], ALU.mult)
-
-        def round_da(first, width, tag):
-            da_bf[first] = keep.tile([P, width, PACK], BF16, name=f"da_bf{first}", tag=tag, align_bytes=64)
-            cols = slice(first % HALF, first % HALF + width)
-            nc.scalar.copy(out=da_bf[first][:], in_=da[first // HALF][:, :, cols].rearrange("p t j -> p j t"))
-
-        def quantize_da(first, width):
-            codes = keep.tile([P, width], I32, name=f"da_codes{first}", align_bytes=64)
-            scales = keep.tile([P, width], U8, name=f"da_s{first}", align_bytes=64)
-            nc.vector.quantize_mx(
-                out=codes[:].bitcast(FP8X4), scales=scales[:], in_=da_bf[first][:].rearrange("p j t -> p (j t)")
-            )
-            for u in range(width // P):
-                da_codes[first // P + u] = codes[:, u * P : (u + 1) * P]
-                da_s[first // P + u] = scales[:, u * P : (u + 1) * P]
-
-        dx = [
-            [keep.tile([P, PACK, HALF], F32, name="dx00"), keep.tile([P, PACK, HALF], F32, name="dx01")],
-            [keep.tile([P, PACK, S], F32, name="dx1")],
-        ]
-
-        def expert_products(s, half, last_tag):
-            blocks = HALF // P
-            by_slot = []
-            for u in range(blocks):
-                b = half * blocks + u
-                e = b * P // C
-                acc = psum.tile([P, BANK], F32, name="acc")
-                nc.tensor.matmul_mx(
-                    out=acc[:],
-                    lhsT=da_codes[b].bitcast(FP8X4),
-                    lhsT_scale=da_s[b],
-                    rhs=w1_codes[e // 2][:, e % 2, 2 * s * BANK : 2 * (s + 1) * BANK].bitcast(FP4X4),
-                    rhs_scale=w1_s[:, e, s * BANK : (s + 1) * BANK],
-                    start=True,
-                    stop=True,
-                )
-                tag = last_tag if u == blocks - 1 else f"by_slot{u}"
-                sorted_k = keep.tile([P, PACK, P], F32, name="by_slot", tag=tag, align_bytes=64)
-                nc.scalar.copy(out=sorted_k[:], in_=acc[:].rearrange("p (m d) -> p d m", d=PACK))
-                by_slot.append(sorted_k)
-            for d in range(PACK):
-                turned = psum.tile([P, HALF], F32, name="turned")
-                for u in range(blocks):
-                    nc.tensor.transpose(turned[:, u * P : (u + 1) * P], by_slot[u][:, d, :], ident[:])
-                rows = dx[0][half][:, d, :] if s == 0 else dx[1][0][:, d, half * HALF : (half + 1) * HALF]
-                nc.scalar.copy(out=rows, in_=turned[:])
-
-        windows = {}
-
-        def scatter(s, d, part, tag=None):
-            if part == 0:
-                windows[s, d] = keep.tile([P, WINDOW], F32, name=f"window{s}{d}", tag=tag, align_bytes=64)
-            width = S // len(dx[s])
-            slots = offsets[:, part * width // LANES : (part + 1) * width // LANES]
-            nc.vector.tensor_copy(windows[s, d][:].indirect(slots), dx[s][part][:, d, :])
-
-        out_rows = out_0.rearrange("(s p d) t -> s d p t", p=P, d=PACK)
-
-        cuts = [[0, T], [0, T // 2, 3 * T // 4, T]]
-        last_set = (1, 1)
-        y_tags = [["hold_y"], ["y_half", "y_third_quarter", "y_last_quarter"]]
-        y_bf = {}
-
-        def hand_out(s, d):
-            spans = [slice(lo, hi) for lo, hi in zip(cuts[s], cuts[s][1:])]
-            if s not in y_bf:
-                y_bf[s] = [
-                    keep.tile([P, cols.stop - cols.start, PACK], BF16, name=f"y_bf{s}{c}", tag=y_tags[s][c], align_bytes=64)
-                    for c, cols in enumerate(spans)
-                ]
-            window = windows[s, d]
-            nc.sync.dma_start(out=out_rows[s, d], in_=window[:, 0:T])
-            for c, cols in enumerate(spans):
-                if (s, d) == last_set and c == 0:
-                    nc.vector.tensor_copy(out=y_bf[s][c][:, :, d], in_=window[:, cols])
-                else:
-                    nc.scalar.copy(out=y_bf[s][c][:, :, d], in_=window[:, cols])
-
-        def quantize_out(s):
-            y_codes = keep.tile([P, T], I32, name=f"y_codes{s}", align_bytes=64)
-            y_s = keep.tile([P, T], U8, name=f"y_s{s}", align_bytes=64)
-            words = out_1[s].rearrange("p t d -> p (t d)").bitcast(I32)
-            for woven, lo, hi in zip(y_bf[s], cuts[s], cuts[s][1:]):
-                nc.vector.quantize_mx(
-                    out=y_codes[:, lo:hi].bitcast(FP8X4), scales=y_s[:, lo:hi], in_=woven[:].rearrange("p t d -> p (t d)")
-                )
-            nc.sync.dma_start(out=words, in_=y_codes[:])
-            for q in range(QUADRANTS):
-                queue = nc.scalar if s == 1 and q % 2 else nc.sync
-                queue.dma_start(
-                    out=out_2[s, 4 * q : 4 * q + 4, :].bitcast(I32), in_=y_s[32 * q : 32 * q + 4, :].bitcast(I32)
-                )
-
-        da[0] = keep.tile([P, PACK, HALF], F32, name="da_first")
-        factor_first = keep.tile([P, PACK, HALF], F32, name="factor_first", tag="hold_factor", align_bytes=64)
-        for t in range(PACK):
+        def make_factor(g):
+            first, width = groups[g]
+            tag = "hold_factor" if g == 2 else f"factor{g}"
+            factor[g] = keep.tile([P, PACK, width], F32, name=f"factor{g}", tag=tag, align_bytes=64)
+            gates = gate_sb[first // HALF][:, first % HALF : first % HALF + width]
             nc.vector.scalar_tensor_tensor(
-                out=factor_first[:, t, :], in0=a_first[t][:], scalar=0.0, in1=gate_sb[0][:], op0=ALU.is_gt, op1=ALU.mult
-            )
-        for t in range(PACK - 1):
-            gather(0, t, factor_first[:, t, :])
-        gather(0, PACK - 1, factor_first[:, PACK - 1, :], 0, C)
-        gather(0, PACK - 1, factor_first[:, PACK - 1, :], C, C)
-        round_da(0, C, "hold_expert0")
-        round_da(C, C, "hold_expert1")
-
-        factor_second = []
-        for i, tag in enumerate(("hold_factor", "hold_expert0")):
-            pair = keep.tile([P, 2, HALF], F32, name="factor_second", tag=tag, align_bytes=64)
-            nc.vector.scalar_tensor_tensor(
-                out=pair[:],
-                in0=a_second[:, 2 * i : 2 * i + 2, :],
+                out=factor[g][:],
+                in0=a_sb[g][:],
                 scalar=0.0,
-                in1=gate_sb[1][:].unsqueeze(1).to_broadcast([P, 2, HALF]),
+                in1=gates.unsqueeze(1).to_broadcast([P, PACK, width]),
                 op0=ALU.is_gt,
                 op1=ALU.mult,
             )
-            quantize_da(i * C, C)
-            factor_second.append(pair)
-        da[1] = keep.tile([P, PACK, HALF], F32, name="da_second", tag="hold_expert1", align_bytes=64)
+
+        def slots(first, width):
+            return offsets[:, first // LANES : (first + width) // LANES]
+
+        dc = [keep.tile([P, T], F32, name=f"dc{t}") for t in range(PACK)]
+
+        def first_product(t, h, engine):
+            cols = slice(h * BANK, (h + 1) * BANK)
+            acc = next_bank()
+            nc.tensor.matmul_mx(
+                out=acc[:],
+                lhsT=w2_codes[:, t * P : (t + 1) * P].bitcast(FP8X4),
+                lhsT_scale=w2_s[:, t * P : (t + 1) * P],
+                rhs=dy_codes[:, cols].bitcast(FP8X4),
+                rhs_scale=dy_s[:, cols],
+                start=True,
+                stop=True,
+            )
+            copy(engine, dc[t][:, cols], acc[:])
+
+        def gather(g, t, engine):
+            first, width = groups[g]
+            if g not in da:
+                da[g] = keep.tile([P, PACK, width], F32, name=f"da{g}", tag=f"hold_da{g}", align_bytes=64)
+            picked = dc[t][:].indirect(slots(first, width))
+            if engine == "vector":
+                nc.vector.tensor_tensor(da[g][:, t, :], picked, factor[g][:, t, :], ALU.mult)
+            else:
+                nc.scalar.activation(da[g][:, t, :], picked, COPY)
+
+        def by_runs(rows):
+            return rows.rearrange("p t (c i) -> p c t i", i=RUN)
+
+        def woven_by_runs(woven):
+            return woven.rearrange("p (c i) t -> p c t i", i=RUN)
+
+        def round_da(g, times_factor):
+            first, width = groups[g]
+            tag = "hold_factor" if g == 0 else f"da_bf{g}"
+            da_bf[g] = keep.tile([P, width, PACK], BF16, name=f"da_bf{g}", tag=tag, align_bytes=64)
+            if times_factor:
+                nc.vector.tensor_tensor(woven_by_runs(da_bf[g][:]), by_runs(da[g][:]), by_runs(factor[g][:]), ALU.mult)
+            else:
+                nc.vector.tensor_copy(out=woven_by_runs(da_bf[g][:]), in_=by_runs(da[g][:]))
+
+        def quantize_da(g):
+            first, width = groups[g]
+            codes = keep.tile([P, width], I32, name=f"da_codes{g}", align_bytes=64)
+            scales = keep.tile([P, width], U8, name=f"da_s{g}", align_bytes=64)
+            nc.vector.quantize_mx(
+                out=codes[:].bitcast(FP8X4), scales=scales[:], in_=da_bf[g][:].rearrange("p j t -> p (j t)")
+            )
+            for u in range(width // C):
+                da_codes[first // C + u] = codes[:, u * C : (u + 1) * C]
+                da_s[first // C + u] = scales[:, u * C : (u + 1) * C]
+
+        def second_product(out, w, e):
+            s, j = divmod(w, PACK)
+            if s == 0:
+                codes = w1_raw[e // 2][:, e % 2, 2 * j * P : 2 * (j + 1) * P]
+                scales = w1_raw_s[:, e, j * P : (j + 1) * P]
+            else:
+                codes = w1_codes[:, e, 2 * j * P : 2 * (j + 1) * P]
+                scales = w1_s[:, e, j * P : (j + 1) * P]
+            nc.tensor.matmul_mx(
+                out=out,
+                lhsT=codes.bitcast(FP4X4),
+                lhsT_scale=scales,
+                rhs=da_codes[e].bitcast(FP8X4),
+                rhs_scale=da_s[e],
+                start=True,
+                stop=True,
+            )
+
+        dx = {}
+
+        def dx_one_expert(e, w, engine):
+            acc = next_bank()
+            for u in range(2):
+                second_product(acc[:, u * C : (u + 1) * C], w + u, e)
+            both = keep.tile([P, BANK], F32, name=f"dx_e{e}w{w}")
+            copy(engine, both[:], acc[:])
+            for u in range(2):
+                dx[w + u, e * C] = both[:, u * C : (u + 1) * C]
+
+        def dx_two_experts(w, h, engine):
+            acc = next_bank()
+            for u in range(2):
+                second_product(acc[:, u * C : (u + 1) * C], w, 2 * h + u)
+            base = 0 if w >= PACK else HALF
+            if (w, base) not in dx:
+                dx[w, base] = keep.tile([P, S - base], F32, name=f"dx_w{w}")[:]
+            copy(engine, dx[w, base][:, h * HALF - base : (h + 1) * HALF - base], acc[:])
+
+        windows = [keep.tile([P, T], F32, name=f"window{w}") for w in range(2 * PACK)]
+
+        def scatter(w, base, first, width, engine):
+            source = dx[w, base][:, first - base : first - base + width]
+            placed = windows[w][:].indirect(slots(first, width))
+            if engine == "vector":
+                nc.vector.tensor_copy(placed, source)
+            else:
+                nc.scalar.activation(placed, source, COPY)
+
+        dealt_rows = out_0[PASS:K].rearrange("(p d) t -> d p t", d=PACK)
+
+        quad = turns.tile([P, PACK, T], F32, name="quad", offset=0, align_bytes=64)
+
+        def store_window(w):
+            rows = out_0[w * P : (w + 1) * P] if w < PACK else dealt_rows[w - PACK]
+            nc.sync.dma_start(out=rows, in_=windows[w][:])
+            if w < PACK:
+                for d in range(PACK):
+                    nc.sync.dma_start(out=quad[32 * w : 32 * w + 32, d, :], in_=windows[w][d:P:PACK, :])
+
+        y_codes = [keep.tile([P, T], I32, name=f"y_codes{s}", align_bytes=64) for s in range(2)]
+        y_s = [keep.tile([P, T], U8, name=f"y_s{s}", align_bytes=64) for s in range(2)]
+
+        def quantize_y(s, woven, lo, hi):
+            nc.vector.quantize_mx(
+                out=y_codes[s][:, lo:hi].bitcast(FP8X4),
+                scales=y_s[s][:, lo:hi],
+                in_=woven[:].rearrange("p t d -> p (t d)"),
+            )
+
+        def store_planes(s):
+            nc.sync.dma_start(out=out_1[s].rearrange("p t d -> p (t d)").bitcast(I32), in_=y_codes[s][:])
+            for q in range(QUADRANTS):
+                queue = nc.scalar if s == 1 and q % 2 else nc.sync
+                queue.dma_start(
+                    out=out_2[s, 4 * q : 4 * q + 4, :].bitcast(I32), in_=y_s[s][32 * q : 32 * q + 4, :].bitcast(I32)
+                )
+
+        make_factor(0)
         for t in range(PACK):
-            gather(1, t, factor_second[t // 2][:, t % 2, :])
+            first_product(t, 0, "scalar")
+            first_product(t, 1, "vector" if t < 1 else "scalar")
+        gather(0, 0, "vector")
+        gather(0, 1, "vector")
+        gather(0, 2, "vector")
+        gather(0, 3, "vector")
+        round_da(0, False)
+        quantize_da(0)
+        make_factor(1)
+        for t in range(PACK):
+            gather(1, t, "scalar")
+        round_da(1, True)
+        make_factor(2)
+        quantize_da(1)
+        for e in range(2):
+            for w in (0, 2):
+                dx_one_expert(e, w, "scalar")
+            for w in range(PACK):
+                scatter(w, e * C, e * C, C, "scalar")
+        for t in range(PACK):
+            gather(2, t, "vector")
+        round_da(2, False)
+        w1_codes = keep.tile([P, E, 2 * PASS], U8, name="w1_codes", tag="hold_factor", align_bytes=64)
+        w1_s = keep.tile([P, E, PASS], U8, name="w1_s", tag="hold_da2", align_bytes=64)
+        for i in range(2):
+            nc.vector.tensor_copy(
+                out=w1_codes[:, 2 * i : 2 * i + 2, :].bitcast(U16).rearrange("p e (d m) -> p e d m", d=PACK),
+                in_=w1_raw[i][:, :, 2 * PASS : 2 * K].bitcast(U16).rearrange("p e (m d) -> p e d m", d=PACK),
+            )
+        quantize_da(2)
+        nc.vector.tensor_copy(
+            out=w1_s[:].rearrange("p e (d m) -> p e d m", d=PACK),
+            in_=w1_raw_s[:, :, PASS:K].rearrange("p e (m d) -> p e d m", d=PACK),
+        )
 
-        expert_products(0, 0, "hold_second")
-        round_da(HALF, HALF, "hold_second")
-        scatter(0, 0, 0, "window00")
-        scatter(0, 2, 0, "window02")
-        quantize_da(HALF, HALF)
-        expert_products(0, 1, "by_slot3")
-        scatter(0, 1, 0, "hold_second")
-        scatter(0, 3, 0, "hold_expert1")
+        for w in (3, 2):
+            dx_two_experts(w, 1, "vector")
+        dx_two_experts(0, 1, "scalar")
+        scatter(0, HALF, HALF, C, "scalar")
+        dx_two_experts(1, 1, "scalar")
+        scatter(0, HALF, HALF + C, C, "scalar")
+        store_window(0)
+        for w in (3, 2):
+            scatter(w, HALF, HALF, HALF, "vector")
+            store_window(w)
+        dx_two_experts(5, 0, "vector")
+        scatter(1, HALF, HALF, C, "scalar")
+        dx_two_experts(5, 1, "scalar")
+        scatter(1, HALF, HALF + C, C, "scalar")
+        store_window(1)
 
-        expert_products(1, 0, "by_slot3")
-        expert_products(1, 1, "hold_y")
-        for d in range(PACK):
-            scatter(0, d, 1)
-            hand_out(0, d)
-        quantize_out(0)
+        thirds = [(0, 384), (384, 384), (768, 256)]
+        pair = keep.tile([P, 2, T], F32, name="pair")
+        for h in range(2):
+            dx_two_experts(4, h, "scalar")
+        for h in range(2):
+            scatter(5, 0, h * HALF, HALF, "vector")
+        store_window(5)
+        nc.sync.dma_start(out=pair[:, 1, :], in_=windows[5][:])
+        for h in range(2):
+            scatter(4, 0, thirds[h][0], thirds[h][1], "scalar")
+            dx_two_experts(7, h, "scalar")
+        scatter(4, 0, thirds[2][0], thirds[2][1], "scalar")
+        store_window(4)
+        nc.sync.dma_start(out=pair[:, 0, :], in_=windows[4][:])
+        for h in range(2):
+            dx_two_experts(6, h, "scalar")
+        for h in range(2):
+            scatter(7, 0, h * HALF, HALF, "vector")
+        store_window(7)
+        for first, width in thirds:
+            scatter(6, 0, first, width, "scalar")
+        store_window(6)
 
-        for d, tag in ((0, "hold_pair"), (2, "window12"), (3, "hold_pair"), (last_set[1], "hold_y")):
-            scatter(1, d, 0, tag)
-            hand_out(1, d)
-        quantize_out(1)
+        y0 = [keep.tile([P, HALF, PACK], BF16, name=f"y0{h}", align_bytes=64) for h in range(2)]
+        for h in range(2):
+            nc.vector.tensor_copy(out=woven_by_runs(y0[h][:]), in_=by_runs(quad[:, :, h * HALF : (h + 1) * HALF]))
+        for h in range(2):
+            quantize_y(0, y0[h], h * HALF, (h + 1) * HALF)
+        store_planes(0)
+
+        cuts = [0, T // 2, 3 * T // 4, T]
+        spans = list(zip(cuts, cuts[1:]))
+        y1 = [
+            turns.tile([P, hi - lo, PACK], BF16, name=f"y1{lo}", offset=2 * PACK * lo, align_bytes=64) for lo, hi in spans
+        ]
+        for woven, (lo, hi) in zip(y1, spans):
+            nc.vector.tensor_copy(out=woven[:, :, 0:2], in_=pair[:, :, lo:hi].rearrange("p d t -> p t d"))
+        for d in (3, 2):
+            for c, (lo, hi) in enumerate(spans):
+                copy("vector" if c < 2 else "scalar", y1[c][:, :, d], windows[PACK + d][:, lo:hi])
+        for woven, (lo, hi) in zip(y1, spans):
+            quantize_y(1, woven, lo, hi)
+        store_planes(1)

@@ -23,7 +23,6 @@ QUADRANTS = 4
 S = E * C
 HALF = S // 2
 PASS = P * PACK
-BANKS = 4
 RUN = 4
 
 
@@ -40,11 +39,9 @@ def tile_moe_sdb_relu_kernel(
         keep = ctx.enter_context(tc.tile_pool(name="keep", bufs=1))
         turns = ctx.enter_context(tc.tile_pool(name="turns", bufs=1))
         psum = ctx.enter_context(tc.psum_pool(name="psum", bufs=1))
-        taken = []
 
-        def next_bank():
-            taken.append(len(taken))
-            return psum.tile([P, BANK], F32, name="acc", tag=f"bank{taken[-1] % BANKS}")
+        def bank(b):
+            return psum.tile([P, BANK], F32, name="acc", tag=f"bank{b}")
 
         def copy(engine, out, in_):
             if engine == "vector":
@@ -115,7 +112,7 @@ def tile_moe_sdb_relu_kernel(
 
         def first_product(t, h, engine):
             cols = slice(h * BANK, (h + 1) * BANK)
-            acc = next_bank()
+            acc = bank(2 * t + h)
             nc.tensor.matmul_mx(
                 out=acc[:],
                 lhsT=w2_codes[:, t * P : (t + 1) * P].bitcast(FP8X4),
@@ -127,15 +124,19 @@ def tile_moe_sdb_relu_kernel(
             )
             copy(engine, dc[t][:, cols], acc[:])
 
-        def gather(g, t, engine):
-            first, width = groups[g]
-            if g not in da:
-                da[g] = keep.tile([P, PACK, width], F32, name=f"da{g}", tag=f"hold_da{g}", align_bytes=64)
-            picked = dc[t][:].indirect(slots(first, width))
+        def factor_of(e):
+            g = min(e, 2)
+            first = e * C - groups[g][0]
+            return factor[g][:, :, first : first + C]
+
+        def gather(e, t, engine):
+            if e not in da:
+                da[e] = keep.tile([P, PACK, C], F32, name=f"da{e}", tag=f"hold_da{e}", align_bytes=64)
+            picked = dc[t][:].indirect(slots(e * C, C))
             if engine == "vector":
-                nc.vector.tensor_tensor(da[g][:, t, :], picked, factor[g][:, t, :], ALU.mult)
+                nc.vector.tensor_tensor(da[e][:, t, :], picked, factor_of(e)[:, t, :], ALU.mult)
             else:
-                nc.scalar.activation(da[g][:, t, :], picked, COPY)
+                nc.scalar.activation(da[e][:, t, :], picked, COPY)
 
         def by_runs(rows):
             return rows.rearrange("p t (c i) -> p c t i", i=RUN)
@@ -143,14 +144,17 @@ def tile_moe_sdb_relu_kernel(
         def woven_by_runs(woven):
             return woven.rearrange("p (c i) t -> p c t i", i=RUN)
 
-        def round_da(g, times_factor):
+        def round_da(e, times_factor):
+            g = min(e, 2)
             first, width = groups[g]
-            tag = "hold_factor" if g == 0 else f"da_bf{g}"
-            da_bf[g] = keep.tile([P, width, PACK], BF16, name=f"da_bf{g}", tag=tag, align_bytes=64)
+            if g not in da_bf:
+                tag = "hold_factor" if g == 0 else f"da_bf{g}"
+                da_bf[g] = keep.tile([P, width, PACK], BF16, name=f"da_bf{g}", tag=tag, align_bytes=64)
+            woven = woven_by_runs(da_bf[g][:, e * C - first : (e + 1) * C - first, :])
             if times_factor:
-                nc.vector.tensor_tensor(woven_by_runs(da_bf[g][:]), by_runs(da[g][:]), by_runs(factor[g][:]), ALU.mult)
+                nc.vector.tensor_tensor(woven, by_runs(da[e][:]), by_runs(factor_of(e)), ALU.mult)
             else:
-                nc.vector.tensor_copy(out=woven_by_runs(da_bf[g][:]), in_=by_runs(da[g][:]))
+                nc.vector.tensor_copy(out=woven, in_=by_runs(da[e][:]))
 
         def quantize_da(g):
             first, width = groups[g]
@@ -181,30 +185,32 @@ def tile_moe_sdb_relu_kernel(
                 stop=True,
             )
 
-        dx = {}
+        pairs = [(0, 3), (1, 2)]
+        dx_pairs = [
+            keep.tile([P, 2, S], F32, name="dx0", tag="hold_dx0"),
+            turns.tile([P, 2, S], F32, name="dx1", offset=16 * 1024, align_bytes=64),
+        ]
+        dx = {w: dx_pairs[i][:, u, :] for i, pair in enumerate(pairs) for u, w in enumerate(pair)}
+        for w in range(PACK, 2 * PACK):
+            dx.setdefault(w, keep.tile([P, S], F32, name=f"dx{w}", tag=f"hold_dx{w}")[:])
 
-        def dx_one_expert(e, w, engine):
-            acc = next_bank()
-            for u in range(2):
-                second_product(acc[:, u * C : (u + 1) * C], w + u, e)
-            both = keep.tile([P, BANK], F32, name=f"dx_e{e}w{w}")
-            copy(engine, both[:], acc[:])
-            for u in range(2):
-                dx[w + u, e * C] = both[:, u * C : (u + 1) * C]
+        def dx_one_expert(e, i, engine):
+            acc = bank(2 * e + i)
+            for u, w in enumerate(pairs[i]):
+                second_product(acc[:, u * C : (u + 1) * C], w, e)
+            copy(engine, dx_pairs[i][:, :, e * C : (e + 1) * C], acc[:].rearrange("p (u j) -> p u j", u=2))
 
-        def dx_two_experts(w, h, engine):
-            acc = next_bank()
+        def dx_two_experts(w, h, engine, b):
+            acc = bank(b)
             for u in range(2):
                 second_product(acc[:, u * C : (u + 1) * C], w, 2 * h + u)
-            base = 0 if w >= PACK else HALF
-            if (w, base) not in dx:
-                dx[w, base] = keep.tile([P, S - base], F32, name=f"dx_w{w}")[:]
-            copy(engine, dx[w, base][:, h * HALF - base : (h + 1) * HALF - base], acc[:])
+            copy(engine, dx[w][:, h * HALF : (h + 1) * HALF], acc[:])
 
-        windows = [keep.tile([P, T], F32, name=f"window{w}") for w in range(2 * PACK)]
+        windows = {w: keep.tile([P, T], F32, name=f"window{w}") for w in range(2 * PACK) if w not in (3, 5, 6, 7)}
+        windows.setdefault(6, turns.tile([P, T], F32, name="window6", offset=17 * 1024, align_bytes=64))
 
-        def scatter(w, base, first, width, engine):
-            source = dx[w, base][:, first - base : first - base + width]
+        def scatter(w, first, width, engine):
+            source = dx[w][:, first : first + width]
             placed = windows[w][:].indirect(slots(first, width))
             if engine == "vector":
                 nc.vector.tensor_copy(placed, source)
@@ -215,9 +221,11 @@ def tile_moe_sdb_relu_kernel(
 
         quad = turns.tile([P, PACK, T], F32, name="quad", offset=0, align_bytes=64)
 
+        trio = keep.tile([P, PACK - 1, T], F32, name="trio")
+
         def store_window(w):
             rows = out_0[w * P : (w + 1) * P] if w < PACK else dealt_rows[w - PACK]
-            nc.sync.dma_start(out=rows, in_=windows[w][:])
+            nc.sync.dma_start(out=rows, in_=trio[:, 2, :] if w == 6 else windows[w][:])
             if w < PACK:
                 for d in range(PACK):
                     nc.sync.dma_start(out=quad[32 * w : 32 * w + 32, d, :], in_=windows[w][d:P:PACK, :])
@@ -251,21 +259,23 @@ def tile_moe_sdb_relu_kernel(
         round_da(0, False)
         quantize_da(0)
         make_factor(1)
-        for t in range(PACK):
-            gather(1, t, "scalar")
+        for e in (1, 2):
+            for t in range(PACK):
+                gather(e, t, "scalar")
         round_da(1, True)
         make_factor(2)
         quantize_da(1)
         for e in range(2):
-            for w in (0, 2):
-                dx_one_expert(e, w, "scalar")
-            for w in range(PACK):
-                scatter(w, e * C, e * C, C, "scalar")
+            for i in range(2):
+                dx_one_expert(e, i, "scalar")
+            for w in range(PACK - 1):
+                scatter(w, e * C, C, "scalar")
+        round_da(2, True)
         for t in range(PACK):
-            gather(2, t, "vector")
-        round_da(2, False)
+            gather(3, t, "vector")
+        round_da(3, False)
         w1_codes = keep.tile([P, E, 2 * PASS], U8, name="w1_codes", tag="hold_factor", align_bytes=64)
-        w1_s = keep.tile([P, E, PASS], U8, name="w1_s", tag="hold_da2", align_bytes=64)
+        w1_s = keep.tile([P, E, PASS], U8, name="w1_s", tag="hold_da3", align_bytes=64)
         for i in range(2):
             nc.vector.tensor_copy(
                 out=w1_codes[:, 2 * i : 2 * i + 2, :].bitcast(U16).rearrange("p e (d m) -> p e d m", d=PACK),
@@ -277,62 +287,57 @@ def tile_moe_sdb_relu_kernel(
             in_=w1_raw_s[:, :, PASS:K].rearrange("p e (m d) -> p e d m", d=PACK),
         )
 
-        for w in (3, 2):
-            dx_two_experts(w, 1, "vector")
-        dx_two_experts(0, 1, "scalar")
-        scatter(0, HALF, HALF, C, "scalar")
-        dx_two_experts(1, 1, "scalar")
-        scatter(0, HALF, HALF + C, C, "scalar")
-        store_window(0)
-        for w in (3, 2):
-            scatter(w, HALF, HALF, HALF, "vector")
+        windows.setdefault(3, keep.tile([P, T], F32, name="window3", tag="da_bf2", align_bytes=64))
+        dx_two_experts(3, 1, "vector", 4)
+        for w in range(PACK - 1):
+            dx_two_experts(w, 1, "scalar", w)
+        for h in range(2):
+            scatter(3, h * HALF, HALF, "vector")
+        store_window(3)
+        for w in range(PACK - 1):
+            for e in (2, 3):
+                scatter(w, e * C, C, "scalar")
             store_window(w)
-        dx_two_experts(5, 0, "vector")
-        scatter(1, HALF, HALF, C, "scalar")
-        dx_two_experts(5, 1, "scalar")
-        scatter(1, HALF, HALF + C, C, "scalar")
-        store_window(1)
 
         thirds = [(0, 384), (384, 384), (768, 256)]
-        pair = keep.tile([P, 2, T], F32, name="pair")
-        for h in range(2):
-            dx_two_experts(4, h, "scalar")
-        for h in range(2):
-            scatter(5, 0, h * HALF, HALF, "vector")
-        store_window(5)
-        nc.sync.dma_start(out=pair[:, 1, :], in_=windows[5][:])
-        for h in range(2):
-            scatter(4, 0, thirds[h][0], thirds[h][1], "scalar")
-            dx_two_experts(7, h, "scalar")
-        scatter(4, 0, thirds[2][0], thirds[2][1], "scalar")
-        store_window(4)
-        nc.sync.dma_start(out=pair[:, 0, :], in_=windows[4][:])
-        for h in range(2):
-            dx_two_experts(6, h, "scalar")
-        for h in range(2):
-            scatter(7, 0, h * HALF, HALF, "vector")
-        store_window(7)
-        for first, width in thirds:
-            scatter(6, 0, first, width, "scalar")
-        store_window(6)
 
-        y0 = [keep.tile([P, HALF, PACK], BF16, name=f"y0{h}", align_bytes=64) for h in range(2)]
+        def whole_window(w, engine, first_bank, pieces):
+            for h in range(2):
+                dx_two_experts(w, h, engine, first_bank + h)
+            for first, width in pieces:
+                scatter(w, first, width, engine)
+            nc.sync.dma_start(out=trio[:, w - PACK, :], in_=windows[w][:])
+            store_window(w)
+
+        windows.setdefault(5, keep.tile([P, T], F32, name="window5", tag="hold_dx0"))
+        whole_window(5, "vector", 6, [(0, HALF), (HALF, HALF)])
+        whole_window(4, "scalar", 3, thirds)
+        whole_window(6, "vector", 5, [(0, HALF), (HALF, HALF)])
+        windows.setdefault(7, keep.tile([P, T], F32, name="window7", tag="hold_dx4"))
         for h in range(2):
-            nc.vector.tensor_copy(out=woven_by_runs(y0[h][:]), in_=by_runs(quad[:, :, h * HALF : (h + 1) * HALF]))
+            dx_two_experts(7, h, "scalar", h)
+        for first, width in thirds:
+            scatter(7, first, width, "scalar")
+        store_window(7)
+
+        halves = [slice(0, HALF), slice(HALF, T)]
+        y0 = [turns.tile([P, HALF, PACK], BF16, name=f"y0{h}", offset=(21 + 4 * h) * 1024, align_bytes=64) for h in range(2)]
+        for h in range(2):
+            nc.vector.tensor_copy(out=woven_by_runs(y0[h][:]), in_=by_runs(quad[:, :, halves[h]]))
         for h in range(2):
             quantize_y(0, y0[h], h * HALF, (h + 1) * HALF)
         store_planes(0)
 
-        cuts = [0, T // 2, 3 * T // 4, T]
-        spans = list(zip(cuts, cuts[1:]))
+        spans = [(0, T // 2), (T // 2, 3 * T // 4), (3 * T // 4, T)]
         y1 = [
-            turns.tile([P, hi - lo, PACK], BF16, name=f"y1{lo}", offset=2 * PACK * lo, align_bytes=64) for lo, hi in spans
+            turns.tile([P, hi - lo, PACK], BF16, name=f"y1{lo}", offset=14 * 1024 + 2 * PACK * lo, align_bytes=64)
+            for lo, hi in spans
         ]
-        for woven, (lo, hi) in zip(y1, spans):
-            nc.vector.tensor_copy(out=woven[:, :, 0:2], in_=pair[:, :, lo:hi].rearrange("p d t -> p t d"))
-        for d in (3, 2):
-            for c, (lo, hi) in enumerate(spans):
-                copy("vector" if c < 2 else "scalar", y1[c][:, :, d], windows[PACK + d][:, lo:hi])
+        for woven, (lo, hi), rows in zip(y1, spans, (3, 3, 2)):
+            nc.vector.tensor_copy(out=woven_by_runs(woven[:, :, 0:rows]), in_=by_runs(trio[:, 0:rows, lo:hi]))
+        for woven, (lo, hi), engine in zip(y1, spans, ("vector", "vector", "scalar")):
+            copy(engine, woven[:, :, 3], windows[7][:, lo:hi])
+        nc.scalar.copy(out=y1[2][:, :, 2], in_=trio[:, 2, spans[2][0] : T])
         for woven, (lo, hi) in zip(y1, spans):
             quantize_y(1, woven, lo, hi)
         store_planes(1)

@@ -23,7 +23,9 @@ QUADRANTS = 4
 S = E * C
 HALF = S // 2
 PASS = P * PACK
-RUN = 4
+RUN = 2
+WIDE = 1376
+KIB = 1024
 
 
 def load_scale_rows(nc, plane, rows):
@@ -188,11 +190,15 @@ def tile_moe_sdb_relu_kernel(
         pairs = [(0, 3), (1, 2)]
         dx_pairs = [
             keep.tile([P, 2, S], F32, name="dx0", tag="hold_dx0"),
-            turns.tile([P, 2, S], F32, name="dx1", offset=16 * 1024, align_bytes=64),
+            turns.tile([P, 2, S], F32, name="dx1", offset=21 * KIB, align_bytes=64),
         ]
         dx = {w: dx_pairs[i][:, u, :] for i, pair in enumerate(pairs) for u, w in enumerate(pair)}
-        for w in range(PACK, 2 * PACK):
-            dx.setdefault(w, keep.tile([P, S], F32, name=f"dx{w}", tag=f"hold_dx{w}")[:])
+        for w in (5, 6):
+            dx.setdefault(w, keep.tile([P, S], F32, name=f"dx{w}")[:])
+        dx.setdefault(4, turns.tile([P, S], F32, name="dx4", offset=32 * KIB, align_bytes=64)[:])
+        dx.setdefault(7, turns.tile([P, S], F32, name="dx7", offset=55 * KIB // 2, align_bytes=64)[:])
+
+        last_bank = []
 
         def dx_one_expert(e, i, engine):
             acc = bank(2 * e + i)
@@ -204,10 +210,19 @@ def tile_moe_sdb_relu_kernel(
             acc = bank(b)
             for u in range(2):
                 second_product(acc[:, u * C : (u + 1) * C], w, 2 * h + u)
-            copy(engine, dx[w][:, h * HALF : (h + 1) * HALF], acc[:])
+            if (w, h) == (7, 1):
+                copy(engine, dx[w][:, HALF : HALF + C], acc[:, 0:C])
+                last_bank.append(acc)
+            else:
+                copy(engine, dx[w][:, h * HALF : (h + 1) * HALF], acc[:])
 
-        windows = {w: keep.tile([P, T], F32, name=f"window{w}") for w in range(2 * PACK) if w not in (3, 5, 6, 7)}
-        windows.setdefault(6, turns.tile([P, T], F32, name="window6", offset=17 * 1024, align_bytes=64))
+        windows = {w: keep.tile([P, T], F32, name=f"window{w}") for w in range(2)}
+        windows.setdefault(2, turns.tile([P, T], F32, name="window2", offset=38 * KIB, align_bytes=64))
+        windows.setdefault(3, keep.tile([P, WIDE], F32, name="window3"))
+        windows.setdefault(4, turns.tile([P, T], F32, name="window4", offset=47 * KIB // 2, align_bytes=64))
+        windows.setdefault(5, keep.tile([P, WIDE], F32, name="window5", tag="hold_dx0"))
+        windows.setdefault(6, turns.tile([P, WIDE], F32, name="window6", offset=18 * KIB, align_bytes=64))
+        windows.setdefault(7, turns.tile([P, T], F32, name="window7", offset=35 * KIB, align_bytes=64))
 
         def scatter(w, first, width, engine):
             source = dx[w][:, first : first + width]
@@ -221,14 +236,11 @@ def tile_moe_sdb_relu_kernel(
 
         quad = turns.tile([P, PACK, T], F32, name="quad", offset=0, align_bytes=64)
 
-        trio = keep.tile([P, PACK - 1, T], F32, name="trio")
+        trio = turns.tile([P, PACK - 1, T], F32, name="trio", offset=41 * KIB, align_bytes=64)
 
         def store_window(w):
             rows = out_0[w * P : (w + 1) * P] if w < PACK else dealt_rows[w - PACK]
-            nc.sync.dma_start(out=rows, in_=trio[:, 2, :] if w == 6 else windows[w][:])
-            if w < PACK:
-                for d in range(PACK):
-                    nc.sync.dma_start(out=quad[32 * w : 32 * w + 32, d, :], in_=windows[w][d:P:PACK, :])
+            nc.sync.dma_start(out=rows, in_=windows[w][:, 0:T])
 
         y_codes = [keep.tile([P, T], I32, name=f"y_codes{s}", align_bytes=64) for s in range(2)]
         y_s = [keep.tile([P, T], U8, name=f"y_s{s}", align_bytes=64) for s in range(2)]
@@ -241,9 +253,11 @@ def tile_moe_sdb_relu_kernel(
             )
 
         def store_planes(s):
-            nc.sync.dma_start(out=out_1[s].rearrange("p t d -> p (t d)").bitcast(I32), in_=y_codes[s][:])
+            (nc.sync if s else nc.scalar).dma_start(
+                out=out_1[s].rearrange("p t d -> p (t d)").bitcast(I32), in_=y_codes[s][:]
+            )
             for q in range(QUADRANTS):
-                queue = nc.scalar if s == 1 and q % 2 else nc.sync
+                queue = nc.scalar if s == 0 or q % 2 else nc.sync
                 queue.dma_start(
                     out=out_2[s, 4 * q : 4 * q + 4, :].bitcast(I32), in_=y_s[s][32 * q : 32 * q + 4, :].bitcast(I32)
                 )
@@ -273,55 +287,66 @@ def tile_moe_sdb_relu_kernel(
         round_da(2, True)
         for t in range(PACK):
             gather(3, t, "vector")
-        round_da(3, False)
         w1_codes = keep.tile([P, E, 2 * PASS], U8, name="w1_codes", tag="hold_factor", align_bytes=64)
-        w1_s = keep.tile([P, E, PASS], U8, name="w1_s", tag="hold_da3", align_bytes=64)
         for i in range(2):
             nc.vector.tensor_copy(
                 out=w1_codes[:, 2 * i : 2 * i + 2, :].bitcast(U16).rearrange("p e (d m) -> p e d m", d=PACK),
                 in_=w1_raw[i][:, :, 2 * PASS : 2 * K].bitcast(U16).rearrange("p e (m d) -> p e d m", d=PACK),
             )
-        quantize_da(2)
+        round_da(3, False)
+        w1_s = keep.tile([P, E, PASS], U8, name="w1_s", tag="hold_da3", align_bytes=64)
         nc.vector.tensor_copy(
             out=w1_s[:].rearrange("p e (d m) -> p e d m", d=PACK),
             in_=w1_raw_s[:, :, PASS:K].rearrange("p e (m d) -> p e d m", d=PACK),
         )
+        quantize_da(2)
 
-        windows.setdefault(3, keep.tile([P, T], F32, name="window3", tag="da_bf2", align_bytes=64))
-        dx_two_experts(3, 1, "vector", 4)
-        for w in range(PACK - 1):
-            dx_two_experts(w, 1, "scalar", w)
-        for h in range(2):
-            scatter(3, h * HALF, HALF, "vector")
-        store_window(3)
-        for w in range(PACK - 1):
-            for e in (2, 3):
-                scatter(w, e * C, C, "scalar")
-            store_window(w)
+        def hand_on(w):
+            nc.sync.dma_start(out=trio[:, w - PACK, :], in_=windows[w][:, 0:T])
 
         thirds = [(0, 384), (384, 384), (768, 256)]
-
-        def whole_window(w, engine, first_bank, pieces):
-            for h in range(2):
-                dx_two_experts(w, h, engine, first_bank + h)
-            for first, width in pieces:
-                scatter(w, first, width, engine)
-            nc.sync.dma_start(out=trio[:, w - PACK, :], in_=windows[w][:])
+        dx_two_experts(5, 0, "vector", 6)
+        dx_two_experts(6, 0, "vector", 7)
+        dx_two_experts(3, 1, "vector", 4)
+        dx_two_experts(0, 1, "scalar", 0)
+        dx_two_experts(1, 1, "scalar", 1)
+        scatter(3, 0, S, "vector")
+        store_window(3)
+        scatter(0, 2 * C, C, "scalar")
+        dx_two_experts(2, 1, "scalar", 2)
+        scatter(0, 3 * C, C, "scalar")
+        store_window(0)
+        dx_two_experts(5, 1, "vector", 5)
+        dx_two_experts(6, 1, "vector", 6)
+        for w in (1, 2):
+            scatter(w, 2 * C, C, "scalar")
+            dx_two_experts(4, w - 1, "scalar", 3 * (2 - w))
+            scatter(w, 3 * C, C, "scalar")
             store_window(w)
-
-        windows.setdefault(5, keep.tile([P, T], F32, name="window5", tag="hold_dx0"))
-        whole_window(5, "vector", 6, [(0, HALF), (HALF, HALF)])
-        whole_window(4, "scalar", 3, thirds)
-        whole_window(6, "vector", 5, [(0, HALF), (HALF, HALF)])
-        windows.setdefault(7, keep.tile([P, T], F32, name="window7", tag="hold_dx4"))
+        back = out_0[0:PASS].rearrange("(p d) t -> p d t", d=PACK)
+        for cols in (slice(0, HALF), slice(HALF, T)):
+            nc.sync.dma_start(out=quad[:, :, cols], in_=back[:, :, cols])
+        scatter(5, 0, S, "vector")
+        store_window(5)
+        hand_on(5)
         for h in range(2):
-            dx_two_experts(7, h, "scalar", h)
-        for first, width in thirds:
+            scatter(4, thirds[h][0], thirds[h][1], "scalar")
+            dx_two_experts(7, h, "scalar", 1 + h)
+        scatter(4, thirds[2][0], thirds[2][1], "scalar")
+        hand_on(4)
+        scatter(6, 0, S, "vector")
+        hand_on(6)
+        even_rows = out_0[PASS:K].rearrange("(p u v) t -> v p u t", u=2, v=2)[0]
+        nc.sync.dma_start(out=even_rows, in_=trio[:, 0 : PACK - 1 : 2, :])
+        for first, width in thirds[0:2]:
             scatter(7, first, width, "scalar")
+        dx_last = turns.tile([P, C], F32, name="dx_last", offset=23 * KIB, align_bytes=64)
+        nc.scalar.copy(out=dx_last[:], in_=last_bank[0][:, C:BANK])
+        nc.scalar.activation(windows[7][:].indirect(slots(S - C, C)), dx_last[:], COPY)
         store_window(7)
 
         halves = [slice(0, HALF), slice(HALF, T)]
-        y0 = [turns.tile([P, HALF, PACK], BF16, name=f"y0{h}", offset=(21 + 4 * h) * 1024, align_bytes=64) for h in range(2)]
+        y0 = [keep.tile([P, HALF, PACK], BF16, name=f"y0{h}", align_bytes=64) for h in range(2)]
         for h in range(2):
             nc.vector.tensor_copy(out=woven_by_runs(y0[h][:]), in_=by_runs(quad[:, :, halves[h]]))
         for h in range(2):
@@ -330,14 +355,14 @@ def tile_moe_sdb_relu_kernel(
 
         spans = [(0, T // 2), (T // 2, 3 * T // 4), (3 * T // 4, T)]
         y1 = [
-            turns.tile([P, hi - lo, PACK], BF16, name=f"y1{lo}", offset=14 * 1024 + 2 * PACK * lo, align_bytes=64)
+            turns.tile([P, hi - lo, PACK], BF16, name=f"y1{lo}", offset=15 * KIB + 2 * PACK * lo, align_bytes=64)
             for lo, hi in spans
         ]
-        for woven, (lo, hi), rows in zip(y1, spans, (3, 3, 2)):
-            nc.vector.tensor_copy(out=woven_by_runs(woven[:, :, 0:rows]), in_=by_runs(trio[:, 0:rows, lo:hi]))
-        for woven, (lo, hi), engine in zip(y1, spans, ("vector", "vector", "scalar")):
-            copy(engine, woven[:, :, 3], windows[7][:, lo:hi])
-        nc.scalar.copy(out=y1[2][:, :, 2], in_=trio[:, 2, spans[2][0] : T])
+        engines = ("vector", "vector", "scalar")
+        for woven, (lo, hi), engine in zip(y1, spans, engines):
+            copy(engine, woven_by_runs(woven[:, :, 0 : PACK - 1]), by_runs(trio[:, :, lo:hi]))
+        for woven, (lo, hi), engine in zip(y1, spans, engines):
+            copy(engine, woven[:, :, PACK - 1], windows[7][:, lo:hi])
         for woven, (lo, hi) in zip(y1, spans):
             quantize_y(1, woven, lo, hi)
         store_planes(1)

@@ -216,8 +216,8 @@ def tile_moe_sdb_relu_kernel(
             else:
                 copy(engine, dx[w][:, h * HALF : (h + 1) * HALF], acc[:])
 
-        windows = {w: keep.tile([P, T], F32, name=f"window{w}") for w in range(2)}
-        windows.setdefault(2, turns.tile([P, T], F32, name="window2", offset=38 * KIB, align_bytes=64))
+        windows = {w: keep.tile([P, T], F32, name=f"window{w}") for w in (0, 2)}
+        windows.setdefault(1, turns.tile([P, T], F32, name="window1", offset=38 * KIB, align_bytes=64))
         windows.setdefault(3, keep.tile([P, WIDE], F32, name="window3"))
         windows.setdefault(4, turns.tile([P, T], F32, name="window4", offset=47 * KIB // 2, align_bytes=64))
         windows.setdefault(5, keep.tile([P, WIDE], F32, name="window5", tag="hold_dx0"))
@@ -306,41 +306,40 @@ def tile_moe_sdb_relu_kernel(
 
         thirds = [(0, 384), (384, 384), (768, 256)]
         dx_two_experts(5, 0, "vector", 6)
-        dx_two_experts(6, 0, "vector", 7)
         dx_two_experts(3, 1, "vector", 4)
+        dx_two_experts(6, 0, "vector", 6)
+        dx_two_experts(2, 1, "scalar", 2)
         dx_two_experts(0, 1, "scalar", 0)
+        scatter(2, 2 * C, C, "scalar")
         dx_two_experts(1, 1, "scalar", 1)
         scatter(3, 0, S, "vector")
         store_window(3)
-        scatter(0, 2 * C, C, "scalar")
-        dx_two_experts(2, 1, "scalar", 2)
-        scatter(0, 3 * C, C, "scalar")
-        store_window(0)
+        scatter(2, 3 * C, C, "vector")
+        store_window(2)
         dx_two_experts(5, 1, "vector", 5)
-        dx_two_experts(6, 1, "vector", 6)
-        for w in (1, 2):
+        dx_two_experts(6, 1, "vector", 7)
+        for w in (0, 1):
             scatter(w, 2 * C, C, "scalar")
-            dx_two_experts(4, w - 1, "scalar", 3 * (2 - w))
+            dx_two_experts(4, w, "scalar", 4 - 2 * w)
             scatter(w, 3 * C, C, "scalar")
             store_window(w)
         back = out_0[0:PASS].rearrange("(p d) t -> p d t", d=PACK)
         for cols in (slice(0, HALF), slice(HALF, T)):
             nc.sync.dma_start(out=quad[:, :, cols], in_=back[:, :, cols])
         scatter(5, 0, S, "vector")
-        store_window(5)
         hand_on(5)
         for h in range(2):
             scatter(4, thirds[h][0], thirds[h][1], "scalar")
-            dx_two_experts(7, h, "scalar", 1 + h)
+            dx_two_experts(7, h, "scalar", h)
         scatter(4, thirds[2][0], thirds[2][1], "scalar")
         hand_on(4)
         scatter(6, 0, S, "vector")
         hand_on(6)
-        even_rows = out_0[PASS:K].rearrange("(p u v) t -> v p u t", u=2, v=2)[0]
-        nc.sync.dma_start(out=even_rows, in_=trio[:, 0 : PACK - 1 : 2, :])
+        for d in (1, 0, 2):
+            nc.sync.dma_start(out=dealt_rows[d], in_=trio[:, d, :])
         for first, width in thirds[0:2]:
             scatter(7, first, width, "scalar")
-        dx_last = turns.tile([P, C], F32, name="dx_last", offset=23 * KIB, align_bytes=64)
+        dx_last = turns.tile([P, C], F32, name="dx_last", offset=24 * KIB, align_bytes=64)
         nc.scalar.copy(out=dx_last[:], in_=last_bank[0][:, C:BANK])
         nc.scalar.activation(windows[7][:].indirect(slots(S - C, C)), dx_last[:], COPY)
         store_window(7)

@@ -60,13 +60,15 @@ def tile_moe_sdb_relu_kernel(
         w2_s = keep.tile([P, H], U8, name="w2_s", align_bytes=64)
         dy_codes = keep.tile([P, T], I32, name="dy_codes", align_bytes=64)
         dy_s = keep.tile([P, T], U8, name="dy_s", align_bytes=64)
-        w1_raw_s = keep.tile([P, E, K], U8, name="w1_raw_s", align_bytes=64)
+        w1_raw_s = keep.tile([P, E, PASS], U8, name="w1_raw_s", align_bytes=64)
+        packed_raw = keep.tile([P, PASS], U8, name="packed_raw", align_bytes=64)
         w1_raw = [keep.tile([P, 2, 2 * K], U8, name=f"w1_raw{i}", align_bytes=64) for i in range(2)]
-        a_sb = [keep.tile([P, PACK, width], F32, name=f"a{g}") for g, (first, width) in enumerate(groups)]
-        gate_sb = [keep.tile([P, HALF], F32, name=f"gate{i}") for i in range(2)]
+        a_first = [keep.tile([P, 2, C], F32, name=f"a_first{u}") for u in range(2)]
+        a_sb = {g: keep.tile([P, PACK, groups[g][1]], F32, name=f"a{g}") for g in (1, 2)}
+        gate_sb = [keep.tile([P, width], F32, name=f"gate{g}") for g, (first, width) in enumerate(groups)]
 
         nc.gpsimd.memset(w2_raw_s[:].bitcast(I32), 0)
-        nc.gpsimd.memset(w1_raw_s[:].bitcast(I32), 0)
+        nc.gpsimd.memset(packed_raw[:].bitcast(I32), 0)
 
         a_rows = a.rearrange("(p t) j -> p t j", t=PACK)
         w1_rows = w1t_words.rearrange("e s p c -> (s p) e c")
@@ -74,13 +76,20 @@ def tile_moe_sdb_relu_kernel(
         nc.sync.dma_start(out=w2_raw[:], in_=w2t_words[0].rearrange("p i d -> p (i d)").bitcast(I32))
         nc.sync.dma_start(out=dy_codes[:], in_=dy_words[0].rearrange("p t d -> p (t d)").bitcast(I32))
         load_scale_rows(nc, w2_raw_s, w2t_scales[0])
-        nc.sync.dma_start(out=gate_sb[0][:], in_=gate[:, 0:HALF])
-        nc.sync.dma_start(out=a_sb[0][:], in_=a_rows[:, :, 0:C])
+        nc.sync.dma_start(out=gate_sb[0][:], in_=gate[:, 0:C])
+        nc.sync.dma_start(out=a_first[0][:], in_=a_rows[:, 0:2, 0:C])
         nc.sync.dma_start(offsets[:], offs)
+        nc.sync.dma_start(out=a_first[1][:], in_=a_rows[:, 2:4, 0:C])
+        nc.sync.dma_start(out=gate_sb[1][:], in_=gate[:, C:HALF])
         nc.sync.dma_start(out=a_sb[1][:], in_=a_rows[:, :, C:HALF])
-        load_scale_rows(nc, w1_raw_s, w1t_scales.rearrange("e s b k -> (s b) e k"))
+        load_scale_rows(nc, w1_raw_s, w1t_scales.rearrange("e s b k -> (s b) e k")[:, :, 0:PASS])
         nc.sync.dma_start(out=w1_raw[0][:].bitcast(I32), in_=w1_rows[:, 0:2, :].bitcast(I32))
-        nc.sync.dma_start(out=gate_sb[1][:], in_=gate[:, HALF:S])
+        for q in range(QUADRANTS):
+            nc.sync.dma_start(
+                out=packed_raw[32 * q : 32 * q + 4 * E].bitcast(I32),
+                in_=w1t_scales[:, 0, 4 * q : 4 * q + 4, PASS:K].bitcast(I32),
+            )
+        nc.sync.dma_start(out=gate_sb[2][:], in_=gate[:, HALF:S])
         nc.sync.dma_start(out=a_sb[2][:], in_=a_rows[:, :, HALF:S])
         nc.sync.dma_start(out=w1_raw[1][:].bitcast(I32), in_=w1_rows[:, 2:4, :].bitcast(I32))
 
@@ -97,15 +106,16 @@ def tile_moe_sdb_relu_kernel(
             first, width = groups[g]
             tag = "hold_factor" if g == 2 else f"factor{g}"
             factor[g] = keep.tile([P, PACK, width], F32, name=f"factor{g}", tag=tag, align_bytes=64)
-            gates = gate_sb[first // HALF][:, first % HALF : first % HALF + width]
-            nc.vector.scalar_tensor_tensor(
-                out=factor[g][:],
-                in0=a_sb[g][:],
-                scalar=0.0,
-                in1=gates.unsqueeze(1).to_broadcast([P, PACK, width]),
-                op0=ALU.is_gt,
-                op1=ALU.mult,
-            )
+            parts = [(a_first[0], 0, 2), (a_first[1], 2, 2)] if g == 0 else [(a_sb[g], 0, PACK)]
+            for rows, t, count in parts:
+                nc.vector.scalar_tensor_tensor(
+                    out=factor[g][:, t : t + count, :],
+                    in0=rows[:],
+                    scalar=0.0,
+                    in1=gate_sb[g][:].unsqueeze(1).to_broadcast([P, count, width]),
+                    op0=ALU.is_gt,
+                    op1=ALU.mult,
+                )
 
         def slots(first, width):
             return offsets[:, first // LANES : (first + width) // LANES]
@@ -175,8 +185,8 @@ def tile_moe_sdb_relu_kernel(
                 codes = w1_raw[e // 2][:, e % 2, 2 * j * P : 2 * (j + 1) * P]
                 scales = w1_raw_s[:, e, j * P : (j + 1) * P]
             else:
-                codes = w1_codes[:, e, 2 * j * P : 2 * (j + 1) * P]
-                scales = w1_s[:, e, j * P : (j + 1) * P]
+                codes = (w1_late if e < 2 else w1_codes)[:, e % 2, 2 * j * P : 2 * (j + 1) * P]
+                scales = (packed[:] if e == 0 else w1_s[:, e - 1, :])[:, j * P : (j + 1) * P]
             nc.tensor.matmul_mx(
                 out=out,
                 lhsT=codes.bitcast(FP4X4),
@@ -189,7 +199,7 @@ def tile_moe_sdb_relu_kernel(
 
         pairs = [(0, 3), (1, 2)]
         dx_pairs = [
-            keep.tile([P, 2, S], F32, name="dx0", tag="hold_dx0"),
+            keep.tile([P, 2, S], F32, name="dx0"),
             turns.tile([P, 2, S], F32, name="dx1", offset=21 * KIB, align_bytes=64),
         ]
         dx = {w: dx_pairs[i][:, u, :] for i, pair in enumerate(pairs) for u, w in enumerate(pair)}
@@ -220,7 +230,7 @@ def tile_moe_sdb_relu_kernel(
         windows.setdefault(1, turns.tile([P, T], F32, name="window1", offset=38 * KIB, align_bytes=64))
         windows.setdefault(3, keep.tile([P, WIDE], F32, name="window3"))
         windows.setdefault(4, turns.tile([P, T], F32, name="window4", offset=47 * KIB // 2, align_bytes=64))
-        windows.setdefault(5, keep.tile([P, WIDE], F32, name="window5", tag="hold_dx0"))
+        windows.setdefault(5, keep.tile([P, WIDE], F32, name="window5"))
         windows.setdefault(6, turns.tile([P, WIDE], F32, name="window6", offset=18 * KIB, align_bytes=64))
         windows.setdefault(7, turns.tile([P, T], F32, name="window7", offset=35 * KIB, align_bytes=64))
 
@@ -272,6 +282,17 @@ def tile_moe_sdb_relu_kernel(
         gather(0, 3, "vector")
         round_da(0, False)
         quantize_da(0)
+        packed = keep.tile([P, PASS], U8, name="packed", tag="hold_da0", align_bytes=64)
+        w1_s = keep.tile([P, E - 1, PASS], U8, name="w1_s", align_bytes=64)
+        nc.vector.tensor_copy(
+            out=packed[:].rearrange("p (d m) -> p d m", d=PACK), in_=packed_raw[:].rearrange("p (m d) -> p d m", d=PACK)
+        )
+        for e in range(1, E):
+            for q in range(QUADRANTS):
+                nc.sync.dma_start(
+                    out=w1_s[32 * q : 32 * q + 4, e - 1, :].bitcast(I32),
+                    in_=packed[32 * q + 4 * e : 32 * q + 4 * e + 4].bitcast(I32),
+                )
         make_factor(1)
         for e in (1, 2):
             for t in range(PACK):
@@ -287,18 +308,18 @@ def tile_moe_sdb_relu_kernel(
         round_da(2, True)
         for t in range(PACK):
             gather(3, t, "vector")
-        w1_codes = keep.tile([P, E, 2 * PASS], U8, name="w1_codes", tag="hold_factor", align_bytes=64)
-        for i in range(2):
+        w1_codes = keep.tile([P, 2, 2 * PASS], U8, name="w1_codes", tag="hold_factor", align_bytes=64)
+        w1_late = keep.tile([P, 2, 2 * PASS], U8, name="w1_late", tag="hold_da3", align_bytes=64)
+
+        def deal_words(dealt, raw):
             nc.vector.tensor_copy(
-                out=w1_codes[:, 2 * i : 2 * i + 2, :].bitcast(U16).rearrange("p e (d m) -> p e d m", d=PACK),
-                in_=w1_raw[i][:, :, 2 * PASS : 2 * K].bitcast(U16).rearrange("p e (m d) -> p e d m", d=PACK),
+                out=dealt[:].bitcast(U16).rearrange("p e (d m) -> p e d m", d=PACK),
+                in_=raw[:, :, 2 * PASS : 2 * K].bitcast(U16).rearrange("p e (m d) -> p e d m", d=PACK),
             )
+
+        deal_words(w1_codes, w1_raw[1])
         round_da(3, False)
-        w1_s = keep.tile([P, E, PASS], U8, name="w1_s", tag="hold_da3", align_bytes=64)
-        nc.vector.tensor_copy(
-            out=w1_s[:].rearrange("p e (d m) -> p e d m", d=PACK),
-            in_=w1_raw_s[:, :, PASS:K].rearrange("p e (m d) -> p e d m", d=PACK),
-        )
+        deal_words(w1_late, w1_raw[0])
         quantize_da(2)
 
         def hand_on(w):
@@ -307,7 +328,6 @@ def tile_moe_sdb_relu_kernel(
         thirds = [(0, 384), (384, 384), (768, 256)]
         dx_two_experts(5, 0, "vector", 6)
         dx_two_experts(3, 1, "vector", 4)
-        dx_two_experts(6, 0, "vector", 6)
         dx_two_experts(2, 1, "scalar", 2)
         dx_two_experts(0, 1, "scalar", 0)
         scatter(2, 2 * C, C, "scalar")
@@ -317,6 +337,7 @@ def tile_moe_sdb_relu_kernel(
         scatter(2, 3 * C, C, "vector")
         store_window(2)
         dx_two_experts(5, 1, "vector", 5)
+        dx_two_experts(6, 0, "vector", 6)
         dx_two_experts(6, 1, "vector", 7)
         for w in (0, 1):
             scatter(w, 2 * C, C, "scalar")

@@ -62,7 +62,8 @@ def tile_moe_sdb_relu_kernel(
         dy_s = keep.tile([P, T], U8, name="dy_s", align_bytes=64)
         w1_raw_s = keep.tile([P, E, PASS], U8, name="w1_raw_s", align_bytes=64)
         packed_raw = keep.tile([P, PASS], U8, name="packed_raw", align_bytes=64)
-        w1_raw = [keep.tile([P, 2, 2 * K], U8, name=f"w1_raw{i}", align_bytes=64) for i in range(2)]
+        w1_first = [keep.tile([P, 2, 2 * PASS], U8, name=f"w1_first{i}", align_bytes=64) for i in range(2)]
+        w1_raw = keep.tile([P, E, 2 * PASS], U8, name="w1_raw", align_bytes=64)
         a_first = [keep.tile([P, 2, C], F32, name=f"a_first{u}") for u in range(2)]
         a_sb = {g: keep.tile([P, PACK, groups[g][1]], F32, name=f"a{g}") for g in (1, 2)}
         gate_sb = [keep.tile([P, width], F32, name=f"gate{g}") for g, (first, width) in enumerate(groups)]
@@ -83,7 +84,7 @@ def tile_moe_sdb_relu_kernel(
         nc.sync.dma_start(out=gate_sb[1][:], in_=gate[:, C:HALF])
         nc.sync.dma_start(out=a_sb[1][:], in_=a_rows[:, :, C:HALF])
         load_scale_rows(nc, w1_raw_s, w1t_scales.rearrange("e s b k -> (s b) e k")[:, :, 0:PASS])
-        nc.sync.dma_start(out=w1_raw[0][:].bitcast(I32), in_=w1_rows[:, 0:2, :].bitcast(I32))
+        nc.sync.dma_start(out=w1_first[0][:].bitcast(I32), in_=w1_rows[:, 0:2, 0 : 2 * PASS].bitcast(I32))
         for q in range(QUADRANTS):
             nc.sync.dma_start(
                 out=packed_raw[32 * q : 32 * q + 4 * E].bitcast(I32),
@@ -91,7 +92,8 @@ def tile_moe_sdb_relu_kernel(
             )
         nc.sync.dma_start(out=gate_sb[2][:], in_=gate[:, HALF:S])
         nc.sync.dma_start(out=a_sb[2][:], in_=a_rows[:, :, HALF:S])
-        nc.sync.dma_start(out=w1_raw[1][:].bitcast(I32), in_=w1_rows[:, 2:4, :].bitcast(I32))
+        nc.sync.dma_start(out=w1_raw[:].bitcast(I32), in_=w1_rows[:, :, 2 * PASS : 2 * K].bitcast(I32))
+        nc.sync.dma_start(out=w1_first[1][:].bitcast(I32), in_=w1_rows[:, 2:4, 0 : 2 * PASS].bitcast(I32))
 
         nc.vector.tensor_copy(
             out=w2_codes[:].rearrange("p (t m) -> p m t", t=PACK), in_=w2_raw[:].rearrange("p (m t) -> p m t", t=PACK)
@@ -182,7 +184,7 @@ def tile_moe_sdb_relu_kernel(
         def second_product(out, w, e):
             s, j = divmod(w, PACK)
             if s == 0:
-                codes = w1_raw[e // 2][:, e % 2, 2 * j * P : 2 * (j + 1) * P]
+                codes = w1_first[e // 2][:, e % 2, 2 * j * P : 2 * (j + 1) * P]
                 scales = w1_raw_s[:, e, j * P : (j + 1) * P]
             else:
                 codes = (w1_late if e < 2 else w1_codes)[:, e % 2, 2 * j * P : 2 * (j + 1) * P]
@@ -275,7 +277,7 @@ def tile_moe_sdb_relu_kernel(
         make_factor(0)
         for t in range(PACK):
             first_product(t, 0, "scalar")
-            first_product(t, 1, "vector" if t < 1 else "scalar")
+            first_product(t, 1, "scalar")
         gather(0, 0, "vector")
         gather(0, 1, "vector")
         gather(0, 2, "vector")
@@ -314,12 +316,12 @@ def tile_moe_sdb_relu_kernel(
         def deal_words(dealt, raw):
             nc.vector.tensor_copy(
                 out=dealt[:].bitcast(U16).rearrange("p e (d m) -> p e d m", d=PACK),
-                in_=raw[:, :, 2 * PASS : 2 * K].bitcast(U16).rearrange("p e (m d) -> p e d m", d=PACK),
+                in_=raw.bitcast(U16).rearrange("p e (m d) -> p e d m", d=PACK),
             )
 
-        deal_words(w1_codes, w1_raw[1])
+        deal_words(w1_codes, w1_raw[:, 2:4, :])
         round_da(3, False)
-        deal_words(w1_late, w1_raw[0])
+        deal_words(w1_late, w1_raw[:, 0:2, :])
         quantize_da(2)
 
         def hand_on(w):

@@ -265,9 +265,9 @@ def tile_moe_sdb_relu_kernel(
             )
 
         def store_planes(s):
-            (nc.sync if s else nc.scalar).dma_start(
-                out=out_1[s].rearrange("p t d -> p (t d)").bitcast(I32), in_=y_codes[s][:]
-            )
+            words = out_1[s].rearrange("p t d -> p (t d)").bitcast(I32)
+            for cols in [slice(0, HALF), slice(HALF, T)] if s else [slice(0, T)]:
+                (nc.sync if s else nc.scalar).dma_start(out=words[:, cols], in_=y_codes[s][:, cols])
             for q in range(QUADRANTS):
                 queue = nc.scalar if s == 0 or q % 2 else nc.sync
                 queue.dma_start(
@@ -358,8 +358,9 @@ def tile_moe_sdb_relu_kernel(
         hand_on(4)
         scatter(6, 0, S, "vector")
         hand_on(6)
-        for d in (1, 0, 2):
-            nc.sync.dma_start(out=dealt_rows[d], in_=trio[:, d, :])
+        dealt_by_partition = out_0[PASS:K].rearrange("(p d) t -> p d t", d=PACK)
+        for planes in (slice(0, 2), slice(2, 3)):
+            nc.sync.dma_start(out=dealt_by_partition[:, planes, :], in_=trio[:, planes, :])
         for first, width in thirds[0:2]:
             scatter(7, first, width, "scalar")
         dx_last = turns.tile([P, C], F32, name="dx_last", offset=24 * KIB, align_bytes=64)

@@ -64,9 +64,9 @@ def tile_moe_sdb_relu_kernel(
         packed_raw = keep.tile([P, PASS], U8, name="packed_raw", align_bytes=64)
         w1_first = [keep.tile([P, 2, 2 * PASS], U8, name=f"w1_first{i}", align_bytes=64) for i in range(2)]
         w1_raw = keep.tile([P, E, 2 * PASS], U8, name="w1_raw", align_bytes=64)
-        a_first = [keep.tile([P, 2, C], F32, name=f"a_first{u}") for u in range(2)]
-        a_sb = {g: keep.tile([P, PACK, groups[g][1]], F32, name=f"a{g}") for g in (1, 2)}
-        gate_sb = [keep.tile([P, width], F32, name=f"gate{g}") for g, (first, width) in enumerate(groups)]
+        a_first = [keep.tile([P, 2, HALF], F32, name=f"a_first{u}") for u in range(2)]
+        a_second = keep.tile([P, PACK, HALF], F32, name="a_second")
+        gate_sb = [keep.tile([P, HALF], F32, name=f"gate{h}") for h in range(2)]
 
         nc.gpsimd.memset(w2_raw_s[:].bitcast(I32), 0)
         nc.gpsimd.memset(packed_raw[:].bitcast(I32), 0)
@@ -77,12 +77,10 @@ def tile_moe_sdb_relu_kernel(
         nc.sync.dma_start(out=w2_raw[:], in_=w2t_words[0].rearrange("p i d -> p (i d)").bitcast(I32))
         nc.sync.dma_start(out=dy_codes[:], in_=dy_words[0].rearrange("p t d -> p (t d)").bitcast(I32))
         load_scale_rows(nc, w2_raw_s, w2t_scales[0])
-        nc.sync.dma_start(out=gate_sb[0][:], in_=gate[:, 0:C])
-        nc.sync.dma_start(out=a_first[0][:], in_=a_rows[:, 0:2, 0:C])
+        nc.sync.dma_start(out=gate_sb[0][:], in_=gate[:, 0:HALF])
+        nc.sync.dma_start(out=a_first[0][:], in_=a_rows[:, 0:2, 0:HALF])
         nc.sync.dma_start(offsets[:], offs)
-        nc.sync.dma_start(out=a_first[1][:], in_=a_rows[:, 2:4, 0:C])
-        nc.sync.dma_start(out=gate_sb[1][:], in_=gate[:, C:HALF])
-        nc.sync.dma_start(out=a_sb[1][:], in_=a_rows[:, :, C:HALF])
+        nc.sync.dma_start(out=a_first[1][:], in_=a_rows[:, 2:4, 0:HALF])
         load_scale_rows(nc, w1_raw_s, w1t_scales.rearrange("e s b k -> (s b) e k")[:, :, 0:PASS])
         nc.sync.dma_start(out=w1_first[0][:].bitcast(I32), in_=w1_rows[:, 0:2, 0 : 2 * PASS].bitcast(I32))
         for q in range(QUADRANTS):
@@ -90,8 +88,8 @@ def tile_moe_sdb_relu_kernel(
                 out=packed_raw[32 * q : 32 * q + 4 * E].bitcast(I32),
                 in_=w1t_scales[:, 0, 4 * q : 4 * q + 4, PASS:K].bitcast(I32),
             )
-        nc.sync.dma_start(out=gate_sb[2][:], in_=gate[:, HALF:S])
-        nc.sync.dma_start(out=a_sb[2][:], in_=a_rows[:, :, HALF:S])
+        nc.sync.dma_start(out=gate_sb[1][:], in_=gate[:, HALF:S])
+        nc.sync.dma_start(out=a_second[:], in_=a_rows[:, :, HALF:S])
         nc.sync.dma_start(out=w1_raw[:].bitcast(I32), in_=w1_rows[:, :, 2 * PASS : 2 * K].bitcast(I32))
         nc.sync.dma_start(out=w1_first[1][:].bitcast(I32), in_=w1_rows[:, 2:4, 0 : 2 * PASS].bitcast(I32))
 
@@ -104,17 +102,15 @@ def tile_moe_sdb_relu_kernel(
 
         factor, da, da_bf, da_codes, da_s = {}, {}, {}, {}, {}
 
-        def make_factor(g):
-            first, width = groups[g]
-            tag = "hold_factor" if g == 2 else f"factor{g}"
-            factor[g] = keep.tile([P, PACK, width], F32, name=f"factor{g}", tag=tag, align_bytes=64)
-            parts = [(a_first[0], 0, 2), (a_first[1], 2, 2)] if g == 0 else [(a_sb[g], 0, PACK)]
+        def make_factor(h):
+            factor[h] = keep.tile([P, PACK, HALF], F32, name=f"factor{h}", tag="hold_factor" if h else "factor0", align_bytes=64)
+            parts = [(a_second, 0, PACK)] if h else [(a_first[0], 0, 2), (a_first[1], 2, 2)]
             for rows, t, count in parts:
                 nc.vector.scalar_tensor_tensor(
-                    out=factor[g][:, t : t + count, :],
+                    out=factor[h][:, t : t + count, :],
                     in0=rows[:],
                     scalar=0.0,
-                    in1=gate_sb[g][:].unsqueeze(1).to_broadcast([P, count, width]),
+                    in1=gate_sb[h][:].unsqueeze(1).to_broadcast([P, count, HALF]),
                     op0=ALU.is_gt,
                     op1=ALU.mult,
                 )
@@ -139,9 +135,7 @@ def tile_moe_sdb_relu_kernel(
             copy(engine, dc[t][:, cols], acc[:])
 
         def factor_of(e):
-            g = min(e, 2)
-            first = e * C - groups[g][0]
-            return factor[g][:, :, first : first + C]
+            return factor[e // 2][:, :, (e % 2) * C : (e % 2 + 1) * C]
 
         def gather(e, t, engine):
             if e not in da:
@@ -295,12 +289,11 @@ def tile_moe_sdb_relu_kernel(
                     out=w1_s[32 * q : 32 * q + 4, e - 1, :].bitcast(I32),
                     in_=packed[32 * q + 4 * e : 32 * q + 4 * e + 4].bitcast(I32),
                 )
-        make_factor(1)
         for e in (1, 2):
             for t in range(PACK):
                 gather(e, t, "scalar")
         round_da(1, True)
-        make_factor(2)
+        make_factor(1)
         quantize_da(1)
         for e in range(2):
             for i in range(2):

@@ -64,23 +64,28 @@ def tile_moe_sdb_relu_kernel(
         packed_raw = keep.tile([P, PASS], U8, name="packed_raw", align_bytes=64)
         w1_first = [keep.tile([P, 2, 2 * PASS], U8, name=f"w1_first{i}", align_bytes=64) for i in range(2)]
         w1_raw = keep.tile([P, E, 2 * PASS], U8, name="w1_raw", align_bytes=64)
-        a_first = [keep.tile([P, 2, HALF], F32, name=f"a_first{u}") for u in range(2)]
+        row_sets = [(0, 1), (1, 1), (2, 2)]
+        a_first = [keep.tile([P, count, HALF], F32, name=f"a_first{t}") for t, count in row_sets]
         a_second = keep.tile([P, PACK, HALF], F32, name="a_second")
         gate_sb = [keep.tile([P, HALF], F32, name=f"gate{h}") for h in range(2)]
 
-        nc.gpsimd.memset(w2_raw_s[:].bitcast(I32), 0)
         nc.gpsimd.memset(packed_raw[:].bitcast(I32), 0)
 
         a_rows = a.rearrange("(p t) j -> p t j", t=PACK)
         w1_rows = w1t_words.rearrange("e s p c -> (s p) e c")
-        load_scale_rows(nc, dy_s, dy_scales[0])
+        for q in range(QUADRANTS):
+            rows = w2t_scales[0, 4 * q : 4 * q + 4].bitcast(I32)
+            nc.sync.dma_start(
+                out=w2_raw_s[32 * q : 32 * q + 32].bitcast(I32), in_=rows.unsqueeze(0).to_broadcast([8, 4, H // 4])
+            )
         nc.sync.dma_start(out=w2_raw[:], in_=w2t_words[0].rearrange("p i d -> p (i d)").bitcast(I32))
         nc.sync.dma_start(out=dy_codes[:], in_=dy_words[0].rearrange("p t d -> p (t d)").bitcast(I32))
-        load_scale_rows(nc, w2_raw_s, w2t_scales[0])
+        load_scale_rows(nc, dy_s, dy_scales[0])
         nc.sync.dma_start(out=gate_sb[0][:], in_=gate[:, 0:HALF])
-        nc.sync.dma_start(out=a_first[0][:], in_=a_rows[:, 0:2, 0:HALF])
+        nc.sync.dma_start(out=a_first[0][:], in_=a_rows[:, 0:1, 0:HALF])
         nc.sync.dma_start(offsets[:], offs)
-        nc.sync.dma_start(out=a_first[1][:], in_=a_rows[:, 2:4, 0:HALF])
+        nc.sync.dma_start(out=a_first[1][:], in_=a_rows[:, 1:2, 0:HALF])
+        nc.sync.dma_start(out=a_first[2][:], in_=a_rows[:, 2:4, 0:HALF])
         load_scale_rows(nc, w1_raw_s, w1t_scales.rearrange("e s b k -> (s b) e k")[:, :, 0:PASS])
         nc.sync.dma_start(out=w1_first[0][:].bitcast(I32), in_=w1_rows[:, 0:2, 0 : 2 * PASS].bitcast(I32))
         for q in range(QUADRANTS):
@@ -104,7 +109,7 @@ def tile_moe_sdb_relu_kernel(
 
         def make_factor(h):
             factor[h] = keep.tile([P, PACK, HALF], F32, name=f"factor{h}", tag="hold_factor" if h else "factor0", align_bytes=64)
-            parts = [(a_second, 0, PACK)] if h else [(a_first[0], 0, 2), (a_first[1], 2, 2)]
+            parts = [(a_second, 0, PACK)] if h else [(rows, t, count) for rows, (t, count) in zip(a_first, row_sets)]
             for rows, t, count in parts:
                 nc.vector.scalar_tensor_tensor(
                     out=factor[h][:, t : t + count, :],
@@ -249,23 +254,25 @@ def tile_moe_sdb_relu_kernel(
             nc.sync.dma_start(out=rows, in_=windows[w][:, 0:T])
 
         y_codes = [keep.tile([P, T], I32, name=f"y_codes{s}", align_bytes=64) for s in range(2)]
-        y_s = [keep.tile([P, T], U8, name=f"y_s{s}", align_bytes=64) for s in range(2)]
+        y_s = keep.tile([P, 2, T], U8, name="y_s", align_bytes=64)
 
         def quantize_y(s, woven, lo, hi):
             nc.vector.quantize_mx(
                 out=y_codes[s][:, lo:hi].bitcast(FP8X4),
-                scales=y_s[s][:, lo:hi],
+                scales=y_s[:, s, lo:hi],
                 in_=woven[:].rearrange("p t d -> p (t d)"),
             )
 
-        def store_planes(s):
+        def store_words(s):
             words = out_1[s].rearrange("p t d -> p (t d)").bitcast(I32)
             for cols in [slice(0, HALF), slice(HALF, T)] if s else [slice(0, T)]:
                 (nc.sync if s else nc.scalar).dma_start(out=words[:, cols], in_=y_codes[s][:, cols])
+
+        def store_scales():
             for q in range(QUADRANTS):
-                queue = nc.scalar if s == 0 or q % 2 else nc.sync
-                queue.dma_start(
-                    out=out_2[s, 4 * q : 4 * q + 4, :].bitcast(I32), in_=y_s[s][32 * q : 32 * q + 4, :].bitcast(I32)
+                (nc.scalar if q % 2 else nc.sync).dma_start(
+                    out=out_2[:, 4 * q : 4 * q + 4, :].rearrange("s b t -> b s t").bitcast(I32),
+                    in_=y_s[32 * q : 32 * q + 4].bitcast(I32),
                 )
 
         make_factor(0)
@@ -277,12 +284,12 @@ def tile_moe_sdb_relu_kernel(
         gather(0, 2, "vector")
         gather(0, 3, "vector")
         round_da(0, False)
-        quantize_da(0)
-        packed = keep.tile([P, PASS], U8, name="packed", tag="hold_da0", align_bytes=64)
+        packed = keep.tile([P, PASS], U8, name="packed", align_bytes=64)
         w1_s = keep.tile([P, E - 1, PASS], U8, name="w1_s", align_bytes=64)
         nc.vector.tensor_copy(
             out=packed[:].rearrange("p (d m) -> p d m", d=PACK), in_=packed_raw[:].rearrange("p (m d) -> p d m", d=PACK)
         )
+        quantize_da(0)
         for e in range(1, E):
             for q in range(QUADRANTS):
                 nc.sync.dma_start(
@@ -323,7 +330,7 @@ def tile_moe_sdb_relu_kernel(
         thirds = [(0, 384), (384, 384), (768, 256)]
         dx_two_experts(5, 0, "vector", 6)
         dx_two_experts(3, 1, "vector", 4)
-        dx_two_experts(2, 1, "scalar", 2)
+        dx_two_experts(2, 1, "vector", 2)
         dx_two_experts(0, 1, "scalar", 0)
         scatter(2, 2 * C, C, "scalar")
         dx_two_experts(1, 1, "scalar", 1)
@@ -367,7 +374,7 @@ def tile_moe_sdb_relu_kernel(
             nc.vector.tensor_copy(out=woven_by_runs(y0[h][:]), in_=by_runs(quad[:, :, halves[h]]))
         for h in range(2):
             quantize_y(0, y0[h], h * HALF, (h + 1) * HALF)
-        store_planes(0)
+        store_words(0)
 
         spans = [(0, T // 2), (T // 2, 3 * T // 4), (3 * T // 4, T)]
         y1 = [
@@ -381,4 +388,5 @@ def tile_moe_sdb_relu_kernel(
             copy(engine, woven[:, :, PACK - 1], windows[7][:, lo:hi])
         for woven, (lo, hi) in zip(y1, spans):
             quantize_y(1, woven, lo, hi)
-        store_planes(1)
+        store_words(1)
+        store_scales()

@@ -66,7 +66,7 @@ def tile_moe_sdb_relu_kernel(
         w1_raw = keep.tile([P, E, 2 * PASS], U8, name="w1_raw", align_bytes=64)
         row_sets = [(0, 1), (1, 1), (2, 2)]
         a_first = [keep.tile([P, count, HALF], F32, name=f"a_first{t}") for t, count in row_sets]
-        a_second = keep.tile([P, PACK, HALF], F32, name="a_second")
+        a_second = [keep.tile([P, PACK, C], F32, name=f"a{e}", tag=f"a{e}", align_bytes=64) for e in (2, 3)]
         gate_sb = [keep.tile([P, HALF], F32, name=f"gate{h}") for h in range(2)]
 
         nc.gpsimd.memset(packed_raw[:].bitcast(I32), 0)
@@ -94,7 +94,8 @@ def tile_moe_sdb_relu_kernel(
                 in_=w1t_scales[:, 0, 4 * q : 4 * q + 4, PASS:K].bitcast(I32),
             )
         nc.sync.dma_start(out=gate_sb[1][:], in_=gate[:, HALF:S])
-        nc.sync.dma_start(out=a_second[:], in_=a_rows[:, :, HALF:S])
+        for u in range(2):
+            nc.sync.dma_start(out=a_second[u][:], in_=a_rows[:, :, HALF + u * C : HALF + (u + 1) * C])
         nc.sync.dma_start(out=w1_raw[:].bitcast(I32), in_=w1_rows[:, :, 2 * PASS : 2 * K].bitcast(I32))
         nc.sync.dma_start(out=w1_first[1][:].bitcast(I32), in_=w1_rows[:, 2:4, 0 : 2 * PASS].bitcast(I32))
 
@@ -109,13 +110,16 @@ def tile_moe_sdb_relu_kernel(
 
         def make_factor(h):
             factor[h] = keep.tile([P, PACK, HALF], F32, name=f"factor{h}", tag="hold_factor" if h else "factor0", align_bytes=64)
-            parts = [(a_second, 0, PACK)] if h else [(rows, t, count) for rows, (t, count) in zip(a_first, row_sets)]
-            for rows, t, count in parts:
+            if h:
+                parts = [(a_second[u], slice(0, PACK), slice(u * C, (u + 1) * C)) for u in range(2)]
+            else:
+                parts = [(rows, slice(t, t + count), slice(0, HALF)) for rows, (t, count) in zip(a_first, row_sets)]
+            for rows, sets, cols in parts:
                 nc.vector.scalar_tensor_tensor(
-                    out=factor[h][:, t : t + count, :],
+                    out=factor[h][:, sets, cols],
                     in0=rows[:],
                     scalar=0.0,
-                    in1=gate_sb[h][:].unsqueeze(1).to_broadcast([P, count, HALF]),
+                    in1=gate_sb[h][:, cols].unsqueeze(1).to_broadcast(rows.shape),
                     op0=ALU.is_gt,
                     op1=ALU.mult,
                 )
@@ -161,7 +165,7 @@ def tile_moe_sdb_relu_kernel(
             g = min(e, 2)
             first, width = groups[g]
             if g not in da_bf:
-                tag = "hold_factor" if g == 0 else f"da_bf{g}"
+                tag = ("hold_factor", "a2", "da_bf2")[g]
                 da_bf[g] = keep.tile([P, width, PACK], BF16, name=f"da_bf{g}", tag=tag, align_bytes=64)
             woven = woven_by_runs(da_bf[g][:, e * C - first : (e + 1) * C - first, :])
             if times_factor:
@@ -296,18 +300,18 @@ def tile_moe_sdb_relu_kernel(
                     out=w1_s[32 * q : 32 * q + 4, e - 1, :].bitcast(I32),
                     in_=packed[32 * q + 4 * e : 32 * q + 4 * e + 4].bitcast(I32),
                 )
-        for e in (1, 2):
+        for e in (2, 1):
             for t in range(PACK):
                 gather(e, t, "scalar")
-        round_da(1, True)
         make_factor(1)
+        round_da(1, True)
+        round_da(2, True)
         quantize_da(1)
         for e in range(2):
             for i in range(2):
                 dx_one_expert(e, i, "scalar")
             for w in range(PACK - 1):
                 scatter(w, e * C, C, "scalar")
-        round_da(2, True)
         for t in range(PACK):
             gather(3, t, "vector")
         w1_codes = keep.tile([P, 2, 2 * PASS], U8, name="w1_codes", tag="hold_factor", align_bytes=64)

@@ -24,8 +24,8 @@ S = E * C
 HALF = S // 2
 PASS = P * PACK
 RUN = 2
-WIDE = 1376
 KIB = 1024
+LAP = 64
 
 
 def load_scale_rows(nc, plane, rows):
@@ -45,34 +45,44 @@ def tile_moe_sdb_relu_kernel(
         def bank(b):
             return psum.tile([P, BANK], F32, name="acc", tag=f"bank{b}")
 
+        def held(shape, dtype, name, tag=None):
+            return keep.tile(shape, dtype, name=name, tag=tag or name, align_bytes=64)
+
+        def placed(shape, dtype, name, offset):
+            return turns.tile(shape, dtype, name=name, offset=offset, align_bytes=64)
+
         def copy(engine, out, in_):
             if engine == "vector":
                 nc.vector.tensor_copy(out=out, in_=in_)
             else:
                 nc.scalar.copy(out=out, in_=in_)
 
-        groups = [(0, C), (C, C), (HALF, HALF)]
-
         offsets = keep.tile([P, S // LANES], U16, name="offsets")
-        w2_raw = keep.tile([P, H], I32, name="w2_raw", align_bytes=64)
-        w2_raw_s = keep.tile([P, H], U8, name="w2_raw_s", align_bytes=64)
-        w2_codes = keep.tile([P, H], I32, name="w2_codes", align_bytes=64)
-        w2_s = keep.tile([P, H], U8, name="w2_s", align_bytes=64)
-        dy_codes = keep.tile([P, T], I32, name="dy_codes", align_bytes=64)
-        dy_s = keep.tile([P, T], U8, name="dy_s", align_bytes=64)
-        w1_raw_s = keep.tile([P, E, PASS], U8, name="w1_raw_s", align_bytes=64)
-        packed_raw = keep.tile([P, PASS], U8, name="packed_raw", align_bytes=64)
-        w1_first = [keep.tile([P, 2, 2 * PASS], U8, name=f"w1_first{i}", align_bytes=64) for i in range(2)]
-        w1_raw = keep.tile([P, E, 2 * PASS], U8, name="w1_raw", align_bytes=64)
-        row_sets = [(0, 1), (1, 1), (2, 2)]
-        a_first = [keep.tile([P, count, HALF], F32, name=f"a_first{t}") for t, count in row_sets]
-        a_second = [keep.tile([P, PACK, C], F32, name=f"a{e}", tag=f"a{e}", align_bytes=64) for e in (2, 3)]
-        gate_sb = [keep.tile([P, HALF], F32, name=f"gate{h}") for h in range(2)]
+        w2_raw = held([P, H], I32, "w2_raw")
+        w2_raw_s = held([P, H], U8, "w2_raw_s")
+        w2_codes = held([P, H], I32, "w2_codes")
+        w2_s = held([P, H], U8, "w2_s")
+        dy_codes = held([P, T], I32, "dy_codes")
+        dy_s = held([P, T], U8, "dy_s")
+        w1_first_s = held([P, E, PASS], U8, "w1_first_s")
+        w1_first = [held([P, 2, 2 * PASS], U8, f"w1_first{i}") for i in range(2)]
+        packed_raw = held([P, PASS], U8, "packed_raw")
+        w1_raw = [held([P, 2, 2 * PASS], U8, f"w1_raw{i}") for i in range(2)]
+        a_sb = [held([P, PACK, C], F32, f"a{e}") for e in range(E)]
+        gate_sb = [held([P, HALF], F32, f"gate{h}") for h in range(2)]
 
         nc.gpsimd.memset(packed_raw[:].bitcast(I32), 0)
 
         a_rows = a.rearrange("(p t) j -> p t j", t=PACK)
         w1_rows = w1t_words.rearrange("e s p c -> (s p) e c")
+
+        def load_a(e):
+            nc.sync.dma_start(out=a_sb[e][:], in_=a_rows[:, :, e * C : (e + 1) * C])
+
+        def load_w1(tiles, i, s):
+            words = w1_rows[:, 2 * i : 2 * i + 2, 2 * s * PASS : 2 * (s + 1) * PASS]
+            nc.sync.dma_start(out=tiles[i][:].bitcast(I32), in_=words.bitcast(I32))
+
         for q in range(QUADRANTS):
             rows = w2t_scales[0, 4 * q : 4 * q + 4].bitcast(I32)
             nc.sync.dma_start(
@@ -82,22 +92,22 @@ def tile_moe_sdb_relu_kernel(
         nc.sync.dma_start(out=dy_codes[:], in_=dy_words[0].rearrange("p t d -> p (t d)").bitcast(I32))
         load_scale_rows(nc, dy_s, dy_scales[0])
         nc.sync.dma_start(out=gate_sb[0][:], in_=gate[:, 0:HALF])
-        nc.sync.dma_start(out=a_first[0][:], in_=a_rows[:, 0:1, 0:HALF])
+        load_a(0)
         nc.sync.dma_start(offsets[:], offs)
-        nc.sync.dma_start(out=a_first[1][:], in_=a_rows[:, 1:2, 0:HALF])
-        nc.sync.dma_start(out=a_first[2][:], in_=a_rows[:, 2:4, 0:HALF])
-        load_scale_rows(nc, w1_raw_s, w1t_scales.rearrange("e s b k -> (s b) e k")[:, :, 0:PASS])
-        nc.sync.dma_start(out=w1_first[0][:].bitcast(I32), in_=w1_rows[:, 0:2, 0 : 2 * PASS].bitcast(I32))
+        load_a(1)
+        load_scale_rows(nc, w1_first_s, w1t_scales.rearrange("e s b k -> (s b) e k")[:, :, 0:PASS])
+        load_w1(w1_first, 0, 0)
+        load_w1(w1_raw, 0, 1)
+        nc.sync.dma_start(out=gate_sb[1][:], in_=gate[:, HALF:S])
+        load_a(2)
+        load_a(3)
+        load_w1(w1_first, 1, 0)
         for q in range(QUADRANTS):
             nc.sync.dma_start(
                 out=packed_raw[32 * q : 32 * q + 4 * E].bitcast(I32),
                 in_=w1t_scales[:, 0, 4 * q : 4 * q + 4, PASS:K].bitcast(I32),
             )
-        nc.sync.dma_start(out=gate_sb[1][:], in_=gate[:, HALF:S])
-        for u in range(2):
-            nc.sync.dma_start(out=a_second[u][:], in_=a_rows[:, :, HALF + u * C : HALF + (u + 1) * C])
-        nc.sync.dma_start(out=w1_raw[:].bitcast(I32), in_=w1_rows[:, :, 2 * PASS : 2 * K].bitcast(I32))
-        nc.sync.dma_start(out=w1_first[1][:].bitcast(I32), in_=w1_rows[:, 2:4, 0 : 2 * PASS].bitcast(I32))
+        load_w1(w1_raw, 1, 1)
 
         nc.vector.tensor_copy(
             out=w2_codes[:].rearrange("p (t m) -> p m t", t=PACK), in_=w2_raw[:].rearrange("p (m t) -> p m t", t=PACK)
@@ -106,54 +116,40 @@ def tile_moe_sdb_relu_kernel(
             out=w2_s[:].rearrange("p (t m) -> p m t", t=PACK), in_=w2_raw_s[:].rearrange("p (m t) -> p m t", t=PACK)
         )
 
-        factor, da, da_bf, da_codes, da_s = {}, {}, {}, {}, {}
-
-        def make_factor(h):
-            factor[h] = keep.tile([P, PACK, HALF], F32, name=f"factor{h}", tag="hold_factor" if h else "factor0", align_bytes=64)
-            if h:
-                parts = [(a_second[u], slice(0, PACK), slice(u * C, (u + 1) * C)) for u in range(2)]
-            else:
-                parts = [(rows, slice(t, t + count), slice(0, HALF)) for rows, (t, count) in zip(a_first, row_sets)]
-            for rows, sets, cols in parts:
-                nc.vector.scalar_tensor_tensor(
-                    out=factor[h][:, sets, cols],
-                    in0=rows[:],
-                    scalar=0.0,
-                    in1=gate_sb[h][:, cols].unsqueeze(1).to_broadcast(rows.shape),
-                    op0=ALU.is_gt,
-                    op1=ALU.mult,
-                )
-
         def slots(first, width):
             return offsets[:, first // LANES : (first + width) // LANES]
 
-        dc = [keep.tile([P, T], F32, name=f"dc{t}") for t in range(PACK)]
-
-        def first_product(t, h, engine):
-            cols = slice(h * BANK, (h + 1) * BANK)
-            acc = bank(2 * t + h)
+        def mx(out, codes, scales, moving, moving_scales):
             nc.tensor.matmul_mx(
-                out=acc[:],
-                lhsT=w2_codes[:, t * P : (t + 1) * P].bitcast(FP8X4),
-                lhsT_scale=w2_s[:, t * P : (t + 1) * P],
-                rhs=dy_codes[:, cols].bitcast(FP8X4),
-                rhs_scale=dy_s[:, cols],
-                start=True,
-                stop=True,
+                out=out, lhsT=codes, lhsT_scale=scales, rhs=moving, rhs_scale=moving_scales, start=True, stop=True
             )
-            copy(engine, dc[t][:, cols], acc[:])
 
-        def factor_of(e):
-            return factor[e // 2][:, :, (e % 2) * C : (e % 2 + 1) * C]
+        dc = [held([P, T], F32, f"dc{t}") for t in range(PACK)]
+        factor, da, da_bf, da_codes, da_s = {}, {}, {}, {}, {}
 
-        def gather(e, t, engine):
-            if e not in da:
-                da[e] = keep.tile([P, PACK, C], F32, name=f"da{e}", tag=f"hold_da{e}", align_bytes=64)
-            picked = dc[t][:].indirect(slots(e * C, C))
-            if engine == "vector":
-                nc.vector.tensor_tensor(da[e][:, t, :], picked, factor_of(e)[:, t, :], ALU.mult)
+        def make_factor(e):
+            factor[e] = held([P, PACK, C], F32, f"factor{e}", ("factor0", "factor1", "da0", "factor1")[e])
+            row = gate_sb[e // 2][:, (e % 2) * C : (e % 2 + 1) * C]
+            nc.vector.scalar_tensor_tensor(
+                out=factor[e][:],
+                in0=a_sb[e][:],
+                scalar=0.0,
+                in1=row.unsqueeze(1).to_broadcast([P, PACK, C]),
+                op0=ALU.is_gt,
+                op1=ALU.mult,
+            )
+
+        def gather(e, engine):
+            if e == E - 1:
+                da[e] = placed([P, PACK, C], F32, f"da{e}", 12 * KIB)
             else:
-                nc.scalar.activation(da[e][:, t, :], picked, COPY)
+                da[e] = held([P, PACK, C], F32, f"da{e}")
+            for t in range(PACK):
+                picked = dc[t][:].indirect(slots(e * C, C))
+                if engine == "vector":
+                    nc.vector.tensor_tensor(da[e][:, t, :], picked, factor[e][:, t, :], ALU.mult)
+                else:
+                    nc.scalar.activation(da[e][:, t, :], picked, COPY)
 
         def by_runs(rows):
             return rows.rearrange("p t (c i) -> p c t i", i=RUN)
@@ -162,103 +158,186 @@ def tile_moe_sdb_relu_kernel(
             return woven.rearrange("p (c i) t -> p c t i", i=RUN)
 
         def round_da(e, times_factor):
-            g = min(e, 2)
-            first, width = groups[g]
-            if g not in da_bf:
-                tag = ("hold_factor", "a2", "da_bf2")[g]
-                da_bf[g] = keep.tile([P, width, PACK], BF16, name=f"da_bf{g}", tag=tag, align_bytes=64)
-            woven = woven_by_runs(da_bf[g][:, e * C - first : (e + 1) * C - first, :])
+            da_bf[e] = held([P, C, PACK], BF16, f"da_bf{e}", ("da_bf0", "da_bf0", "da_bf2", "da_bf3")[e])
+            woven = woven_by_runs(da_bf[e][:])
             if times_factor:
-                nc.vector.tensor_tensor(woven, by_runs(da[e][:]), by_runs(factor_of(e)), ALU.mult)
+                nc.vector.tensor_tensor(woven, by_runs(da[e][:]), by_runs(factor[e][:]), ALU.mult)
             else:
                 nc.vector.tensor_copy(out=woven, in_=by_runs(da[e][:]))
 
-        def quantize_da(g):
-            first, width = groups[g]
-            codes = keep.tile([P, width], I32, name=f"da_codes{g}", align_bytes=64)
-            scales = keep.tile([P, width], U8, name=f"da_s{g}", align_bytes=64)
+        def quantize_da(e):
+            da_codes[e] = held([P, C], I32, f"da_codes{e}")
+            da_s[e] = held([P, C], U8, f"da_s{e}")
             nc.vector.quantize_mx(
-                out=codes[:].bitcast(FP8X4), scales=scales[:], in_=da_bf[g][:].rearrange("p j t -> p (j t)")
+                out=da_codes[e][:].bitcast(FP8X4), scales=da_s[e][:], in_=da_bf[e][:].rearrange("p j t -> p (j t)")
             )
-            for u in range(width // C):
-                da_codes[first // C + u] = codes[:, u * C : (u + 1) * C]
-                da_s[first // C + u] = scales[:, u * C : (u + 1) * C]
+
+        dealt = {}
+
+        def deal_words(i, offset, engine):
+            dealt[i] = placed([P, 2, 2 * PASS], U8, f"dealt{i}", offset)
+            copy(
+                engine,
+                dealt[i][:].bitcast(U16).rearrange("p e (d m) -> p e d m", d=PACK),
+                w1_raw[i][:].bitcast(U16).rearrange("p e (m d) -> p e d m", d=PACK),
+            )
 
         def second_product(out, w, e):
             s, j = divmod(w, PACK)
             if s == 0:
-                codes = w1_first[e // 2][:, e % 2, 2 * j * P : 2 * (j + 1) * P]
-                scales = w1_raw_s[:, e, j * P : (j + 1) * P]
+                codes, scales = w1_first[e // 2][:, e % 2, :], w1_first_s[:, e, :]
             else:
-                codes = (w1_late if e < 2 else w1_codes)[:, e % 2, 2 * j * P : 2 * (j + 1) * P]
-                scales = (packed[:] if e == 0 else w1_s[:, e - 1, :])[:, j * P : (j + 1) * P]
-            nc.tensor.matmul_mx(
-                out=out,
-                lhsT=codes.bitcast(FP4X4),
-                lhsT_scale=scales,
-                rhs=da_codes[e].bitcast(FP8X4),
-                rhs_scale=da_s[e],
-                start=True,
-                stop=True,
+                codes, scales = dealt[e // 2][:, e % 2, :], (packed[:] if e == 0 else w1_s[:, e - 1, :])
+            mx(
+                out,
+                codes[:, 2 * j * P : 2 * (j + 1) * P].bitcast(FP4X4),
+                scales[:, j * P : (j + 1) * P],
+                da_codes[e][:].bitcast(FP8X4),
+                da_s[e][:],
             )
 
-        pairs = [(0, 3), (1, 2)]
-        dx_pairs = [
-            keep.tile([P, 2, S], F32, name="dx0"),
-            turns.tile([P, 2, S], F32, name="dx1", offset=21 * KIB, align_bytes=64),
-        ]
-        dx = {w: dx_pairs[i][:, u, :] for i, pair in enumerate(pairs) for u, w in enumerate(pair)}
-        for w in (5, 6):
-            dx.setdefault(w, keep.tile([P, S], F32, name=f"dx{w}")[:])
-        dx.setdefault(4, turns.tile([P, S], F32, name="dx4", offset=32 * KIB, align_bytes=64)[:])
-        dx.setdefault(7, turns.tile([P, S], F32, name="dx7", offset=55 * KIB // 2, align_bytes=64)[:])
-
-        last_bank = []
-
-        def dx_one_expert(e, i, engine):
-            acc = bank(2 * e + i)
-            for u, w in enumerate(pairs[i]):
-                second_product(acc[:, u * C : (u + 1) * C], w, e)
-            copy(engine, dx_pairs[i][:, :, e * C : (e + 1) * C], acc[:].rearrange("p (u j) -> p u j", u=2))
-
-        def dx_two_experts(w, h, engine, b):
+        def fill_bank(b, parts):
             acc = bank(b)
-            for u in range(2):
-                second_product(acc[:, u * C : (u + 1) * C], w, 2 * h + u)
-            if (w, h) == (7, 1):
-                copy(engine, dx[w][:, HALF : HALF + C], acc[:, 0:C])
-                last_bank.append(acc)
-            else:
-                copy(engine, dx[w][:, h * HALF : (h + 1) * HALF], acc[:])
+            for u, (w, e) in enumerate(parts):
+                second_product(acc[:, u * C : (u + 1) * C], w, e)
+            return acc
 
-        windows = {w: keep.tile([P, T], F32, name=f"window{w}") for w in (0, 2)}
-        windows.setdefault(1, turns.tile([P, T], F32, name="window1", offset=38 * KIB, align_bytes=64))
-        windows.setdefault(3, keep.tile([P, WIDE], F32, name="window3"))
-        windows.setdefault(4, turns.tile([P, T], F32, name="window4", offset=47 * KIB // 2, align_bytes=64))
-        windows.setdefault(5, keep.tile([P, WIDE], F32, name="window5"))
-        windows.setdefault(6, turns.tile([P, WIDE], F32, name="window6", offset=18 * KIB, align_bytes=64))
-        windows.setdefault(7, turns.tile([P, T], F32, name="window7", offset=35 * KIB, align_bytes=64))
+        def two_windows(b, e, w, out):
+            acc = fill_bank(b, [(w, e), (w + 1, e)])
+            nc.scalar.copy(out=out, in_=acc[:].rearrange("p (u j) -> p u j", u=2))
 
-        def scatter(w, first, width, engine):
-            source = dx[w][:, first : first + width]
-            placed = windows[w][:].indirect(slots(first, width))
+        windows = {}
+
+        def scatter(w, first, source, engine):
+            target = windows[w][:].indirect(slots(first, source.shape[1]))
             if engine == "vector":
-                nc.vector.tensor_copy(placed, source)
+                nc.vector.tensor_copy(target, source)
             else:
-                nc.scalar.activation(placed, source, COPY)
-
-        dealt_rows = out_0[PASS:K].rearrange("(p d) t -> d p t", d=PACK)
-
-        quad = turns.tile([P, PACK, T], F32, name="quad", offset=0, align_bytes=64)
-
-        trio = turns.tile([P, PACK - 1, T], F32, name="trio", offset=41 * KIB, align_bytes=64)
+                nc.scalar.activation(target, source, COPY)
 
         def store_window(w):
-            rows = out_0[w * P : (w + 1) * P] if w < PACK else dealt_rows[w - PACK]
-            nc.sync.dma_start(out=rows, in_=windows[w][:, 0:T])
+            nc.sync.dma_start(out=out_0[w * P : (w + 1) * P], in_=windows[w][:])
 
-        y_codes = [keep.tile([P, T], I32, name=f"y_codes{s}", align_bytes=64) for s in range(2)]
-        y_s = keep.tile([P, 2, T], U8, name="y_s", align_bytes=64)
+        make_factor(0)
+        for t in range(PACK):
+            for h in range(2):
+                cols = slice(h * BANK, (h + 1) * BANK)
+                acc = bank(2 * t + h)
+                mx(
+                    acc[:],
+                    w2_codes[:, t * P : (t + 1) * P].bitcast(FP8X4),
+                    w2_s[:, t * P : (t + 1) * P],
+                    dy_codes[:, cols].bitcast(FP8X4),
+                    dy_s[:, cols],
+                )
+                nc.scalar.copy(out=dc[t][:, cols], in_=acc[:])
+        gather(0, "vector")
+        make_factor(1)
+        round_da(0, False)
+        quantize_da(0)
+        gather(1, "scalar")
+        deal_words(0, 68 * KIB, "scalar")
+        make_factor(2)
+        round_da(1, True)
+        quantize_da(1)
+        gather(2, "vector")
+        round_da(2, False)
+        quantize_da(2)
+        make_factor(3)
+        gather(3, "vector")
+        round_da(3, False)
+        quantize_da(3)
+
+        packed = held([P, PASS], U8, "packed", "da_bf2")
+        w1_s = held([P, E - 1, PASS], U8, "w1_s")
+        nc.vector.tensor_copy(
+            out=packed[:].rearrange("p (d m) -> p d m", d=PACK), in_=packed_raw[:].rearrange("p (m d) -> p d m", d=PACK)
+        )
+        for e in range(1, E):
+            for q in range(QUADRANTS):
+                nc.sync.dma_start(
+                    out=w1_s[32 * q : 32 * q + 4, e - 1, :].bitcast(I32),
+                    in_=packed[32 * q + 4 * e : 32 * q + 4 * e + 4].bitcast(I32),
+                )
+
+        for w in range(PACK):
+            windows[w] = placed([P, T], F32, f"window{w}", 4 * w * KIB)
+        dx01 = placed([P, 2, S], F32, "dx01", 24 * KIB)
+        dx23 = held([P, 2, HALF], F32, "dx23")
+        for e in range(2):
+            cols = slice(e * C, (e + 1) * C)
+            two_windows(2 * e, e, 0, dx01[:, :, cols])
+            two_windows(2 * e + 1, e, 2, dx23[:, :, cols])
+            for w in range(3):
+                scatter(w, e * C, (dx01[:, w, cols] if w < 2 else dx23[:, 0, cols]), "scalar")
+        scatter(3, 0, dx23[:, 1, :], "vector")
+        late = {2: placed([P, HALF], F32, "late2", 60 * KIB), 3: placed([P, HALF], F32, "late3", 64 * KIB)}
+        two_windows(4, 2, 0, dx01[:, :, 2 * C : 3 * C])
+        nc.vector.tensor_copy(out=late[3][:], in_=fill_bank(5, [(3, 2), (3, 3)])[:])
+        nc.vector.tensor_copy(out=late[2][:], in_=fill_bank(6, [(2, 2), (2, 3)])[:])
+        for w in range(2):
+            scatter(w, 2 * C, dx01[:, w, 2 * C : 3 * C], "scalar")
+        two_windows(7, 3, 0, dx01[:, :, 3 * C : S])
+        scatter(3, HALF, late[3][:], "vector")
+        store_window(3)
+
+        for w in range(2):
+            scatter(w, 3 * C, dx01[:, w, 3 * C : S], "scalar")
+            store_window(w)
+        scatter(2, HALF, late[2][:], "vector")
+        store_window(2)
+        halves = [slice(0, HALF), slice(HALF, T)]
+        quad = held([P, PACK, T], F32, "quad")
+        back = out_0[0:PASS].rearrange("(p d) t -> p d t", d=PACK)
+        for cols in halves:
+            nc.sync.dma_start(out=quad[:, :, cols], in_=back[:, :, cols])
+
+        def half_bank(b, w, h):
+            return fill_bank(b, [(w, 2 * h), (w, 2 * h + 1)])
+
+        dx4 = placed([P, S], F32, "dx4", 20 * KIB + LAP)
+        dx6 = [placed([P, HALF], F32, "dx6a", 24 * KIB + LAP), placed([P, HALF], F32, "dx6b", 22 * KIB)]
+        dx5 = [placed([P, HALF], F32, "dx5a", 26 * KIB + LAP), placed([P, HALF], F32, "dx5b", 28 * KIB + LAP)]
+        dx7 = placed([P, 3 * C], F32, "dx7", 32 * KIB - LAP)
+        windows.setdefault(4, placed([P, T], F32, "window4", 40 * KIB))
+        windows.setdefault(5, held([P, T], F32, "window5"))
+        windows.setdefault(6, held([P, T], F32, "window6"))
+        windows.setdefault(7, placed([P, T], F32, "window7", 33 * KIB // 2))
+        trio = placed([P, PACK - 1, T], F32, "trio", 2 * KIB)
+        thirds = [slice(0, 384), slice(384, 768), slice(768, S)]
+
+        deal_words(1, 64 * KIB, "vector")
+        nc.scalar.copy(out=dx5[0][:], in_=half_bank(0, 5, 0)[:])
+        nc.scalar.copy(out=dx4[:, halves[0]], in_=half_bank(1, 4, 0)[:])
+        nc.scalar.copy(out=dx6[0][:], in_=half_bank(2, 6, 0)[:])
+        scatter(5, 0, dx5[0][:], "vector")
+        scatter(4, 0, dx4[:, thirds[0]], "scalar")
+        nc.scalar.copy(out=dx4[:, halves[1]], in_=half_bank(3, 4, 1)[:])
+        nc.scalar.copy(out=dx5[1][:], in_=half_bank(4, 5, 1)[:])
+        scatter(6, 0, dx6[0][:], "vector")
+        scatter(4, 384, dx4[:, thirds[1]], "scalar")
+        nc.scalar.copy(out=dx7[:, halves[0]], in_=half_bank(6, 7, 0)[:])
+        scatter(5, HALF, dx5[1][:], "vector")
+        nc.sync.dma_start(out=trio[:, 1, :], in_=windows[5][:])
+        scatter(4, 768, dx4[:, thirds[2]], "scalar")
+        nc.sync.dma_start(out=trio[:, 0, :], in_=windows[4][:])
+        last_bank = half_bank(7, 7, 1)
+        nc.scalar.copy(out=dx7[:, HALF : 3 * C], in_=last_bank[:, 0:C])
+        nc.vector.tensor_copy(out=dx6[1][:], in_=half_bank(5, 6, 1)[:])
+        scatter(6, HALF, dx6[1][:], "vector")
+        nc.vector.tensor_copy(out=trio[:, 2, :], in_=windows[6][:])
+        dealt_rows = out_0[PASS:K].rearrange("(p d) t -> p d t", d=PACK)
+        for planes in (slice(0, 2), slice(2, 3)):
+            nc.sync.dma_start(out=dealt_rows[:, planes, :], in_=trio[:, planes, :])
+        scatter(7, 0, dx7[:, thirds[0]], "scalar")
+        scatter(7, 384, dx7[:, thirds[1]], "scalar")
+        dx_last = placed([P, C], F32, "dx_last", 40 * KIB)
+        nc.scalar.copy(out=dx_last[:], in_=last_bank[:, C:BANK])
+        scatter(7, 768, dx_last[:], "scalar")
+        nc.sync.dma_start(out=dealt_rows[:, PACK - 1, :], in_=windows[7][:])
+
+        y_codes = [held([P, T], I32, f"y_codes{s}") for s in range(2)]
+        y_s = held([P, 2, T], U8, "y_s")
 
         def quantize_y(s, woven, lo, hi):
             nc.vector.quantize_mx(
@@ -267,124 +346,26 @@ def tile_moe_sdb_relu_kernel(
                 in_=woven[:].rearrange("p t d -> p (t d)"),
             )
 
-        def store_words(s):
+        def store_words(s, cols):
             words = out_1[s].rearrange("p t d -> p (t d)").bitcast(I32)
-            for cols in [slice(0, HALF), slice(HALF, T)] if s else [slice(0, T)]:
-                (nc.sync if s else nc.scalar).dma_start(out=words[:, cols], in_=y_codes[s][:, cols])
+            nc.sync.dma_start(out=words[:, cols], in_=y_codes[s][:, cols])
 
-        def store_scales():
-            for q in range(QUADRANTS):
-                (nc.scalar if q % 2 else nc.sync).dma_start(
-                    out=out_2[:, 4 * q : 4 * q + 4, :].rearrange("s b t -> b s t").bitcast(I32),
-                    in_=y_s[32 * q : 32 * q + 4].bitcast(I32),
-                )
-
-        make_factor(0)
-        for t in range(PACK):
-            first_product(t, 0, "scalar")
-            first_product(t, 1, "scalar")
-        gather(0, 0, "vector")
-        gather(0, 1, "vector")
-        gather(0, 2, "vector")
-        gather(0, 3, "vector")
-        round_da(0, False)
-        packed = keep.tile([P, PASS], U8, name="packed", align_bytes=64)
-        w1_s = keep.tile([P, E - 1, PASS], U8, name="w1_s", align_bytes=64)
-        nc.vector.tensor_copy(
-            out=packed[:].rearrange("p (d m) -> p d m", d=PACK), in_=packed_raw[:].rearrange("p (m d) -> p d m", d=PACK)
-        )
-        quantize_da(0)
-        for e in range(1, E):
-            for q in range(QUADRANTS):
-                nc.sync.dma_start(
-                    out=w1_s[32 * q : 32 * q + 4, e - 1, :].bitcast(I32),
-                    in_=packed[32 * q + 4 * e : 32 * q + 4 * e + 4].bitcast(I32),
-                )
-        for e in (2, 1):
-            for t in range(PACK):
-                gather(e, t, "scalar")
-        make_factor(1)
-        round_da(1, True)
-        round_da(2, True)
-        quantize_da(1)
-        for e in range(2):
-            for i in range(2):
-                dx_one_expert(e, i, "scalar")
-            for w in range(PACK - 1):
-                scatter(w, e * C, C, "scalar")
-        for t in range(PACK):
-            gather(3, t, "vector")
-        w1_codes = keep.tile([P, 2, 2 * PASS], U8, name="w1_codes", tag="hold_factor", align_bytes=64)
-        w1_late = keep.tile([P, 2, 2 * PASS], U8, name="w1_late", tag="hold_da3", align_bytes=64)
-
-        def deal_words(dealt, raw):
-            nc.vector.tensor_copy(
-                out=dealt[:].bitcast(U16).rearrange("p e (d m) -> p e d m", d=PACK),
-                in_=raw.bitcast(U16).rearrange("p e (m d) -> p e d m", d=PACK),
+        y0 = [placed([P, HALF, PACK], BF16, f"y0{h}", (48 + 4 * h) * KIB) for h in range(2)]
+        for h in range(2):
+            nc.gpsimd.tensor_scalar(
+                out=y0[h][:],
+                in0=quad[:, :, halves[h]].rearrange("p d t -> p t d"),
+                scalar1=1.0,
+                scalar2=-0.0,
+                op0=ALU.mult,
+                op1=ALU.add,
             )
-
-        deal_words(w1_codes, w1_raw[:, 2:4, :])
-        round_da(3, False)
-        deal_words(w1_late, w1_raw[:, 0:2, :])
-        quantize_da(2)
-
-        def hand_on(w):
-            nc.sync.dma_start(out=trio[:, w - PACK, :], in_=windows[w][:, 0:T])
-
-        thirds = [(0, 384), (384, 384), (768, 256)]
-        dx_two_experts(5, 0, "vector", 6)
-        dx_two_experts(3, 1, "vector", 4)
-        dx_two_experts(2, 1, "vector", 2)
-        dx_two_experts(0, 1, "scalar", 0)
-        scatter(2, 2 * C, C, "scalar")
-        dx_two_experts(1, 1, "scalar", 1)
-        scatter(3, 0, S, "vector")
-        store_window(3)
-        scatter(2, 3 * C, C, "vector")
-        store_window(2)
-        dx_two_experts(5, 1, "vector", 5)
-        dx_two_experts(6, 0, "vector", 6)
-        dx_two_experts(6, 1, "vector", 7)
-        for w in (0, 1):
-            scatter(w, 2 * C, C, "scalar")
-            dx_two_experts(4, w, "scalar", 4 - 2 * w)
-            scatter(w, 3 * C, C, "scalar")
-            store_window(w)
-        back = out_0[0:PASS].rearrange("(p d) t -> p d t", d=PACK)
-        for cols in (slice(0, HALF), slice(HALF, T)):
-            nc.sync.dma_start(out=quad[:, :, cols], in_=back[:, :, cols])
-        scatter(5, 0, S, "vector")
-        hand_on(5)
-        for h in range(2):
-            scatter(4, thirds[h][0], thirds[h][1], "scalar")
-            dx_two_experts(7, h, "scalar", h)
-        scatter(4, thirds[2][0], thirds[2][1], "scalar")
-        hand_on(4)
-        scatter(6, 0, S, "vector")
-        hand_on(6)
-        dealt_by_partition = out_0[PASS:K].rearrange("(p d) t -> p d t", d=PACK)
-        for planes in (slice(0, 2), slice(2, 3)):
-            nc.sync.dma_start(out=dealt_by_partition[:, planes, :], in_=trio[:, planes, :])
-        for first, width in thirds[0:2]:
-            scatter(7, first, width, "scalar")
-        dx_last = turns.tile([P, C], F32, name="dx_last", offset=24 * KIB, align_bytes=64)
-        nc.scalar.copy(out=dx_last[:], in_=last_bank[0][:, C:BANK])
-        nc.scalar.activation(windows[7][:].indirect(slots(S - C, C)), dx_last[:], COPY)
-        store_window(7)
-
-        halves = [slice(0, HALF), slice(HALF, T)]
-        y0 = [keep.tile([P, HALF, PACK], BF16, name=f"y0{h}", align_bytes=64) for h in range(2)]
-        for h in range(2):
-            nc.vector.tensor_copy(out=woven_by_runs(y0[h][:]), in_=by_runs(quad[:, :, halves[h]]))
         for h in range(2):
             quantize_y(0, y0[h], h * HALF, (h + 1) * HALF)
-        store_words(0)
+        store_words(0, slice(0, T))
 
         spans = [(0, T // 2), (T // 2, 3 * T // 4), (3 * T // 4, T)]
-        y1 = [
-            turns.tile([P, hi - lo, PACK], BF16, name=f"y1{lo}", offset=15 * KIB + 2 * PACK * lo, align_bytes=64)
-            for lo, hi in spans
-        ]
+        y1 = [placed([P, hi - lo, PACK], BF16, f"y1{lo}", 50 * KIB + 2 * PACK * lo) for lo, hi in spans]
         engines = ("vector", "vector", "scalar")
         for woven, (lo, hi), engine in zip(y1, spans, engines):
             copy(engine, woven_by_runs(woven[:, :, 0 : PACK - 1]), by_runs(trio[:, :, lo:hi]))
@@ -392,5 +373,10 @@ def tile_moe_sdb_relu_kernel(
             copy(engine, woven[:, :, PACK - 1], windows[7][:, lo:hi])
         for woven, (lo, hi) in zip(y1, spans):
             quantize_y(1, woven, lo, hi)
-        store_words(1)
-        store_scales()
+        for cols in halves:
+            store_words(1, cols)
+        for q in range(QUADRANTS):
+            (nc.scalar if q % 2 else nc.sync).dma_start(
+                out=out_2[:, 4 * q : 4 * q + 4, :].rearrange("s b t -> b s t").bitcast(I32),
+                in_=y_s[32 * q : 32 * q + 4].bitcast(I32),
+            )

@@ -26,6 +26,7 @@ PASS = P * PACK
 RUN = 2
 KIB = 1024
 LAP = 64
+WIDE = 1376
 
 
 def load_scale_rows(nc, plane, rows):
@@ -67,8 +68,10 @@ def tile_moe_sdb_relu_kernel(
         w1_first_s = held([P, E, PASS], U8, "w1_first_s")
         w1_first = [held([P, 2, 2 * PASS], U8, f"w1_first{i}") for i in range(2)]
         packed_raw = held([P, PASS], U8, "packed_raw")
-        w1_raw = [held([P, 2, 2 * PASS], U8, f"w1_raw{i}") for i in range(2)]
-        a_sb = [held([P, PACK, C], F32, f"a{e}") for e in range(E)]
+        w1_raw = held([P, E, 2 * PASS], U8, "w1_raw")
+        row_sets = [(0, 1), (1, 1), (2, 2)]
+        a_first = [held([P, count, HALF], F32, f"a_first{t}") for t, count in row_sets]
+        a_sb = {e: held([P, PACK, C], F32, f"a{e}") for e in (2, 3)}
         gate_sb = [held([P, HALF], F32, f"gate{h}") for h in range(2)]
 
         nc.gpsimd.memset(packed_raw[:].bitcast(I32), 0)
@@ -79,9 +82,9 @@ def tile_moe_sdb_relu_kernel(
         def load_a(e):
             nc.sync.dma_start(out=a_sb[e][:], in_=a_rows[:, :, e * C : (e + 1) * C])
 
-        def load_w1(tiles, i, s):
-            words = w1_rows[:, 2 * i : 2 * i + 2, 2 * s * PASS : 2 * (s + 1) * PASS]
-            nc.sync.dma_start(out=tiles[i][:].bitcast(I32), in_=words.bitcast(I32))
+        def load_w1_first(i):
+            words = w1_rows[:, 2 * i : 2 * i + 2, 0 : 2 * PASS]
+            nc.sync.dma_start(out=w1_first[i][:].bitcast(I32), in_=words.bitcast(I32))
 
         for q in range(QUADRANTS):
             rows = w2t_scales[0, 4 * q : 4 * q + 4].bitcast(I32)
@@ -92,22 +95,21 @@ def tile_moe_sdb_relu_kernel(
         nc.sync.dma_start(out=dy_codes[:], in_=dy_words[0].rearrange("p t d -> p (t d)").bitcast(I32))
         load_scale_rows(nc, dy_s, dy_scales[0])
         nc.sync.dma_start(out=gate_sb[0][:], in_=gate[:, 0:HALF])
-        load_a(0)
+        for rows, (t, count) in zip(a_first, row_sets):
+            nc.sync.dma_start(out=rows[:], in_=a_rows[:, t : t + count, 0:HALF])
         nc.sync.dma_start(offsets[:], offs)
-        load_a(1)
         load_scale_rows(nc, w1_first_s, w1t_scales.rearrange("e s b k -> (s b) e k")[:, :, 0:PASS])
-        load_w1(w1_first, 0, 0)
-        load_w1(w1_raw, 0, 1)
         nc.sync.dma_start(out=gate_sb[1][:], in_=gate[:, HALF:S])
         load_a(2)
+        load_w1_first(0)
         load_a(3)
-        load_w1(w1_first, 1, 0)
+        load_w1_first(1)
         for q in range(QUADRANTS):
             nc.sync.dma_start(
                 out=packed_raw[32 * q : 32 * q + 4 * E].bitcast(I32),
                 in_=w1t_scales[:, 0, 4 * q : 4 * q + 4, PASS:K].bitcast(I32),
             )
-        load_w1(w1_raw, 1, 1)
+        nc.sync.dma_start(out=w1_raw[:].bitcast(I32), in_=w1_rows[:, :, 2 * PASS : 2 * K].bitcast(I32))
 
         nc.vector.tensor_copy(
             out=w2_codes[:].rearrange("p (t m) -> p m t", t=PACK), in_=w2_raw[:].rearrange("p (m t) -> p m t", t=PACK)
@@ -127,23 +129,30 @@ def tile_moe_sdb_relu_kernel(
         dc = [held([P, T], F32, f"dc{t}") for t in range(PACK)]
         factor, da, da_bf, da_codes, da_s = {}, {}, {}, {}, {}
 
-        def make_factor(e):
-            factor[e] = held([P, PACK, C], F32, f"factor{e}", ("factor0", "factor1", "da0", "factor1")[e])
-            row = gate_sb[e // 2][:, (e % 2) * C : (e % 2 + 1) * C]
+        def mask_times_gate(out, rows, weights):
             nc.vector.scalar_tensor_tensor(
-                out=factor[e][:],
-                in0=a_sb[e][:],
+                out=out,
+                in0=rows[:],
                 scalar=0.0,
-                in1=row.unsqueeze(1).to_broadcast([P, PACK, C]),
+                in1=weights.unsqueeze(1).to_broadcast(rows.shape),
                 op0=ALU.is_gt,
                 op1=ALU.mult,
             )
 
+        def make_first_factors():
+            both = held([P, PACK, HALF], F32, "first_factors")
+            for rows, (t, count) in zip(a_first, row_sets):
+                mask_times_gate(both[:, t : t + count, :], rows, gate_sb[0][:])
+            for e in range(2):
+                factor.setdefault(e, both[:, :, e * C : (e + 1) * C])
+
+        def make_factor(e):
+            tile = placed([P, PACK, C], F32, f"factor{e}", (12, 76)[e - 2] * KIB)
+            mask_times_gate(tile[:], a_sb[e], gate_sb[1][:, (e - 2) * C : (e - 1) * C])
+            factor.setdefault(e, tile[:])
+
         def gather(e, engine):
-            if e == E - 1:
-                da[e] = placed([P, PACK, C], F32, f"da{e}", 12 * KIB)
-            else:
-                da[e] = held([P, PACK, C], F32, f"da{e}")
+            da[e] = placed([P, PACK, C], F32, f"da{e}", (12, 72, 76, 80)[e] * KIB)
             for t in range(PACK):
                 picked = dc[t][:].indirect(slots(e * C, C))
                 if engine == "vector":
@@ -157,11 +166,18 @@ def tile_moe_sdb_relu_kernel(
         def woven_by_runs(woven):
             return woven.rearrange("p (c i) t -> p c t i", i=RUN)
 
+        def weave_on_gpsimd(woven, rows):
+            nc.gpsimd.tensor_scalar(
+                out=woven, in0=rows.rearrange("p d t -> p t d"), scalar1=1.0, scalar2=-0.0, op0=ALU.mult, op1=ALU.add
+            )
+
         def round_da(e, times_factor):
-            da_bf[e] = held([P, C, PACK], BF16, f"da_bf{e}", ("da_bf0", "da_bf0", "da_bf2", "da_bf3")[e])
+            da_bf[e] = placed([P, C, PACK], BF16, f"da_bf{e}", (88, 88, 83, 86)[e] * KIB)
             woven = woven_by_runs(da_bf[e][:])
-            if times_factor:
-                nc.vector.tensor_tensor(woven, by_runs(da[e][:]), by_runs(factor[e][:]), ALU.mult)
+            if e >= 2:
+                weave_on_gpsimd(da_bf[e][:], da[e][:])
+            elif times_factor:
+                nc.vector.tensor_tensor(woven, by_runs(da[e][:]), by_runs(factor[e]), ALU.mult)
             else:
                 nc.vector.tensor_copy(out=woven, in_=by_runs(da[e][:]))
 
@@ -172,22 +188,12 @@ def tile_moe_sdb_relu_kernel(
                 out=da_codes[e][:].bitcast(FP8X4), scales=da_s[e][:], in_=da_bf[e][:].rearrange("p j t -> p (j t)")
             )
 
-        dealt = {}
-
-        def deal_words(i, offset, engine):
-            dealt[i] = placed([P, 2, 2 * PASS], U8, f"dealt{i}", offset)
-            copy(
-                engine,
-                dealt[i][:].bitcast(U16).rearrange("p e (d m) -> p e d m", d=PACK),
-                w1_raw[i][:].bitcast(U16).rearrange("p e (m d) -> p e d m", d=PACK),
-            )
-
         def second_product(out, w, e):
             s, j = divmod(w, PACK)
             if s == 0:
                 codes, scales = w1_first[e // 2][:, e % 2, :], w1_first_s[:, e, :]
             else:
-                codes, scales = dealt[e // 2][:, e % 2, :], (packed[:] if e == 0 else w1_s[:, e - 1, :])
+                codes, scales = dealt[:, e, :], (packed[:] if e == 0 else w1_s[:, e - 1, :])
             mx(
                 out,
                 codes[:, 2 * j * P : 2 * (j + 1) * P].bitcast(FP4X4),
@@ -202,9 +208,9 @@ def tile_moe_sdb_relu_kernel(
                 second_product(acc[:, u * C : (u + 1) * C], w, e)
             return acc
 
-        def two_windows(b, e, w, out):
+        def two_windows(b, e, w, out, engine):
             acc = fill_bank(b, [(w, e), (w + 1, e)])
-            nc.scalar.copy(out=out, in_=acc[:].rearrange("p (u j) -> p u j", u=2))
+            copy(engine, out, acc[:].rearrange("p (u j) -> p u j", u=2))
 
         windows = {}
 
@@ -218,7 +224,7 @@ def tile_moe_sdb_relu_kernel(
         def store_window(w):
             nc.sync.dma_start(out=out_0[w * P : (w + 1) * P], in_=windows[w][:])
 
-        make_factor(0)
+        make_first_factors()
         for t in range(PACK):
             for h in range(2):
                 cols = slice(h * BANK, (h + 1) * BANK)
@@ -232,23 +238,15 @@ def tile_moe_sdb_relu_kernel(
                 )
                 nc.scalar.copy(out=dc[t][:, cols], in_=acc[:])
         gather(0, "vector")
-        make_factor(1)
         round_da(0, False)
         quantize_da(0)
         gather(1, "scalar")
-        deal_words(0, 68 * KIB, "scalar")
         make_factor(2)
         round_da(1, True)
         quantize_da(1)
         gather(2, "vector")
-        round_da(2, False)
-        quantize_da(2)
-        make_factor(3)
-        gather(3, "vector")
-        round_da(3, False)
-        quantize_da(3)
 
-        packed = held([P, PASS], U8, "packed", "da_bf2")
+        packed = placed([P, PASS], U8, "packed", 72 * KIB)
         w1_s = held([P, E - 1, PASS], U8, "w1_s")
         nc.vector.tensor_copy(
             out=packed[:].rearrange("p (d m) -> p d m", d=PACK), in_=packed_raw[:].rearrange("p (m d) -> p d m", d=PACK)
@@ -260,32 +258,50 @@ def tile_moe_sdb_relu_kernel(
                     in_=packed[32 * q + 4 * e : 32 * q + 4 * e + 4].bitcast(I32),
                 )
 
+        dx01 = placed([P, 2, S], F32, "dx01", 24 * KIB)
+        early = held([P, 2, HALF], F32, "early")
+        late = {e: placed([P, 2, C], F32, f"late{e}", (52 + 4 * e) * KIB) for e in (2, 3)}
         for w in range(PACK):
             windows[w] = placed([P, T], F32, f"window{w}", 4 * w * KIB)
-        dx01 = placed([P, 2, S], F32, "dx01", 24 * KIB)
-        dx23 = held([P, 2, HALF], F32, "dx23")
+
+        def first_two_windows(e):
+            cols = slice(e * C, (e + 1) * C)
+            for w in range(2):
+                scatter(w, e * C, dx01[:, w, cols], "scalar")
+
         for e in range(2):
             cols = slice(e * C, (e + 1) * C)
-            two_windows(2 * e, e, 0, dx01[:, :, cols])
-            two_windows(2 * e + 1, e, 2, dx23[:, :, cols])
-            for w in range(3):
-                scatter(w, e * C, (dx01[:, w, cols] if w < 2 else dx23[:, 0, cols]), "scalar")
-        scatter(3, 0, dx23[:, 1, :], "vector")
-        late = {2: placed([P, HALF], F32, "late2", 60 * KIB), 3: placed([P, HALF], F32, "late3", 64 * KIB)}
-        two_windows(4, 2, 0, dx01[:, :, 2 * C : 3 * C])
-        nc.vector.tensor_copy(out=late[3][:], in_=fill_bank(5, [(3, 2), (3, 3)])[:])
-        nc.vector.tensor_copy(out=late[2][:], in_=fill_bank(6, [(2, 2), (2, 3)])[:])
-        for w in range(2):
-            scatter(w, 2 * C, dx01[:, w, 2 * C : 3 * C], "scalar")
-        two_windows(7, 3, 0, dx01[:, :, 3 * C : S])
-        scatter(3, HALF, late[3][:], "vector")
-        store_window(3)
-
-        for w in range(2):
-            scatter(w, 3 * C, dx01[:, w, 3 * C : S], "scalar")
+            two_windows(2 * e, e, 0, dx01[:, :, cols], "scalar")
+            two_windows(2 * e + 1, e, 2, early[:, :, cols], "vector" if e else "scalar")
+        for e in range(2):
+            first_two_windows(e)
+            scatter(2, e * C, early[:, 0, e * C : (e + 1) * C], "scalar")
+        round_da(2, False)
+        scatter(3, 0, early[:, 1, :], "vector")
+        quantize_da(2)
+        make_factor(3)
+        gather(3, "vector")
+        two_windows(4, 2, 0, dx01[:, :, 2 * C : 3 * C], "scalar")
+        two_windows(5, 2, 2, late[2][:], "vector")
+        round_da(3, False)
+        scatter(3, 2 * C, late[2][:, 1, :], "vector")
+        quantize_da(3)
+        dealt = placed([P, E, 2 * PASS], U8, "dealt", 81 * KIB)
+        nc.vector.tensor_copy(
+            out=dealt[:].bitcast(U16).rearrange("p e (d m) -> p e d m", d=PACK),
+            in_=w1_raw[:].bitcast(U16).rearrange("p e (m d) -> p e d m", d=PACK),
+        )
+        scatter(2, 2 * C, late[2][:, 0, :], "scalar")
+        first_two_windows(2)
+        acc = fill_bank(6, [(2, 3), (3, 3)])
+        for u in (1, 0):
+            nc.vector.tensor_copy(out=late[3][:, u, :], in_=acc[:, u * C : (u + 1) * C])
+        two_windows(7, 3, 0, dx01[:, :, 3 * C : S], "scalar")
+        first_two_windows(3)
+        for w in (3, 2):
+            scatter(w, 3 * C, late[3][:, w - 2, :], "vector")
+        for w in (3, 2, 0, 1):
             store_window(w)
-        scatter(2, HALF, late[2][:], "vector")
-        store_window(2)
         halves = [slice(0, HALF), slice(HALF, T)]
         quad = held([P, PACK, T], F32, "quad")
         back = out_0[0:PASS].rearrange("(p d) t -> p d t", d=PACK)
@@ -296,38 +312,37 @@ def tile_moe_sdb_relu_kernel(
             return fill_bank(b, [(w, 2 * h), (w, 2 * h + 1)])
 
         dx4 = placed([P, S], F32, "dx4", 20 * KIB + LAP)
-        dx6 = [placed([P, HALF], F32, "dx6a", 24 * KIB + LAP), placed([P, HALF], F32, "dx6b", 22 * KIB)]
-        dx5 = [placed([P, HALF], F32, "dx5a", 26 * KIB + LAP), placed([P, HALF], F32, "dx5b", 28 * KIB + LAP)]
+        dx6 = placed([P, S], F32, "dx6", 65 * KIB)
+        dx5 = placed([P, S], F32, "dx5", 61 * KIB)
         dx7 = placed([P, 3 * C], F32, "dx7", 32 * KIB - LAP)
         windows.setdefault(4, placed([P, T], F32, "window4", 40 * KIB))
-        windows.setdefault(5, held([P, T], F32, "window5"))
-        windows.setdefault(6, held([P, T], F32, "window6"))
+        windows.setdefault(5, placed([P, WIDE], F32, "window5", 92 * KIB))
+        windows.setdefault(6, placed([P, WIDE], F32, "window6", 57 * KIB))
         windows.setdefault(7, placed([P, T], F32, "window7", 33 * KIB // 2))
         trio = placed([P, PACK - 1, T], F32, "trio", 2 * KIB)
         thirds = [slice(0, 384), slice(384, 768), slice(768, S)]
 
-        deal_words(1, 64 * KIB, "vector")
-        nc.scalar.copy(out=dx5[0][:], in_=half_bank(0, 5, 0)[:])
-        nc.scalar.copy(out=dx4[:, halves[0]], in_=half_bank(1, 4, 0)[:])
-        nc.scalar.copy(out=dx6[0][:], in_=half_bank(2, 6, 0)[:])
-        scatter(5, 0, dx5[0][:], "vector")
-        scatter(4, 0, dx4[:, thirds[0]], "scalar")
-        nc.scalar.copy(out=dx4[:, halves[1]], in_=half_bank(3, 4, 1)[:])
-        nc.scalar.copy(out=dx5[1][:], in_=half_bank(4, 5, 1)[:])
-        scatter(6, 0, dx6[0][:], "vector")
-        scatter(4, 384, dx4[:, thirds[1]], "scalar")
-        nc.scalar.copy(out=dx7[:, halves[0]], in_=half_bank(6, 7, 0)[:])
-        scatter(5, HALF, dx5[1][:], "vector")
-        nc.sync.dma_start(out=trio[:, 1, :], in_=windows[5][:])
-        scatter(4, 768, dx4[:, thirds[2]], "scalar")
-        nc.sync.dma_start(out=trio[:, 0, :], in_=windows[4][:])
-        last_bank = half_bank(7, 7, 1)
+        for h in range(2):
+            nc.vector.tensor_copy(out=dx5[:, halves[h]], in_=half_bank(4 * h, 5, h)[:])
+        nc.vector.tensor_copy(out=dx6[:, halves[0]], in_=half_bank(1, 6, 0)[:])
+        scatter(5, 0, dx5[:], "vector")
+        nc.scalar.copy(out=dx6[:, halves[1]], in_=half_bank(7, 6, 1)[:])
+        scatter(6, 0, dx6[:], "vector")
+        nc.scalar.copy(out=dx4[:, halves[0]], in_=half_bank(2, 4, 0)[:])
+        acc = half_bank(6, 4, 1)
+        nc.scalar.copy(out=dx4[:, HALF : 3 * C], in_=acc[:, 0:C])
+        scatter(4, thirds[0].start, dx4[:, thirds[0]], "scalar")
+        nc.scalar.copy(out=dx4[:, 3 * C : S], in_=acc[:, C:BANK])
+        scatter(4, thirds[1].start, dx4[:, thirds[1]], "scalar")
+        nc.scalar.copy(out=dx7[:, halves[0]], in_=half_bank(3, 7, 0)[:])
+        scatter(4, thirds[2].start, dx4[:, thirds[2]], "scalar")
+        last_bank = half_bank(5, 7, 1)
         nc.scalar.copy(out=dx7[:, HALF : 3 * C], in_=last_bank[:, 0:C])
-        nc.vector.tensor_copy(out=dx6[1][:], in_=half_bank(5, 6, 1)[:])
-        scatter(6, HALF, dx6[1][:], "vector")
-        nc.vector.tensor_copy(out=trio[:, 2, :], in_=windows[6][:])
+        for w in (5, 4):
+            nc.sync.dma_start(out=trio[:, w - PACK, :], in_=windows[w][:, 0:T])
+        nc.vector.tensor_copy(out=trio[:, 2, :], in_=windows[6][:, 0:T])
         dealt_rows = out_0[PASS:K].rearrange("(p d) t -> p d t", d=PACK)
-        for planes in (slice(0, 2), slice(2, 3)):
+        for planes in (slice(1, 2), slice(0, 3, 2)):
             nc.sync.dma_start(out=dealt_rows[:, planes, :], in_=trio[:, planes, :])
         scatter(7, 0, dx7[:, thirds[0]], "scalar")
         scatter(7, 384, dx7[:, thirds[1]], "scalar")
@@ -352,20 +367,13 @@ def tile_moe_sdb_relu_kernel(
 
         y0 = [placed([P, HALF, PACK], BF16, f"y0{h}", (48 + 4 * h) * KIB) for h in range(2)]
         for h in range(2):
-            nc.gpsimd.tensor_scalar(
-                out=y0[h][:],
-                in0=quad[:, :, halves[h]].rearrange("p d t -> p t d"),
-                scalar1=1.0,
-                scalar2=-0.0,
-                op0=ALU.mult,
-                op1=ALU.add,
-            )
+            weave_on_gpsimd(y0[h][:], quad[:, :, halves[h]])
         for h in range(2):
             quantize_y(0, y0[h], h * HALF, (h + 1) * HALF)
         store_words(0, slice(0, T))
 
         spans = [(0, T // 2), (T // 2, 3 * T // 4), (3 * T // 4, T)]
-        y1 = [placed([P, hi - lo, PACK], BF16, f"y1{lo}", 50 * KIB + 2 * PACK * lo) for lo, hi in spans]
+        y1 = [placed([P, hi - lo, PACK], BF16, f"y1{lo}", at * KIB) for (lo, hi), at in zip(spans, (48, 52, 40))]
         engines = ("vector", "vector", "scalar")
         for woven, (lo, hi), engine in zip(y1, spans, engines):
             copy(engine, woven_by_runs(woven[:, :, 0 : PACK - 1]), by_runs(trio[:, :, lo:hi]))

@@ -25,8 +25,6 @@ HALF = S // 2
 PASS = P * PACK
 RUN = 2
 KIB = 1024
-LAP = 64
-WIDE = 1376
 
 
 def load_scale_rows(nc, plane, rows):
@@ -67,17 +65,18 @@ def tile_moe_sdb_relu_kernel(
         dy_s = held([P, T], U8, "dy_s")
         w1_first_s = held([P, E, PASS], U8, "w1_first_s")
         w1_first = [held([P, 2, 2 * PASS], U8, f"w1_first{i}") for i in range(2)]
-        packed_raw = held([P, PASS], U8, "packed_raw")
+        w1_raw_s = held([P, E, PASS], U8, "w1_raw_s")
         w1_raw = held([P, E, 2 * PASS], U8, "w1_raw")
         row_sets = [(0, 1), (1, 1), (2, 2)]
         a_first = [held([P, count, HALF], F32, f"a_first{t}") for t, count in row_sets]
         a_sb = {e: held([P, PACK, C], F32, f"a{e}") for e in (2, 3)}
         gate_sb = [held([P, HALF], F32, f"gate{h}") for h in range(2)]
 
-        nc.gpsimd.memset(packed_raw[:].bitcast(I32), 0)
+        nc.gpsimd.memset(w1_raw_s[:].rearrange("p e k -> p (e k)").bitcast(I32), 0)
 
         a_rows = a.rearrange("(p t) j -> p t j", t=PACK)
         w1_rows = w1t_words.rearrange("e s p c -> (s p) e c")
+        w1_scale_rows = w1t_scales.rearrange("e s b k -> (s b) e k")
 
         def load_a(e):
             nc.sync.dma_start(out=a_sb[e][:], in_=a_rows[:, :, e * C : (e + 1) * C])
@@ -98,18 +97,14 @@ def tile_moe_sdb_relu_kernel(
         for rows, (t, count) in zip(a_first, row_sets):
             nc.sync.dma_start(out=rows[:], in_=a_rows[:, t : t + count, 0:HALF])
         nc.sync.dma_start(offsets[:], offs)
-        load_scale_rows(nc, w1_first_s, w1t_scales.rearrange("e s b k -> (s b) e k")[:, :, 0:PASS])
+        load_scale_rows(nc, w1_first_s, w1_scale_rows[:, :, 0:PASS])
         nc.sync.dma_start(out=gate_sb[1][:], in_=gate[:, HALF:S])
         load_a(2)
         load_w1_first(0)
         load_a(3)
         load_w1_first(1)
-        for q in range(QUADRANTS):
-            nc.sync.dma_start(
-                out=packed_raw[32 * q : 32 * q + 4 * E].bitcast(I32),
-                in_=w1t_scales[:, 0, 4 * q : 4 * q + 4, PASS:K].bitcast(I32),
-            )
         nc.sync.dma_start(out=w1_raw[:].bitcast(I32), in_=w1_rows[:, :, 2 * PASS : 2 * K].bitcast(I32))
+        load_scale_rows(nc, w1_raw_s, w1_scale_rows[:, :, PASS:K])
 
         nc.vector.tensor_copy(
             out=w2_codes[:].rearrange("p (t m) -> p m t", t=PACK), in_=w2_raw[:].rearrange("p (m t) -> p m t", t=PACK)
@@ -126,39 +121,41 @@ def tile_moe_sdb_relu_kernel(
                 out=out, lhsT=codes, lhsT_scale=scales, rhs=moving, rhs_scale=moving_scales, start=True, stop=True
             )
 
+        def of(e):
+            return slice(e * C, (e + 1) * C)
+
         dc = [held([P, T], F32, f"dc{t}") for t in range(PACK)]
-        factor, da, da_bf, da_codes, da_s = {}, {}, {}, {}, {}
+        first_factors = held([P, PACK, HALF], F32, "first_factors")
+        dx01 = held([P, 2, S], F32, "dx01")
+        dx23 = held([P, 2, S], F32, "dx23")
+        da = [
+            placed([P, PACK, C], F32, "da0", 16 * KIB),
+            held([P, PACK, C], F32, "da1"),
+            held([P, PACK, C], F32, "da2"),
+            placed([P, PACK, C], F32, "da3", 12 * KIB),
+        ]
+        da_bf, da_codes, da_s = {}, {}, {}
 
         def mask_times_gate(out, rows, weights):
             nc.vector.scalar_tensor_tensor(
                 out=out,
-                in0=rows[:],
+                in0=rows,
                 scalar=0.0,
                 in1=weights.unsqueeze(1).to_broadcast(rows.shape),
                 op0=ALU.is_gt,
                 op1=ALU.mult,
             )
 
-        def make_first_factors():
-            both = held([P, PACK, HALF], F32, "first_factors")
-            for rows, (t, count) in zip(a_first, row_sets):
-                mask_times_gate(both[:, t : t + count, :], rows, gate_sb[0][:])
-            for e in range(2):
-                factor.setdefault(e, both[:, :, e * C : (e + 1) * C])
+        def late_factor(e, t, out):
+            rows = a_sb[e][:, t : t + out.shape[1], :]
+            mask_times_gate(out, rows, gate_sb[1][:, of(e - 2)])
 
-        def make_factor(e):
-            tile = placed([P, PACK, C], F32, f"factor{e}", (12, 76)[e - 2] * KIB)
-            mask_times_gate(tile[:], a_sb[e], gate_sb[1][:, (e - 2) * C : (e - 1) * C])
-            factor.setdefault(e, tile[:])
-
-        def gather(e, engine):
-            da[e] = placed([P, PACK, C], F32, f"da{e}", (12, 72, 76, 80)[e] * KIB)
-            for t in range(PACK):
-                picked = dc[t][:].indirect(slots(e * C, C))
-                if engine == "vector":
-                    nc.vector.tensor_tensor(da[e][:, t, :], picked, factor[e][:, t, :], ALU.mult)
-                else:
-                    nc.scalar.activation(da[e][:, t, :], picked, COPY)
+        def gather(e, t, factor):
+            picked = dc[t][:].indirect(slots(e * C, C))
+            if factor is None:
+                nc.scalar.activation(da[e][:, t, :], picked, COPY)
+            else:
+                nc.vector.tensor_tensor(da[e][:, t, :], picked, factor, ALU.mult)
 
         def by_runs(rows):
             return rows.rearrange("p t (c i) -> p c t i", i=RUN)
@@ -166,20 +163,13 @@ def tile_moe_sdb_relu_kernel(
         def woven_by_runs(woven):
             return woven.rearrange("p (c i) t -> p c t i", i=RUN)
 
-        def weave_on_gpsimd(woven, rows):
-            nc.gpsimd.tensor_scalar(
-                out=woven, in0=rows.rearrange("p d t -> p t d"), scalar1=1.0, scalar2=-0.0, op0=ALU.mult, op1=ALU.add
-            )
-
-        def round_da(e, times_factor):
-            da_bf[e] = placed([P, C, PACK], BF16, f"da_bf{e}", (88, 88, 83, 86)[e] * KIB)
+        def round_da(e, factor=None):
+            da_bf[e] = placed([P, C, PACK], BF16, f"da_bf{e}", (28, 28, 20, 32)[e] * KIB)
             woven = woven_by_runs(da_bf[e][:])
-            if e >= 2:
-                weave_on_gpsimd(da_bf[e][:], da[e][:])
-            elif times_factor:
-                nc.vector.tensor_tensor(woven, by_runs(da[e][:]), by_runs(factor[e]), ALU.mult)
-            else:
+            if factor is None:
                 nc.vector.tensor_copy(out=woven, in_=by_runs(da[e][:]))
+            else:
+                nc.vector.tensor_tensor(woven, by_runs(da[e][:]), by_runs(factor), ALU.mult)
 
         def quantize_da(e):
             da_codes[e] = held([P, C], I32, f"da_codes{e}")
@@ -188,29 +178,32 @@ def tile_moe_sdb_relu_kernel(
                 out=da_codes[e][:].bitcast(FP8X4), scales=da_s[e][:], in_=da_bf[e][:].rearrange("p j t -> p (j t)")
             )
 
-        def second_product(out, w, e):
-            s, j = divmod(w, PACK)
-            if s == 0:
-                codes, scales = w1_first[e // 2][:, e % 2, :], w1_first_s[:, e, :]
-            else:
-                codes, scales = dealt[:, e, :], (packed[:] if e == 0 else w1_s[:, e - 1, :])
-            mx(
-                out,
-                codes[:, 2 * j * P : 2 * (j + 1) * P].bitcast(FP4X4),
-                scales[:, j * P : (j + 1) * P],
-                da_codes[e][:].bitcast(FP8X4),
-                da_s[e][:],
-            )
-
         def fill_bank(b, parts):
             acc = bank(b)
             for u, (w, e) in enumerate(parts):
-                second_product(acc[:, u * C : (u + 1) * C], w, e)
+                s, j = divmod(w, PACK)
+                if s == 0:
+                    codes, scales = w1_first[e // 2][:, e % 2, :], w1_first_s[:, e, :]
+                else:
+                    codes, scales = dealt[:, e, :], dealt_s[:, e, :]
+                mx(
+                    acc[:, of(u)],
+                    codes[:, 2 * j * P : 2 * (j + 1) * P].bitcast(FP4X4),
+                    scales[:, j * P : (j + 1) * P],
+                    da_codes[e][:].bitcast(FP8X4),
+                    da_s[e][:],
+                )
             return acc
 
-        def two_windows(b, e, w, out, engine):
-            acc = fill_bank(b, [(w, e), (w + 1, e)])
-            copy(engine, out, acc[:].rearrange("p (u j) -> p u j", u=2))
+        def pair_bank(e, i):
+            return fill_bank(2 * e + i, [(2 * i, e), (2 * i + 1, e)])
+
+        def empty_pair(engine, acc, out, order=None):
+            if order is None:
+                copy(engine, out, acc[:].rearrange("p (u j) -> p u j", u=2))
+            else:
+                for u in order:
+                    copy(engine, out[:, u, :], acc[:, of(u)])
 
         windows = {}
 
@@ -221,10 +214,8 @@ def tile_moe_sdb_relu_kernel(
             else:
                 nc.scalar.activation(target, source, COPY)
 
-        def store_window(w):
-            nc.sync.dma_start(out=out_0[w * P : (w + 1) * P], in_=windows[w][:])
-
-        make_first_factors()
+        for rows, (t, count) in zip(a_first, row_sets):
+            mask_times_gate(first_factors[:, t : t + count, :], rows[:], gate_sb[0][:])
         for t in range(PACK):
             for h in range(2):
                 cols = slice(h * BANK, (h + 1) * BANK)
@@ -237,118 +228,124 @@ def tile_moe_sdb_relu_kernel(
                     dy_s[:, cols],
                 )
                 nc.scalar.copy(out=dc[t][:, cols], in_=acc[:])
-        gather(0, "vector")
-        round_da(0, False)
+        for t in range(PACK):
+            gather(0, t, first_factors[:, t, of(0)])
+        for t in range(PACK):
+            gather(1, t, None)
+        late_factor(2, 0, first_factors[:, 2:3, of(0)])
+        round_da(0)
+        late_factor(2, 1, first_factors[:, 3:4, of(0)])
         quantize_da(0)
-        gather(1, "scalar")
-        make_factor(2)
-        round_da(1, True)
+        factor2 = placed([P, 2, C], F32, "factor2", 16 * KIB)
+        late_factor(2, 2, factor2[:])
+        round_da(1, first_factors[:, :, of(1)])
+        gather(2, 0, first_factors[:, 2, of(0)])
         quantize_da(1)
-        gather(2, "vector")
+        gather(2, 1, first_factors[:, 3, of(0)])
+        for t in (2, 3):
+            gather(2, t, factor2[:, t - 2, :])
+        late_factor(3, 0, dx23[:, :, of(1)])
+        round_da(2)
+        late_factor(3, 2, dx23[:, :, of(2)])
+        quantize_da(2)
+        for t in range(PACK):
+            gather(3, t, dx23[:, t % 2, of(1 + t // 2)])
 
-        packed = placed([P, PASS], U8, "packed", 72 * KIB)
-        w1_s = held([P, E - 1, PASS], U8, "w1_s")
-        nc.vector.tensor_copy(
-            out=packed[:].rearrange("p (d m) -> p d m", d=PACK), in_=packed_raw[:].rearrange("p (m d) -> p d m", d=PACK)
-        )
-        for e in range(1, E):
-            for q in range(QUADRANTS):
-                nc.sync.dma_start(
-                    out=w1_s[32 * q : 32 * q + 4, e - 1, :].bitcast(I32),
-                    in_=packed[32 * q + 4 * e : 32 * q + 4 * e + 4].bitcast(I32),
-                )
-
-        dx01 = placed([P, 2, S], F32, "dx01", 24 * KIB)
-        early = held([P, 2, HALF], F32, "early")
-        late = {e: placed([P, 2, C], F32, f"late{e}", (52 + 4 * e) * KIB) for e in (2, 3)}
+        accs = {(e, i): pair_bank(e, i) for e in range(3) for i in range(2)}
+        empty_pair("vector", accs[1, 1], dx23[:, :, of(1)])
+        round_da(3)
+        empty_pair("vector", accs[2, 1], dx23[:, :, of(2)])
+        quantize_da(3)
         for w in range(PACK):
             windows[w] = placed([P, T], F32, f"window{w}", 4 * w * KIB)
 
-        def first_two_windows(e):
-            cols = slice(e * C, (e + 1) * C)
-            for w in range(2):
-                scatter(w, e * C, dx01[:, w, cols], "scalar")
+        dealt_s = placed([P, E, PASS], U8, "dealt_s", 31 * KIB)
+        dealt = placed([P, E, 2 * PASS], U8, "dealt", 33 * KIB)
+        for i in range(2):
+            pair = slice(2 * i, 2 * i + 2)
+            nc.gpsimd.tensor_copy(
+                out=dealt_s[:, pair, :].rearrange("p e (d m) -> p e d m", d=PACK),
+                in_=w1_raw_s[:, pair, :].rearrange("p e (m d) -> p e d m", d=PACK),
+            )
+            nc.gpsimd.tensor_copy(
+                out=dealt[:, pair, :].rearrange("p e (d m b) -> p e d m b", d=PACK, b=2),
+                in_=w1_raw[:, pair, :].rearrange("p e (m d b) -> p e d m b", d=PACK, b=2),
+            )
 
-        for e in range(2):
-            cols = slice(e * C, (e + 1) * C)
-            two_windows(2 * e, e, 0, dx01[:, :, cols], "scalar")
-            two_windows(2 * e + 1, e, 2, early[:, :, cols], "vector" if e else "scalar")
-        for e in range(2):
+        def first_two_windows(e):
+            for w in range(2):
+                scatter(w, e * C, dx01[:, w, of(e)], "scalar")
+
+        empty_pair("scalar", accs[0, 0], dx01[:, :, of(0)])
+        empty_pair("scalar", accs[0, 1], dx23[:, :, of(0)])
+        first_two_windows(0)
+        scatter(2, 0, dx23[:, 0, of(0)], "scalar")
+        for e in (1, 2):
+            empty_pair("scalar", accs[e, 0], dx01[:, :, of(e)], order=(0, 1))
             first_two_windows(e)
-            scatter(2, e * C, early[:, 0, e * C : (e + 1) * C], "scalar")
-        round_da(2, False)
-        scatter(3, 0, early[:, 1, :], "vector")
-        quantize_da(2)
-        make_factor(3)
-        gather(3, "vector")
-        two_windows(4, 2, 0, dx01[:, :, 2 * C : 3 * C], "scalar")
-        two_windows(5, 2, 2, late[2][:], "vector")
-        round_da(3, False)
-        scatter(3, 2 * C, late[2][:, 1, :], "vector")
-        quantize_da(3)
-        dealt = placed([P, E, 2 * PASS], U8, "dealt", 81 * KIB)
-        nc.vector.tensor_copy(
-            out=dealt[:].bitcast(U16).rearrange("p e (d m) -> p e d m", d=PACK),
-            in_=w1_raw[:].bitcast(U16).rearrange("p e (m d) -> p e d m", d=PACK),
-        )
-        scatter(2, 2 * C, late[2][:, 0, :], "scalar")
-        first_two_windows(2)
-        acc = fill_bank(6, [(2, 3), (3, 3)])
-        for u in (1, 0):
-            nc.vector.tensor_copy(out=late[3][:, u, :], in_=acc[:, u * C : (u + 1) * C])
-        two_windows(7, 3, 0, dx01[:, :, 3 * C : S], "scalar")
+        shared = 640
+        scatter(2, C, dx23[:, 0, C:shared], "scalar")
+        scatter(3, 0, dx23[:, 1, 0 : 3 * C], "vector")
+        empty_pair("vector", pair_bank(3, 1), dx23[:, :, of(3)], order=(1, 0))
+        empty_pair("scalar", pair_bank(3, 0), dx01[:, :, of(3)], order=(0, 1))
         first_two_windows(3)
-        for w in (3, 2):
-            scatter(w, 3 * C, late[3][:, w - 2, :], "vector")
-        for w in (3, 2, 0, 1):
-            store_window(w)
-        halves = [slice(0, HALF), slice(HALF, T)]
-        quad = held([P, PACK, T], F32, "quad")
+        scatter(3, 3 * C, dx23[:, 1, of(3)], "vector")
+        scatter(2, shared, dx23[:, 0, shared:S], "vector")
+        for w in (3, 0, 2, 1):
+            nc.sync.dma_start(out=out_0[w * P : (w + 1) * P], in_=windows[w][:])
+        quarters = [slice(q * C, (q + 1) * C) for q in range(PACK)]
+        quad = [placed([P, PACK, C], F32, f"quad{q}", (40, 52, 44, 68)[q] * KIB) for q in range(PACK)]
         back = out_0[0:PASS].rearrange("(p d) t -> p d t", d=PACK)
-        for cols in halves:
-            nc.sync.dma_start(out=quad[:, :, cols], in_=back[:, :, cols])
+        for q in range(PACK):
+            nc.sync.dma_start(out=quad[q][:], in_=back[:, :, quarters[q]])
+        y0 = placed([P, T, PACK], BF16, "y0", 60 * KIB)
+        for q in range(PACK):
+            nc.gpsimd.tensor_scalar(
+                out=y0[:, quarters[q], :],
+                in0=quad[q][:].rearrange("p d t -> p t d"),
+                scalar1=1.0,
+                scalar2=-0.0,
+                op0=ALU.mult,
+                op1=ALU.add,
+            )
+
+        halves = [slice(0, HALF), slice(HALF, T)]
+        thirds = [slice(0, 384), slice(384, 768), slice(768, S)]
+        dx = {w: held([P, S], F32, f"dx{w}") for w in (4, 5, 6)}
+        dx7 = held([P, 3 * C], F32, "dx7")
+        for w in (4, 5, 6):
+            windows[w] = placed([P, T], F32, f"window{w}", (60 + 4 * w) * KIB)
+        windows.setdefault(7, placed([P, T], F32, "window7", 49 * KIB))
+        trio = placed([P, PACK - 1, T], F32, "trio", 2 * KIB)
 
         def half_bank(b, w, h):
             return fill_bank(b, [(w, 2 * h), (w, 2 * h + 1)])
 
-        dx4 = placed([P, S], F32, "dx4", 20 * KIB + LAP)
-        dx6 = placed([P, S], F32, "dx6", 65 * KIB)
-        dx5 = placed([P, S], F32, "dx5", 61 * KIB)
-        dx7 = placed([P, 3 * C], F32, "dx7", 32 * KIB - LAP)
-        windows.setdefault(4, placed([P, T], F32, "window4", 40 * KIB))
-        windows.setdefault(5, placed([P, WIDE], F32, "window5", 92 * KIB))
-        windows.setdefault(6, placed([P, WIDE], F32, "window6", 57 * KIB))
-        windows.setdefault(7, placed([P, T], F32, "window7", 33 * KIB // 2))
-        trio = placed([P, PACK - 1, T], F32, "trio", 2 * KIB)
-        thirds = [slice(0, 384), slice(384, 768), slice(768, S)]
-
-        for h in range(2):
-            nc.vector.tensor_copy(out=dx5[:, halves[h]], in_=half_bank(4 * h, 5, h)[:])
-        nc.vector.tensor_copy(out=dx6[:, halves[0]], in_=half_bank(1, 6, 0)[:])
-        scatter(5, 0, dx5[:], "vector")
-        nc.scalar.copy(out=dx6[:, halves[1]], in_=half_bank(7, 6, 1)[:])
-        scatter(6, 0, dx6[:], "vector")
-        nc.scalar.copy(out=dx4[:, halves[0]], in_=half_bank(2, 4, 0)[:])
-        acc = half_bank(6, 4, 1)
-        nc.scalar.copy(out=dx4[:, HALF : 3 * C], in_=acc[:, 0:C])
-        scatter(4, thirds[0].start, dx4[:, thirds[0]], "scalar")
-        nc.scalar.copy(out=dx4[:, 3 * C : S], in_=acc[:, C:BANK])
-        scatter(4, thirds[1].start, dx4[:, thirds[1]], "scalar")
+        nc.vector.tensor_copy(out=dx[5][:, halves[0]], in_=half_bank(0, 5, 0)[:])
+        nc.scalar.copy(out=dx[6][:, halves[0]], in_=half_bank(1, 6, 0)[:])
+        nc.scalar.copy(out=dx[4][:, halves[0]], in_=half_bank(2, 4, 0)[:])
         nc.scalar.copy(out=dx7[:, halves[0]], in_=half_bank(3, 7, 0)[:])
-        scatter(4, thirds[2].start, dx4[:, thirds[2]], "scalar")
-        last_bank = half_bank(5, 7, 1)
+        scatter(4, thirds[0].start, dx[4][:, thirds[0]], "scalar")
+        for b, w in ((4, 4), (5, 5), (6, 6)):
+            nc.scalar.copy(out=dx[w][:, halves[1]], in_=half_bank(b, w, 1)[:])
+        last_bank = half_bank(7, 7, 1)
+        scatter(4, thirds[1].start, dx[4][:, thirds[1]], "scalar")
         nc.scalar.copy(out=dx7[:, HALF : 3 * C], in_=last_bank[:, 0:C])
-        for w in (5, 4):
-            nc.sync.dma_start(out=trio[:, w - PACK, :], in_=windows[w][:, 0:T])
-        nc.vector.tensor_copy(out=trio[:, 2, :], in_=windows[6][:, 0:T])
+        scatter(4, thirds[2].start, dx[4][:, thirds[2]], "scalar")
+        for h in range(2):
+            for w in (5, 6):
+                scatter(w, h * HALF, dx[w][:, halves[h]], "vector")
+        for w in (4, 5):
+            nc.sync.dma_start(out=trio[:, w - PACK, :], in_=windows[w][:])
+        nc.vector.tensor_copy(out=trio[:, 2, :], in_=windows[6][:])
         dealt_rows = out_0[PASS:K].rearrange("(p d) t -> p d t", d=PACK)
-        for planes in (slice(1, 2), slice(0, 3, 2)):
+        for planes in (slice(0, 1), slice(1, 3)):
             nc.sync.dma_start(out=dealt_rows[:, planes, :], in_=trio[:, planes, :])
-        scatter(7, 0, dx7[:, thirds[0]], "scalar")
-        scatter(7, 384, dx7[:, thirds[1]], "scalar")
-        dx_last = placed([P, C], F32, "dx_last", 40 * KIB)
+        scatter(7, thirds[0].start, dx7[:, thirds[0]], "scalar")
+        scatter(7, thirds[1].start, dx7[:, thirds[1]], "scalar")
+        dx_last = placed([P, C], F32, "dx_last", 159 * KIB // 2)
         nc.scalar.copy(out=dx_last[:], in_=last_bank[:, C:BANK])
-        scatter(7, 768, dx_last[:], "scalar")
+        scatter(7, thirds[2].start, dx_last[:], "scalar")
         nc.sync.dma_start(out=dealt_rows[:, PACK - 1, :], in_=windows[7][:])
 
         y_codes = [held([P, T], I32, f"y_codes{s}") for s in range(2)]
@@ -365,15 +362,11 @@ def tile_moe_sdb_relu_kernel(
             words = out_1[s].rearrange("p t d -> p (t d)").bitcast(I32)
             nc.sync.dma_start(out=words[:, cols], in_=y_codes[s][:, cols])
 
-        y0 = [placed([P, HALF, PACK], BF16, f"y0{h}", (48 + 4 * h) * KIB) for h in range(2)]
-        for h in range(2):
-            weave_on_gpsimd(y0[h][:], quad[:, :, halves[h]])
-        for h in range(2):
-            quantize_y(0, y0[h], h * HALF, (h + 1) * HALF)
+        quantize_y(0, y0, 0, T)
         store_words(0, slice(0, T))
 
         spans = [(0, T // 2), (T // 2, 3 * T // 4), (3 * T // 4, T)]
-        y1 = [placed([P, hi - lo, PACK], BF16, f"y1{lo}", at * KIB) for (lo, hi), at in zip(spans, (48, 52, 40))]
+        y1 = [placed([P, hi - lo, PACK], BF16, f"y1{lo}", at * KIB) for (lo, hi), at in zip(spans, (60, 64, 66))]
         engines = ("vector", "vector", "scalar")
         for woven, (lo, hi), engine in zip(y1, spans, engines):
             copy(engine, woven_by_runs(woven[:, :, 0 : PACK - 1]), by_runs(trio[:, :, lo:hi]))

@@ -251,7 +251,8 @@ def tile_moe_sdb_relu_kernel(
         for t in range(PACK):
             gather(3, t, dx23[:, t % 2, of(1 + t // 2)])
 
-        accs = {(e, i): pair_bank(e, i) for e in range(3) for i in range(2)}
+        alone = [fill_bank(b, [(w, 0)]) for w, b in enumerate((7, 0))]
+        accs = {(e, i): pair_bank(e, i) for e in range(3) for i in range(2) if e or i}
         empty_pair("vector", accs[1, 1], dx23[:, :, of(1)])
         round_da(3)
         empty_pair("vector", accs[2, 1], dx23[:, :, of(2)])
@@ -276,9 +277,11 @@ def tile_moe_sdb_relu_kernel(
             for w in range(2):
                 scatter(w, e * C, dx01[:, w, of(e)], "scalar")
 
-        empty_pair("scalar", accs[0, 0], dx01[:, :, of(0)])
+        for w in range(2):
+            nc.scalar.copy(out=dx01[:, w, of(0)], in_=alone[w][:, 0:C])
+        scatter(0, 0, dx01[:, 0, of(0)], "scalar")
         empty_pair("scalar", accs[0, 1], dx23[:, :, of(0)])
-        first_two_windows(0)
+        scatter(1, 0, dx01[:, 1, of(0)], "scalar")
         scatter(2, 0, dx23[:, 0, of(0)], "scalar")
         for e in (1, 2):
             empty_pair("scalar", accs[e, 0], dx01[:, :, of(e)], order=(0, 1))
@@ -294,15 +297,17 @@ def tile_moe_sdb_relu_kernel(
         for w in (3, 0, 2, 1):
             nc.sync.dma_start(out=out_0[w * P : (w + 1) * P], in_=windows[w][:])
         quarters = [slice(q * C, (q + 1) * C) for q in range(PACK)]
-        quad = [placed([P, PACK, C], F32, f"quad{q}", (40, 52, 44, 68)[q] * KIB) for q in range(PACK)]
+        second_half = placed([P, 2, PACK, C], F32, "second_half", 60 * KIB)
+        quad = [placed([P, PACK, C], F32, f"quad{q}", (52, 40)[q] * KIB)[:] for q in range(2)]
+        quad.extend(second_half[:, u] for u in range(2))
         back = out_0[0:PASS].rearrange("(p d) t -> p d t", d=PACK)
         for q in range(PACK):
-            nc.sync.dma_start(out=quad[q][:], in_=back[:, :, quarters[q]])
-        y0 = placed([P, T, PACK], BF16, "y0", 60 * KIB)
+            nc.sync.dma_start(out=quad[q], in_=back[:, :, quarters[q]])
+        y0 = held([P, T, PACK], BF16, "y0")
         for q in range(PACK):
             nc.gpsimd.tensor_scalar(
                 out=y0[:, quarters[q], :],
-                in0=quad[q][:].rearrange("p d t -> p t d"),
+                in0=quad[q].rearrange("p d t -> p t d"),
                 scalar1=1.0,
                 scalar2=-0.0,
                 op0=ALU.mult,
@@ -314,27 +319,28 @@ def tile_moe_sdb_relu_kernel(
         dx = {w: held([P, S], F32, f"dx{w}") for w in (4, 5, 6)}
         dx7 = held([P, 3 * C], F32, "dx7")
         for w in (4, 5, 6):
-            windows[w] = placed([P, T], F32, f"window{w}", (60 + 4 * w) * KIB)
+            windows[w] = placed([P, T], F32, f"window{w}", (76, 68, 80)[w - PACK] * KIB)
         windows.setdefault(7, placed([P, T], F32, "window7", 49 * KIB))
         trio = placed([P, PACK - 1, T], F32, "trio", 2 * KIB)
 
         def half_bank(b, w, h):
             return fill_bank(b, [(w, 2 * h), (w, 2 * h + 1)])
 
-        nc.vector.tensor_copy(out=dx[5][:, halves[0]], in_=half_bank(0, 5, 0)[:])
-        nc.scalar.copy(out=dx[6][:, halves[0]], in_=half_bank(1, 6, 0)[:])
+        for b, w, engine in ((0, 5, "vector"), (1, 6, "scalar")):
+            copy(engine, dx[w][:, halves[0]], half_bank(b, w, 0)[:])
+        for w in (5, 6):
+            scatter(w, 0, dx[w][:, halves[0]], "vector")
         nc.scalar.copy(out=dx[4][:, halves[0]], in_=half_bank(2, 4, 0)[:])
         nc.scalar.copy(out=dx7[:, halves[0]], in_=half_bank(3, 7, 0)[:])
         scatter(4, thirds[0].start, dx[4][:, thirds[0]], "scalar")
         for b, w in ((4, 4), (5, 5), (6, 6)):
             nc.scalar.copy(out=dx[w][:, halves[1]], in_=half_bank(b, w, 1)[:])
-        last_bank = half_bank(7, 7, 1)
         scatter(4, thirds[1].start, dx[4][:, thirds[1]], "scalar")
+        last_bank = half_bank(7, 7, 1)
         nc.scalar.copy(out=dx7[:, HALF : 3 * C], in_=last_bank[:, 0:C])
         scatter(4, thirds[2].start, dx[4][:, thirds[2]], "scalar")
-        for h in range(2):
-            for w in (5, 6):
-                scatter(w, h * HALF, dx[w][:, halves[h]], "vector")
+        for w in (5, 6):
+            scatter(w, HALF, dx[w][:, halves[1]], "vector")
         for w in (4, 5):
             nc.sync.dma_start(out=trio[:, w - PACK, :], in_=windows[w][:])
         nc.vector.tensor_copy(out=trio[:, 2, :], in_=windows[6][:])
@@ -343,39 +349,42 @@ def tile_moe_sdb_relu_kernel(
             nc.sync.dma_start(out=dealt_rows[:, planes, :], in_=trio[:, planes, :])
         scatter(7, thirds[0].start, dx7[:, thirds[0]], "scalar")
         scatter(7, thirds[1].start, dx7[:, thirds[1]], "scalar")
-        dx_last = placed([P, C], F32, "dx_last", 159 * KIB // 2)
+        dx_last = placed([P, C], F32, "dx_last", 68 * KIB)
         nc.scalar.copy(out=dx_last[:], in_=last_bank[:, C:BANK])
         scatter(7, thirds[2].start, dx_last[:], "scalar")
         nc.sync.dma_start(out=dealt_rows[:, PACK - 1, :], in_=windows[7][:])
 
-        y_codes = [held([P, T], I32, f"y_codes{s}") for s in range(2)]
         y_s = held([P, 2, T], U8, "y_s")
 
-        def quantize_y(s, woven, lo, hi):
+        def quantize_y(s, codes, woven, lo, hi):
             nc.vector.quantize_mx(
-                out=y_codes[s][:, lo:hi].bitcast(FP8X4),
+                out=codes.bitcast(FP8X4),
                 scales=y_s[:, s, lo:hi],
                 in_=woven[:].rearrange("p t d -> p (t d)"),
             )
 
-        def store_words(s, cols):
+        def store_words(s, codes, lo, hi):
             words = out_1[s].rearrange("p t d -> p (t d)").bitcast(I32)
-            nc.sync.dma_start(out=words[:, cols], in_=y_codes[s][:, cols])
+            nc.sync.dma_start(out=words[:, lo:hi], in_=codes[:])
 
-        quantize_y(0, y0, 0, T)
-        store_words(0, slice(0, T))
+        y0_codes = held([P, T], I32, "y0_codes")
+        quantize_y(0, y0_codes[:], y0, 0, T)
+        store_words(0, y0_codes, 0, T)
 
         spans = [(0, T // 2), (T // 2, 3 * T // 4), (3 * T // 4, T)]
-        y1 = [placed([P, hi - lo, PACK], BF16, f"y1{lo}", at * KIB) for (lo, hi), at in zip(spans, (60, 64, 66))]
+        y1 = [placed([P, hi - lo, PACK], BF16, f"y1{lo}", at * KIB) for (lo, hi), at in zip(spans, (60, 64, 67))]
         engines = ("vector", "vector", "scalar")
         for woven, (lo, hi), engine in zip(y1, spans, engines):
             copy(engine, woven_by_runs(woven[:, :, 0 : PACK - 1]), by_runs(trio[:, :, lo:hi]))
         for woven, (lo, hi), engine in zip(y1, spans, engines):
             copy(engine, woven[:, :, PACK - 1], windows[7][:, lo:hi])
-        for woven, (lo, hi) in zip(y1, spans):
-            quantize_y(1, woven, lo, hi)
-        for cols in halves:
-            store_words(1, cols)
+        y1_codes = held([P, 3 * C], I32, "y1_codes")
+        for woven, (lo, hi) in zip(y1[0:2], spans):
+            quantize_y(1, y1_codes[:, lo:hi], woven, lo, hi)
+        store_words(1, y1_codes, 0, 3 * C)
+        last_codes = placed([P, C], I32, "last_codes", 60 * KIB)
+        quantize_y(1, last_codes[:], y1[2], 3 * C, T)
+        store_words(1, last_codes, 3 * C, T)
         for q in range(QUADRANTS):
             (nc.scalar if q % 2 else nc.sync).dma_start(
                 out=out_2[:, 4 * q : 4 * q + 4, :].rearrange("s b t -> b s t").bitcast(I32),

@@ -37,6 +37,7 @@ def tile_moe_sdb_relu_kernel(
 ):
     nc = tc.nc
     with ExitStack() as ctx:
+        apart = ctx.enter_context(tc.tile_pool(name="apart", bufs=1))
         keep = ctx.enter_context(tc.tile_pool(name="keep", bufs=1))
         turns = ctx.enter_context(tc.tile_pool(name="turns", bufs=1))
         psum = ctx.enter_context(tc.psum_pool(name="psum", bufs=1))
@@ -49,6 +50,9 @@ def tile_moe_sdb_relu_kernel(
 
         def placed(shape, dtype, name, offset):
             return turns.tile(shape, dtype, name=name, offset=offset, align_bytes=64)
+
+        def for_scalar(shape, name, offset):
+            return apart.tile(shape, F32, name=name, offset=offset, align_bytes=64)
 
         def copy(engine, out, in_):
             if engine == "vector":
@@ -126,8 +130,8 @@ def tile_moe_sdb_relu_kernel(
 
         dc = [held([P, T], F32, f"dc{t}") for t in range(PACK)]
         first_factors = held([P, PACK, HALF], F32, "first_factors")
-        dx01 = held([P, 2, S], F32, "dx01")
-        dx23 = held([P, 2, S], F32, "dx23")
+        dx01 = for_scalar([P, 2, S], "dx01", 12 * KIB)
+        dx23 = placed([P, 2, S], F32, "dx23", 84 * KIB)
         da = [
             placed([P, PACK, C], F32, "da0", 16 * KIB),
             held([P, PACK, C], F32, "da1"),
@@ -258,7 +262,7 @@ def tile_moe_sdb_relu_kernel(
         empty_pair("vector", accs[2, 1], dx23[:, :, of(2)])
         quantize_da(3)
         for w in range(PACK):
-            windows[w] = placed([P, T], F32, f"window{w}", 4 * w * KIB)
+            windows[w] = (placed([P, T], F32, f"window{w}", 4 * w * KIB) if w > 1 else for_scalar([P, T], f"window{w}", 4 * w * KIB))
 
         dealt_s = placed([P, E, PASS], U8, "dealt_s", 31 * KIB)
         dealt = placed([P, E, 2 * PASS], U8, "dealt", 33 * KIB)
@@ -298,7 +302,7 @@ def tile_moe_sdb_relu_kernel(
             nc.sync.dma_start(out=out_0[w * P : (w + 1) * P], in_=windows[w][:])
         quarters = [slice(q * C, (q + 1) * C) for q in range(PACK)]
         second_half = placed([P, 2, PACK, C], F32, "second_half", 60 * KIB)
-        quad = [placed([P, PACK, C], F32, f"quad{q}", (52, 40)[q] * KIB)[:] for q in range(2)]
+        quad = [for_scalar([P, PACK, C], f"quad{q}", (20, 28)[q] * KIB)[:] for q in range(2)]
         quad.extend(second_half[:, u] for u in range(2))
         back = out_0[0:PASS].rearrange("(p d) t -> p d t", d=PACK)
         for q in range(PACK):
@@ -316,12 +320,14 @@ def tile_moe_sdb_relu_kernel(
 
         halves = [slice(0, HALF), slice(HALF, T)]
         thirds = [slice(0, 384), slice(384, 768), slice(768, S)]
-        dx = {w: held([P, S], F32, f"dx{w}") for w in (4, 5, 6)}
-        dx7 = held([P, 3 * C], F32, "dx7")
-        for w in (4, 5, 6):
-            windows[w] = placed([P, T], F32, f"window{w}", (76, 68, 80)[w - PACK] * KIB)
-        windows.setdefault(7, placed([P, T], F32, "window7", 49 * KIB))
-        trio = placed([P, PACK - 1, T], F32, "trio", 2 * KIB)
+        dx = {w: placed([P, S], F32, f"dx{w}", (72, 76)[w - 5] * KIB) for w in (5, 6)}
+        dx.setdefault(4, for_scalar([P, S], "dx4", 32 * KIB))
+        dx7 = for_scalar([P, 3 * C], "dx7", 36 * KIB)
+        for w in (5, 6):
+            windows[w] = placed([P, T], F32, f"window{w}", (68, 80)[w - 5] * KIB)
+        windows.setdefault(4, for_scalar([P, T], "window4", 40 * KIB))
+        windows.setdefault(7, for_scalar([P, T], "window7", 23 * KIB))
+        trio = for_scalar([P, PACK - 1, T], "trio", 0)
 
         def half_bank(b, w, h):
             return fill_bank(b, [(w, 2 * h), (w, 2 * h + 1)])

@@ -131,12 +131,12 @@ def tile_moe_sdb_relu_kernel(
         dc = [held([P, T], F32, f"dc{t}") for t in range(PACK)]
         first_factors = held([P, PACK, HALF], F32, "first_factors")
         dx01 = for_scalar([P, 2, S], "dx01", 12 * KIB)
-        dx23 = placed([P, 2, S], F32, "dx23", 84 * KIB)
+        dx23 = [placed([P, 2, C], F32, f"dx23_{e}", (84, 46)[e] * KIB) for e in range(2)]
         da = [
             placed([P, PACK, C], F32, "da0", 16 * KIB),
             held([P, PACK, C], F32, "da1"),
-            held([P, PACK, C], F32, "da2"),
-            placed([P, PACK, C], F32, "da3", 12 * KIB),
+            placed([P, PACK, C], F32, "da2", 44 * KIB),
+            placed([P, PACK, C], F32, "da3", 41 * KIB),
         ]
         da_bf, da_codes, da_s = {}, {}, {}
 
@@ -167,10 +167,17 @@ def tile_moe_sdb_relu_kernel(
         def woven_by_runs(woven):
             return woven.rearrange("p (c i) t -> p c t i", i=RUN)
 
+        def weave_on_gpsimd(woven, rows):
+            nc.gpsimd.tensor_scalar(
+                out=woven, in0=rows.rearrange("p d t -> p t d"), scalar1=1.0, scalar2=-0.0, op0=ALU.mult, op1=ALU.add
+            )
+
         def round_da(e, factor=None):
             da_bf[e] = placed([P, C, PACK], BF16, f"da_bf{e}", (28, 28, 20, 32)[e] * KIB)
             woven = woven_by_runs(da_bf[e][:])
-            if factor is None:
+            if e >= 2:
+                weave_on_gpsimd(da_bf[e][:], da[e][:])
+            elif factor is None:
                 nc.vector.tensor_copy(out=woven, in_=by_runs(da[e][:]))
             else:
                 nc.vector.tensor_tensor(woven, by_runs(da[e][:]), by_runs(factor), ALU.mult)
@@ -189,7 +196,7 @@ def tile_moe_sdb_relu_kernel(
                 if s == 0:
                     codes, scales = w1_first[e // 2][:, e % 2, :], w1_first_s[:, e, :]
                 else:
-                    codes, scales = dealt[:, e, :], dealt_s[:, e, :]
+                    codes, scales = dealt[:, e, :], dealt_s[e // 2][:, e % 2, :]
                 mx(
                     acc[:, of(u)],
                     codes[:, 2 * j * P : 2 * (j + 1) * P].bitcast(FP4X4),
@@ -246,59 +253,68 @@ def tile_moe_sdb_relu_kernel(
         gather(2, 0, first_factors[:, 2, of(0)])
         quantize_da(1)
         gather(2, 1, first_factors[:, 3, of(0)])
-        for t in (2, 3):
-            gather(2, t, factor2[:, t - 2, :])
-        late_factor(3, 0, dx23[:, :, of(1)])
-        round_da(2)
-        late_factor(3, 2, dx23[:, :, of(2)])
-        quantize_da(2)
-        for t in range(PACK):
-            gather(3, t, dx23[:, t % 2, of(1 + t // 2)])
+        factor3 = held([P, PACK, C], F32, "factor3")
+        for t in (0, 2):
+            late_factor(3, t, factor3[:, t : t + 2, :])
 
-        alone = [fill_bank(b, [(w, 0)]) for w, b in enumerate((7, 0))]
-        accs = {(e, i): pair_bank(e, i) for e in range(3) for i in range(2) if e or i}
-        empty_pair("vector", accs[1, 1], dx23[:, :, of(1)])
-        round_da(3)
-        empty_pair("vector", accs[2, 1], dx23[:, :, of(2)])
-        quantize_da(3)
         for w in range(PACK):
             windows[w] = (placed([P, T], F32, f"window{w}", 4 * w * KIB) if w > 1 else for_scalar([P, T], f"window{w}", 4 * w * KIB))
+        dealt_s = {}
 
-        dealt_s = placed([P, E, PASS], U8, "dealt_s", 31 * KIB)
-        dealt = placed([P, E, 2 * PASS], U8, "dealt", 33 * KIB)
-        for i in range(2):
-            pair = slice(2 * i, 2 * i + 2)
+        def deal_scales(i, offset):
+            dealt_s[i] = placed([P, 2, PASS], U8, f"dealt_s{i}", offset)
             nc.gpsimd.tensor_copy(
-                out=dealt_s[:, pair, :].rearrange("p e (d m) -> p e d m", d=PACK),
-                in_=w1_raw_s[:, pair, :].rearrange("p e (m d) -> p e d m", d=PACK),
+                out=dealt_s[i][:].rearrange("p e (d m) -> p e d m", d=PACK),
+                in_=w1_raw_s[:, 2 * i : 2 * i + 2, :].rearrange("p e (m d) -> p e d m", d=PACK),
             )
+
+        def deal_words(i):
+            pair = slice(2 * i, 2 * i + 2)
             nc.gpsimd.tensor_copy(
                 out=dealt[:, pair, :].rearrange("p e (d m b) -> p e d m b", d=PACK, b=2),
                 in_=w1_raw[:, pair, :].rearrange("p e (m d b) -> p e d m b", d=PACK, b=2),
             )
 
         def first_two_windows(e):
+            empty_pair("scalar", pair_bank(e, 0), dx01[:, :, of(e)], order=(0, 1))
             for w in range(2):
                 scatter(w, e * C, dx01[:, w, of(e)], "scalar")
 
+        alone = [fill_bank(b, [(w, 0)]) for w, b in enumerate((7, 0))]
         for w in range(2):
             nc.scalar.copy(out=dx01[:, w, of(0)], in_=alone[w][:, 0:C])
         scatter(0, 0, dx01[:, 0, of(0)], "scalar")
-        empty_pair("scalar", accs[0, 1], dx23[:, :, of(0)])
+        empty_pair("scalar", pair_bank(0, 1), dx23[0][:])
         scatter(1, 0, dx01[:, 1, of(0)], "scalar")
-        scatter(2, 0, dx23[:, 0, of(0)], "scalar")
-        for e in (1, 2):
-            empty_pair("scalar", accs[e, 0], dx01[:, :, of(e)], order=(0, 1))
-            first_two_windows(e)
-        shared = 640
-        scatter(2, C, dx23[:, 0, C:shared], "scalar")
-        scatter(3, 0, dx23[:, 1, 0 : 3 * C], "vector")
-        empty_pair("vector", pair_bank(3, 1), dx23[:, :, of(3)], order=(1, 0))
-        empty_pair("scalar", pair_bank(3, 0), dx01[:, :, of(3)], order=(0, 1))
+        scatter(2, 0, dx23[0][:, 0, :], "scalar")
+        first_two_windows(1)
+
+        for t in (2, 3):
+            gather(2, t, factor2[:, t - 2, :])
+        round_da(2)
+        scatter(3, 0, dx23[0][:, 1, :], "vector")
+        quantize_da(2)
+        for t in range(PACK - 1):
+            gather(3, t, factor3[:, t, :])
+        empty_pair("vector", pair_bank(1, 1), dx23[1][:])
+        gather(3, 3, factor3[:, 3, :])
+        scatter(2, C, dx23[1][:, 0, :], "scalar")
+        first_two_windows(2)
+        round_da(3)
+        scatter(3, C, dx23[1][:, 1, :], "vector")
+        quantize_da(3)
+        dealt = placed([P, E, 2 * PASS], U8, "dealt", 67 * KIB // 2)
+        for i in range(2):
+            deal_scales(i, (63 + 2 * i) * KIB // 2)
+            deal_words(i)
+        late23 = placed([P, 2, HALF], F32, "late23", 41 * KIB)
+        empty_pair("vector", pair_bank(2, 1), late23[:, :, of(0)], order=(1, 0))
+        scatter(3, HALF, late23[:, 1, of(0)], "vector")
         first_two_windows(3)
-        scatter(3, 3 * C, dx23[:, 1, of(3)], "vector")
-        scatter(2, shared, dx23[:, 0, shared:S], "vector")
-        for w in (3, 0, 2, 1):
+        empty_pair("vector", pair_bank(3, 1), late23[:, :, of(1)], order=(1, 0))
+        scatter(3, 3 * C, late23[:, 1, of(1)], "vector")
+        scatter(2, HALF, late23[:, 0, :], "vector")
+        for w in (3, 0, 1, 2):
             nc.sync.dma_start(out=out_0[w * P : (w + 1) * P], in_=windows[w][:])
         quarters = [slice(q * C, (q + 1) * C) for q in range(PACK)]
         second_half = placed([P, 2, PACK, C], F32, "second_half", 60 * KIB)
@@ -309,14 +325,7 @@ def tile_moe_sdb_relu_kernel(
             nc.sync.dma_start(out=quad[q], in_=back[:, :, quarters[q]])
         y0 = held([P, T, PACK], BF16, "y0")
         for q in range(PACK):
-            nc.gpsimd.tensor_scalar(
-                out=y0[:, quarters[q], :],
-                in0=quad[q].rearrange("p d t -> p t d"),
-                scalar1=1.0,
-                scalar2=-0.0,
-                op0=ALU.mult,
-                op1=ALU.add,
-            )
+            weave_on_gpsimd(y0[:, quarters[q], :], quad[q])
 
         halves = [slice(0, HALF), slice(HALF, T)]
         thirds = [slice(0, 384), slice(384, 768), slice(768, S)]
@@ -327,19 +336,22 @@ def tile_moe_sdb_relu_kernel(
             windows[w] = placed([P, T], F32, f"window{w}", (68, 80)[w - 5] * KIB)
         windows.setdefault(4, for_scalar([P, T], "window4", 40 * KIB))
         windows.setdefault(7, for_scalar([P, T], "window7", 23 * KIB))
-        trio = for_scalar([P, PACK - 1, T], "trio", 0)
+        trio = placed([P, PACK - 1, T], F32, "trio", 4 * KIB)
 
         def half_bank(b, w, h):
             return fill_bank(b, [(w, 2 * h), (w, 2 * h + 1)])
 
-        for b, w, engine in ((0, 5, "vector"), (1, 6, "scalar")):
+        for b, w, engine in ((0, 5, "scalar"), (1, 6, "scalar")):
             copy(engine, dx[w][:, halves[0]], half_bank(b, w, 0)[:])
         for w in (5, 6):
             scatter(w, 0, dx[w][:, halves[0]], "vector")
         nc.scalar.copy(out=dx[4][:, halves[0]], in_=half_bank(2, 4, 0)[:])
         nc.scalar.copy(out=dx7[:, halves[0]], in_=half_bank(3, 7, 0)[:])
         scatter(4, thirds[0].start, dx[4][:, thirds[0]], "scalar")
-        for b, w in ((4, 4), (5, 5), (6, 6)):
+        acc = half_bank(4, 4, 1)
+        nc.scalar.copy(out=dx[4][:, HALF : 3 * C], in_=acc[:, of(0)])
+        nc.vector.tensor_copy(out=dx[4][:, 3 * C : S], in_=acc[:, of(1)])
+        for b, w in ((5, 5), (6, 6)):
             nc.scalar.copy(out=dx[w][:, halves[1]], in_=half_bank(b, w, 1)[:])
         scatter(4, thirds[1].start, dx[4][:, thirds[1]], "scalar")
         last_bank = half_bank(7, 7, 1)

@@ -131,12 +131,12 @@ def tile_moe_sdb_relu_kernel(
         dc = [held([P, T], F32, f"dc{t}") for t in range(PACK)]
         first_factors = held([P, PACK, HALF], F32, "first_factors")
         dx01 = for_scalar([P, 2, S], "dx01", 12 * KIB)
-        dx23 = [placed([P, 2, C], F32, f"dx23_{e}", (84, 46)[e] * KIB) for e in range(2)]
+        dx23 = [placed([P, 2, C], F32, f"dx23_{e}", (84, 30)[e] * KIB) for e in range(2)]
         da = [
-            placed([P, PACK, C], F32, "da0", 16 * KIB),
+            placed([P, PACK, C], F32, "da0", 0),
             held([P, PACK, C], F32, "da1"),
-            placed([P, PACK, C], F32, "da2", 44 * KIB),
-            placed([P, PACK, C], F32, "da3", 41 * KIB),
+            placed([P, PACK, C], F32, "da2", 28 * KIB),
+            placed([P, PACK, C], F32, "da3", 25 * KIB),
         ]
         da_bf, da_codes, da_s = {}, {}, {}
 
@@ -173,7 +173,7 @@ def tile_moe_sdb_relu_kernel(
             )
 
         def round_da(e, factor=None):
-            da_bf[e] = placed([P, C, PACK], BF16, f"da_bf{e}", (28, 28, 20, 32)[e] * KIB)
+            da_bf[e] = placed([P, C, PACK], BF16, f"da_bf{e}", (12, 12, 4, 16)[e] * KIB)
             woven = woven_by_runs(da_bf[e][:])
             if e >= 2:
                 weave_on_gpsimd(da_bf[e][:], da[e][:])
@@ -247,7 +247,7 @@ def tile_moe_sdb_relu_kernel(
         round_da(0)
         late_factor(2, 1, first_factors[:, 3:4, of(0)])
         quantize_da(0)
-        factor2 = placed([P, 2, C], F32, "factor2", 16 * KIB)
+        factor2 = placed([P, 2, C], F32, "factor2", 0)
         late_factor(2, 2, factor2[:])
         round_da(1, first_factors[:, :, of(1)])
         gather(2, 0, first_factors[:, 2, of(0)])
@@ -258,7 +258,7 @@ def tile_moe_sdb_relu_kernel(
             late_factor(3, t, factor3[:, t : t + 2, :])
 
         for w in range(PACK):
-            windows[w] = (placed([P, T], F32, f"window{w}", 4 * w * KIB) if w > 1 else for_scalar([P, T], f"window{w}", 4 * w * KIB))
+            windows[w] = (placed([P, T], F32, f"window{w}", (82 + 4 * w) * KIB) if w > 1 else for_scalar([P, T], f"window{w}", 4 * w * KIB))
         dealt_s = {}
 
         def deal_scales(i, offset):
@@ -303,11 +303,11 @@ def tile_moe_sdb_relu_kernel(
         round_da(3)
         scatter(3, C, dx23[1][:, 1, :], "vector")
         quantize_da(3)
-        dealt = placed([P, E, 2 * PASS], U8, "dealt", 67 * KIB // 2)
+        dealt = placed([P, E, 2 * PASS], U8, "dealt", 35 * KIB // 2)
         for i in range(2):
-            deal_scales(i, (63 + 2 * i) * KIB // 2)
+            deal_scales(i, (31 + 2 * i) * KIB // 2)
             deal_words(i)
-        late23 = placed([P, 2, HALF], F32, "late23", 41 * KIB)
+        late23 = placed([P, 2, HALF], F32, "late23", 25 * KIB)
         empty_pair("vector", pair_bank(2, 1), late23[:, :, of(0)], order=(1, 0))
         scatter(3, HALF, late23[:, 1, of(0)], "vector")
         first_two_windows(3)
@@ -317,8 +317,8 @@ def tile_moe_sdb_relu_kernel(
         for w in (3, 0, 1, 2):
             nc.sync.dma_start(out=out_0[w * P : (w + 1) * P], in_=windows[w][:])
         quarters = [slice(q * C, (q + 1) * C) for q in range(PACK)]
-        second_half = placed([P, 2, PACK, C], F32, "second_half", 60 * KIB)
-        quad = [for_scalar([P, PACK, C], f"quad{q}", (20, 28)[q] * KIB)[:] for q in range(2)]
+        second_half = placed([P, 2, PACK, C], F32, "second_half", 32 * KIB)
+        quad = [for_scalar([P, PACK, C], "quad0", 20 * KIB)[:], placed([P, PACK, C], F32, "quad1", 44 * KIB)[:]]
         quad.extend(second_half[:, u] for u in range(2))
         back = out_0[0:PASS].rearrange("(p d) t -> p d t", d=PACK)
         for q in range(PACK):
@@ -333,10 +333,10 @@ def tile_moe_sdb_relu_kernel(
         dx.setdefault(4, for_scalar([P, S], "dx4", 32 * KIB))
         dx7 = for_scalar([P, 3 * C], "dx7", 36 * KIB)
         for w in (5, 6):
-            windows[w] = placed([P, T], F32, f"window{w}", (68, 80)[w - 5] * KIB)
+            windows[w] = placed([P, T], F32, f"window{w}", (40, 80)[w - 5] * KIB)
         windows.setdefault(4, for_scalar([P, T], "window4", 40 * KIB))
         windows.setdefault(7, for_scalar([P, T], "window7", 23 * KIB))
-        trio = placed([P, PACK - 1, T], F32, "trio", 4 * KIB)
+        trio = placed([P, PACK - 1, T], F32, "trio", 86 * KIB)
 
         def half_bank(b, w, h):
             return fill_bank(b, [(w, 2 * h), (w, 2 * h + 1)])
@@ -367,7 +367,7 @@ def tile_moe_sdb_relu_kernel(
             nc.sync.dma_start(out=dealt_rows[:, planes, :], in_=trio[:, planes, :])
         scatter(7, thirds[0].start, dx7[:, thirds[0]], "scalar")
         scatter(7, thirds[1].start, dx7[:, thirds[1]], "scalar")
-        dx_last = placed([P, C], F32, "dx_last", 68 * KIB)
+        dx_last = placed([P, C], F32, "dx_last", 40 * KIB)
         nc.scalar.copy(out=dx_last[:], in_=last_bank[:, C:BANK])
         scatter(7, thirds[2].start, dx_last[:], "scalar")
         nc.sync.dma_start(out=dealt_rows[:, PACK - 1, :], in_=windows[7][:])
@@ -390,7 +390,7 @@ def tile_moe_sdb_relu_kernel(
         store_words(0, y0_codes, 0, T)
 
         spans = [(0, T // 2), (T // 2, 3 * T // 4), (3 * T // 4, T)]
-        y1 = [placed([P, hi - lo, PACK], BF16, f"y1{lo}", at * KIB) for (lo, hi), at in zip(spans, (60, 64, 67))]
+        y1 = [placed([P, hi - lo, PACK], BF16, f"y1{lo}", at * KIB) for (lo, hi), at in zip(spans, (32, 36, 39))]
         engines = ("vector", "vector", "scalar")
         for woven, (lo, hi), engine in zip(y1, spans, engines):
             copy(engine, woven_by_runs(woven[:, :, 0 : PACK - 1]), by_runs(trio[:, :, lo:hi]))
@@ -400,7 +400,7 @@ def tile_moe_sdb_relu_kernel(
         for woven, (lo, hi) in zip(y1[0:2], spans):
             quantize_y(1, y1_codes[:, lo:hi], woven, lo, hi)
         store_words(1, y1_codes, 0, 3 * C)
-        last_codes = placed([P, C], I32, "last_codes", 60 * KIB)
+        last_codes = placed([P, C], I32, "last_codes", 32 * KIB)
         quantize_y(1, last_codes[:], y1[2], 3 * C, T)
         store_words(1, last_codes, 3 * C, T)
         for q in range(QUADRANTS):

from contextlib import ExitStack

import concourse.mybir as mybir

K, T, E, C, H, N = 1024, 1024, 4, 256, 512, 512
FLOPS = 2 * N * H * T + 2 * H * K * E * C

F32 = mybir.dt.float32
BF16 = mybir.dt.bfloat16
I32 = mybir.dt.int32
U16 = mybir.dt.uint16
U8 = mybir.dt.uint8
FP8X4 = mybir.dt.float8_e4m3fn_x4
FP4X4 = mybir.dt.float4_e2m1fn_x4
ALU = mybir.AluOpType
COPY = mybir.ActivationFunctionType.Copy

P = 128
PACK = 4
BANK = 512
LANES = 16
QUADRANTS = 4
S = E * C
HALF = S // 2
PASS = P * PACK
RUN = 2
KIB = 1024


def load_scale_rows(nc, plane, rows):
    for q in range(QUADRANTS):
        nc.sync.dma_start(out=plane[32 * q : 32 * q + 4].bitcast(I32), in_=rows[4 * q : 4 * q + 4].bitcast(I32))


def tile_moe_sdb_relu_kernel(
    tc, dy_words, dy_scales, w2t_words, w2t_scales, w1t_words, w1t_scales, a, gate, offs, out_0, out_1, out_2
):
    nc = tc.nc
    with ExitStack() as ctx:
        apart = ctx.enter_context(tc.tile_pool(name="apart", bufs=1))
        keep = ctx.enter_context(tc.tile_pool(name="keep", bufs=1))
        turns = ctx.enter_context(tc.tile_pool(name="turns", bufs=1))
        psum = ctx.enter_context(tc.psum_pool(name="psum", bufs=1))

        def bank(b):
            return psum.tile([P, BANK], F32, name="acc", tag=f"bank{b}")

        def held(shape, dtype, name, tag=None):
            return keep.tile(shape, dtype, name=name, tag=tag or name, align_bytes=64)

        def placed(shape, dtype, name, offset):
            return turns.tile(shape, dtype, name=name, offset=offset, align_bytes=64)

        def for_scalar(shape, name, offset):
            return apart.tile(shape, F32, name=name, offset=offset, align_bytes=64)

        def copy(engine, out, in_):
            if engine == "vector":
                nc.vector.tensor_copy(out=out, in_=in_)
            else:
                nc.scalar.copy(out=out, in_=in_)

        offsets = keep.tile([P, S // LANES], U16, name="offsets")
        w2_raw = held([P, H], I32, "w2_raw")
        w2_raw_s = held([P, H], U8, "w2_raw_s")
        w2_codes = held([P, H], I32, "w2_codes")
        w2_s = held([P, H], U8, "w2_s")
        dy_codes = held([P, T], I32, "dy_codes")
        dy_s = held([P, T], U8, "dy_s")
        w1_first_s = held([P, E, PASS], U8, "w1_first_s")
        w1_first = [held([P, 2, 2 * PASS], U8, f"w1_first{i}") for i in range(2)]
        w1_raw_s = held([P, E, PASS], U8, "w1_raw_s")
        w1_raw = held([P, E, 2 * PASS], U8, "w1_raw")
        row_sets = [(0, 1), (1, 1), (2, 2)]
        a_first = [held([P, count, HALF], F32, f"a_first{t}") for t, count in row_sets]
        a_sb = {e: held([P, PACK, C], F32, f"a{e}") for e in (2, 3)}
        gate_sb = [held([P, HALF], F32, f"gate{h}") for h in range(2)]

        nc.gpsimd.memset(w1_raw_s[:].rearrange("p e k -> p (e k)").bitcast(I32), 0)

        a_rows = a.rearrange("(p t) j -> p t j", t=PACK)
        w1_rows = w1t_words.rearrange("e s p c -> (s p) e c")
        w1_scale_rows = w1t_scales.rearrange("e s b k -> (s b) e k")

        def load_a(e):
            nc.sync.dma_start(out=a_sb[e][:], in_=a_rows[:, :, e * C : (e + 1) * C])

        def load_w1_first(i):
            words = w1_rows[:, 2 * i : 2 * i + 2, 0 : 2 * PASS]
            nc.sync.dma_start(out=w1_first[i][:].bitcast(I32), in_=words.bitcast(I32))

        for q in range(QUADRANTS):
            rows = w2t_scales[0, 4 * q : 4 * q + 4].bitcast(I32)
            nc.sync.dma_start(
                out=w2_raw_s[32 * q : 32 * q + 32].bitcast(I32), in_=rows.unsqueeze(0).to_broadcast([8, 4, H // 4])
            )
        nc.sync.dma_start(out=w2_raw[:], in_=w2t_words[0].rearrange("p i d -> p (i d)").bitcast(I32))
        nc.sync.dma_start(out=dy_codes[:], in_=dy_words[0].rearrange("p t d -> p (t d)").bitcast(I32))
        load_scale_rows(nc, dy_s, dy_scales[0])
        nc.sync.dma_start(out=gate_sb[0][:], in_=gate[:, 0:HALF])
        for rows, (t, count) in zip(a_first, row_sets):
            nc.sync.dma_start(out=rows[:], in_=a_rows[:, t : t + count, 0:HALF])
        nc.sync.dma_start(offsets[:], offs)
        load_scale_rows(nc, w1_first_s, w1_scale_rows[:, :, 0:PASS])
        nc.sync.dma_start(out=gate_sb[1][:], in_=gate[:, HALF:S])
        load_a(2)
        load_w1_first(0)
        load_a(3)
        load_w1_first(1)
        nc.sync.dma_start(out=w1_raw[:].bitcast(I32), in_=w1_rows[:, :, 2 * PASS : 2 * K].bitcast(I32))
        load_scale_rows(nc, w1_raw_s, w1_scale_rows[:, :, PASS:K])

        nc.vector.tensor_copy(
            out=w2_codes[:].rearrange("p (t m) -> p m t", t=PACK), in_=w2_raw[:].rearrange("p (m t) -> p m t", t=PACK)
        )
        nc.vector.tensor_copy(
            out=w2_s[:].rearrange("p (t m) -> p m t", t=PACK), in_=w2_raw_s[:].rearrange("p (m t) -> p m t", t=PACK)
        )

        def slots(first, width):
            return offsets[:, first // LANES : (first + width) // LANES]

        def mx(out, codes, scales, moving, moving_scales):
            nc.tensor.matmul_mx(
                out=out, lhsT=codes, lhsT_scale=scales, rhs=moving, rhs_scale=moving_scales, start=True, stop=True
            )

        def of(e):
            return slice(e * C, (e + 1) * C)

        dc = [held([P, T], F32, f"dc{t}") for t in range(PACK)]
        first_factors = held([P, PACK, HALF], F32, "first_factors")
        dx01 = for_scalar([P, 2, S], "dx01", 12 * KIB)
        dx23 = [placed([P, 2, C], F32, f"dx23_{e}", (84, 30)[e] * KIB) for e in range(2)]
        da = [
            placed([P, PACK, C], F32, "da0", 0),
            held([P, PACK, C], F32, "da1"),
            placed([P, PACK, C], F32, "da2", 28 * KIB),
            placed([P, PACK, C], F32, "da3", 25 * KIB),
        ]
        da_bf, da_codes, da_s = {}, {}, {}

        def mask_times_gate(out, rows, weights):
            nc.vector.scalar_tensor_tensor(
                out=out,
                in0=rows,
                scalar=0.0,
                in1=weights.unsqueeze(1).to_broadcast(rows.shape),
                op0=ALU.is_gt,
                op1=ALU.mult,
            )

        def late_factor(e, t, out):
            rows = a_sb[e][:, t : t + out.shape[1], :]
            mask_times_gate(out, rows, gate_sb[1][:, of(e - 2)])

        def gather(e, t, factor):
            picked = dc[t][:].indirect(slots(e * C, C))
            if factor is None:
                nc.scalar.activation(da[e][:, t, :], picked, COPY)
            else:
                nc.vector.tensor_tensor(da[e][:, t, :], picked, factor, ALU.mult)

        def by_runs(rows):
            return rows.rearrange("p t (c i) -> p c t i", i=RUN)

        def woven_by_runs(woven):
            return woven.rearrange("p (c i) t -> p c t i", i=RUN)

        def weave_on_gpsimd(woven, rows):
            nc.gpsimd.tensor_scalar(
                out=woven, in0=rows.rearrange("p d t -> p t d"), scalar1=1.0, scalar2=-0.0, op0=ALU.mult, op1=ALU.add
            )

        def round_da(e, factor=None):
            da_bf[e] = placed([P, C, PACK], BF16, f"da_bf{e}", (12, 12, 4, 16)[e] * KIB)
            woven = woven_by_runs(da_bf[e][:])
            if e >= 2:
                weave_on_gpsimd(da_bf[e][:], da[e][:])
            elif factor is None:
                nc.vector.tensor_copy(out=woven, in_=by_runs(da[e][:]))
            else:
                nc.vector.tensor_tensor(woven, by_runs(da[e][:]), by_runs(factor), ALU.mult)

        def quantize_da(e):
            da_codes[e] = held([P, C], I32, f"da_codes{e}")
            da_s[e] = held([P, C], U8, f"da_s{e}")
            nc.vector.quantize_mx(
                out=da_codes[e][:].bitcast(FP8X4), scales=da_s[e][:], in_=da_bf[e][:].rearrange("p j t -> p (j t)")
            )

        def fill_bank(b, parts):
            acc = bank(b)
            for u, (w, e) in enumerate(parts):
                s, j = divmod(w, PACK)
                if s == 0:
                    codes, scales = w1_first[e // 2][:, e % 2, :], w1_first_s[:, e, :]
                else:
                    codes, scales = dealt[:, e, :], dealt_s[e // 2][:, e % 2, :]
                mx(
                    acc[:, of(u)],
                    codes[:, 2 * j * P : 2 * (j + 1) * P].bitcast(FP4X4),
                    scales[:, j * P : (j + 1) * P],
                    da_codes[e][:].bitcast(FP8X4),
                    da_s[e][:],
                )
            return acc

        def pair_bank(e, i):
            return fill_bank(2 * e + i, [(2 * i, e), (2 * i + 1, e)])

        def empty_pair(engine, acc, out, order=None):
            if order is None:
                copy(engine, out, acc[:].rearrange("p (u j) -> p u j", u=2))
            else:
                for u in order:
                    copy(engine, out[:, u, :], acc[:, of(u)])

        windows = {}

        def scatter(w, first, source, engine):
            target = windows[w][:].indirect(slots(first, source.shape[1]))
            if engine == "vector":
                nc.vector.tensor_copy(target, source)
            else:
                nc.scalar.activation(target, source, COPY)

        for rows, (t, count) in zip(a_first, row_sets):
            mask_times_gate(first_factors[:, t : t + count, :], rows[:], gate_sb[0][:])
        for t in range(PACK):
            for h in range(2):
                cols = slice(h * BANK, (h + 1) * BANK)
                acc = bank(2 * t + h)
                mx(
                    acc[:],
                    w2_codes[:, t * P : (t + 1) * P].bitcast(FP8X4),
                    w2_s[:, t * P : (t + 1) * P],
                    dy_codes[:, cols].bitcast(FP8X4),
                    dy_s[:, cols],
                )
                nc.scalar.copy(out=dc[t][:, cols], in_=acc[:])
        for t in range(PACK):
            gather(0, t, first_factors[:, t, of(0)])
        for t in range(PACK):
            gather(1, t, None)
        late_factor(2, 0, first_factors[:, 2:3, of(0)])
        round_da(0)
        late_factor(2, 1, first_factors[:, 3:4, of(0)])
        quantize_da(0)
        factor2 = placed([P, 2, C], F32, "factor2", 0)
        late_factor(2, 2, factor2[:])
        round_da(1, first_factors[:, :, of(1)])
        gather(2, 0, first_factors[:, 2, of(0)])
        quantize_da(1)
        gather(2, 1, first_factors[:, 3, of(0)])
        factor3 = held([P, PACK, C], F32, "factor3")
        for t in (0, 2):
            late_factor(3, t, factor3[:, t : t + 2, :])

        for w in range(PACK):
            windows[w] = (placed([P, T], F32, f"window{w}", (82 + 4 * w) * KIB) if w > 1 else for_scalar([P, T], f"window{w}", 4 * w * KIB))
        dealt_s = {}

        def deal_scales(i, offset):
            dealt_s[i] = placed([P, 2, PASS], U8, f"dealt_s{i}", offset)
            nc.gpsimd.tensor_copy(
                out=dealt_s[i][:].rearrange("p e (d m) -> p e d m", d=PACK),
                in_=w1_raw_s[:, 2 * i : 2 * i + 2, :].rearrange("p e (m d) -> p e d m", d=PACK),
            )

        def deal_words(i):
            pair = slice(2 * i, 2 * i + 2)
            nc.gpsimd.tensor_copy(
                out=dealt[:, pair, :].rearrange("p e (d m b) -> p e d m b", d=PACK, b=2),
                in_=w1_raw[:, pair, :].rearrange("p e (m d b) -> p e d m b", d=PACK, b=2),
            )

        def first_two_windows(e):
            empty_pair("scalar", pair_bank(e, 0), dx01[:, :, of(e)], order=(0, 1))
            for w in range(2):
                scatter(w, e * C, dx01[:, w, of(e)], "scalar")

        alone = [fill_bank(b, [(w, 0)]) for w, b in enumerate((7, 0))]
        for w in range(2):
            nc.scalar.copy(out=dx01[:, w, of(0)], in_=alone[w][:, 0:C])
        scatter(0, 0, dx01[:, 0, of(0)], "scalar")
        empty_pair("scalar", pair_bank(0, 1), dx23[0][:])
        scatter(1, 0, dx01[:, 1, of(0)], "scalar")
        scatter(2, 0, dx23[0][:, 0, :], "scalar")
        first_two_windows(1)

        for t in (2, 3):
            gather(2, t, factor2[:, t - 2, :])
        round_da(2)
        scatter(3, 0, dx23[0][:, 1, :], "vector")
        quantize_da(2)
        for t in range(PACK - 1):
            gather(3, t, factor3[:, t, :])
        empty_pair("vector", pair_bank(1, 1), dx23[1][:])
        gather(3, 3, factor3[:, 3, :])
        scatter(2, C, dx23[1][:, 0, :], "scalar")
        first_two_windows(2)
        round_da(3)
        scatter(3, C, dx23[1][:, 1, :], "vector")
        quantize_da(3)
        dealt = placed([P, E, 2 * PASS], U8, "dealt", 35 * KIB // 2)
        for i in range(2):
            deal_scales(i, (31 + 2 * i) * KIB // 2)
            deal_words(i)
        late23 = placed([P, 2, HALF], F32, "late23", 25 * KIB)
        empty_pair("vector", pair_bank(2, 1), late23[:, :, of(0)], order=(1, 0))
        scatter(3, HALF, late23[:, 1, of(0)], "vector")
        first_two_windows(3)
        empty_pair("vector", pair_bank(3, 1), late23[:, :, of(1)], order=(1, 0))
        scatter(3, 3 * C, late23[:, 1, of(1)], "vector")
        scatter(2, HALF, late23[:, 0, :], "vector")
        for w in (3, 0, 1, 2):
            nc.sync.dma_start(out=out_0[w * P : (w + 1) * P], in_=windows[w][:])
        quarters = [slice(q * C, (q + 1) * C) for q in range(PACK)]
        second_half = placed([P, 2, PACK, C], F32, "second_half", 32 * KIB)
        quad = [for_scalar([P, PACK, C], "quad0", 20 * KIB)[:], placed([P, PACK, C], F32, "quad1", 44 * KIB)[:]]
        quad.extend(second_half[:, u] for u in range(2))
        back = out_0[0:PASS].rearrange("(p d) t -> p d t", d=PACK)
        for q in range(PACK):
            nc.sync.dma_start(out=quad[q], in_=back[:, :, quarters[q]])
        y0 = held([P, T, PACK], BF16, "y0")
        for q in range(PACK):
            weave_on_gpsimd(y0[:, quarters[q], :], quad[q])

        halves = [slice(0, HALF), slice(HALF, T)]
        thirds = [slice(0, 384), slice(384, 768), slice(768, S)]
        dx = {w: placed([P, S], F32, f"dx{w}", (72, 76)[w - 5] * KIB) for w in (5, 6)}
        dx.setdefault(4, for_scalar([P, S], "dx4", 32 * KIB))
        dx7 = for_scalar([P, 3 * C], "dx7", 36 * KIB)
        for w in (5, 6):
            windows[w] = placed([P, T], F32, f"window{w}", (40, 80)[w - 5] * KIB)
        windows.setdefault(4, for_scalar([P, T], "window4", 40 * KIB))
        windows.setdefault(7, for_scalar([P, T], "window7", 23 * KIB))
        trio = placed([P, PACK - 1, T], F32, "trio", 86 * KIB)

        def half_bank(b, w, h):
            return fill_bank(b, [(w, 2 * h), (w, 2 * h + 1)])

        for b, w, engine in ((0, 5, "scalar"), (1, 6, "scalar")):
            copy(engine, dx[w][:, halves[0]], half_bank(b, w, 0)[:])
        for w in (5, 6):
            scatter(w, 0, dx[w][:, halves[0]], "vector")
        nc.scalar.copy(out=dx[4][:, halves[0]], in_=half_bank(2, 4, 0)[:])
        nc.scalar.copy(out=dx7[:, halves[0]], in_=half_bank(3, 7, 0)[:])
        scatter(4, thirds[0].start, dx[4][:, thirds[0]], "scalar")
        acc = half_bank(4, 4, 1)
        nc.scalar.copy(out=dx[4][:, HALF : 3 * C], in_=acc[:, of(0)])
        nc.vector.tensor_copy(out=dx[4][:, 3 * C : S], in_=acc[:, of(1)])
        for b, w in ((5, 5), (6, 6)):
            nc.scalar.copy(out=dx[w][:, halves[1]], in_=half_bank(b, w, 1)[:])
        scatter(4, thirds[1].start, dx[4][:, thirds[1]], "scalar")
        last_bank = half_bank(7, 7, 1)
        nc.scalar.copy(out=dx7[:, HALF : 3 * C], in_=last_bank[:, 0:C])
        scatter(4, thirds[2].start, dx[4][:, thirds[2]], "scalar")
        for w in (5, 6):
            scatter(w, HALF, dx[w][:, halves[1]], "vector")
        for w in (4, 5):
            nc.sync.dma_start(out=trio[:, w - PACK, :], in_=windows[w][:])
        nc.vector.tensor_copy(out=trio[:, 2, :], in_=windows[6][:])
        dealt_rows = out_0[PASS:K].rearrange("(p d) t -> p d t", d=PACK)
        for planes in (slice(0, 1), slice(1, 3)):
            nc.sync.dma_start(out=dealt_rows[:, planes, :], in_=trio[:, planes, :])
        scatter(7, thirds[0].start, dx7[:, thirds[0]], "scalar")
        scatter(7, thirds[1].start, dx7[:, thirds[1]], "scalar")
        dx_last = placed([P, C], F32, "dx_last", 40 * KIB)
        nc.scalar.copy(out=dx_last[:], in_=last_bank[:, C:BANK])
        scatter(7, thirds[2].start, dx_last[:], "scalar")
        nc.sync.dma_start(out=dealt_rows[:, PACK - 1, :], in_=windows[7][:])

        y_s = held([P, 2, T], U8, "y_s")

        def quantize_y(s, codes, woven, lo, hi):
            nc.vector.quantize_mx(
                out=codes.bitcast(FP8X4),
                scales=y_s[:, s, lo:hi],
                in_=woven[:].rearrange("p t d -> p (t d)"),
            )

        def store_words(s, codes, lo, hi):
            words = out_1[s].rearrange("p t d -> p (t d)").bitcast(I32)
            nc.sync.dma_start(out=words[:, lo:hi], in_=codes[:])

        y0_codes = held([P, T], I32, "y0_codes")
        quantize_y(0, y0_codes[:], y0, 0, T)
        store_words(0, y0_codes, 0, T)

        spans = [(0, T // 2), (T // 2, 3 * T // 4), (3 * T // 4, T)]
        y1 = [placed([P, hi - lo, PACK], BF16, f"y1{lo}", at * KIB) for (lo, hi), at in zip(spans, (32, 36, 39))]
        engines = ("vector", "vector", "scalar")
        for woven, (lo, hi), engine in zip(y1, spans, engines):
            copy(engine, woven_by_runs(woven[:, :, 0 : PACK - 1]), by_runs(trio[:, :, lo:hi]))
        for woven, (lo, hi), engine in zip(y1, spans, engines):
            copy(engine, woven[:, :, PACK - 1], windows[7][:, lo:hi])
        y1_codes = held([P, 3 * C], I32, "y1_codes")
        for woven, (lo, hi) in zip(y1[0:2], spans):
            quantize_y(1, y1_codes[:, lo:hi], woven, lo, hi)
        store_words(1, y1_codes, 0, 3 * C)
        last_codes = placed([P, C], I32, "last_codes", 32 * KIB)
        quantize_y(1, last_codes[:], y1[2], 3 * C, T)
        store_words(1, last_codes, 3 * C, T)
        for q in range(QUADRANTS):
            (nc.scalar if q % 2 else nc.sync).dma_start(
                out=out_2[:, 4 * q : 4 * q + 4, :].rearrange("s b t -> b s t").bitcast(I32),
                in_=y_s[32 * q : 32 * q + 4].bitcast(I32),
            )
